import numpy as np
import ml_dtypes


def mxq(x, axis, fmt="e4m3"):
    dtype, down = {"e4m3": (ml_dtypes.float8_e4m3fn, 7), "e5m2": (ml_dtypes.float8_e5m2, 14)}[fmt]
    v = np.moveaxis(np.asarray(x, np.float32).astype(ml_dtypes.bfloat16).astype(np.float64), axis, -1)
    blocks = v.reshape(v.shape[:-1] + (-1, 32))
    amax = np.abs(blocks).max(-1, keepdims=True)
    byte = np.maximum(np.where(amax > 0, np.frexp(amax)[1] - 1 + 127, 0) - down, 1)
    scale = np.exp2(byte - 127.0)
    codes = (blocks / scale).astype(np.float32).astype(dtype).astype(np.float64)
    return np.moveaxis((codes * scale).reshape(v.shape), -1, axis)


WIDE = False


def mx_kscale(k):
    if not WIDE:
        return np.ones(k)
    levels = np.array([10, -10, 5, -5, 0])
    if k % 512:
        return np.exp2(np.random.permutation(np.resize(levels, k // 32))).repeat(32)
    a = np.empty((k // 512, 16))
    for p in range(k // 512):
        a[p, :8] = np.random.permutation(np.resize(levels, 8))
        for g in range(8):
            far = levels[np.abs(levels - a[p, g]) >= 10]
            a[p, g + 8] = far[np.random.randint(len(far))]
    return np.exp2(a.ravel()).repeat(32)


def f64(x):
    return np.asarray(x).astype(np.float64)


def striped(idx):
    return np.tile(idx.reshape(-1, 16).T, (8, 1)).astype(np.uint16)


def unstriped(offs):
    return offs[:16].T.reshape(-1).astype(np.int64)


def pack_weight(w):
    k, n = w.shape
    w = f64(np.asarray(w, np.float32).astype(ml_dtypes.bfloat16)).reshape(k // 32, 32, n)
    amax = np.abs(w).max(1)
    byte = np.clip(np.where(amax > 0, np.frexp(amax)[1] - 1 + 127 - 7, 1), 1, 254)
    scaled = (w * np.exp2(127.0 - byte)[:, None, :]).reshape(k, n).astype(np.float32)
    words = np.ascontiguousarray(scaled.reshape(k // 512, 128, 4, n).transpose(0, 1, 3, 2)).astype(ml_dtypes.float8_e4m3fn).view(np.uint8)
    return words, np.ascontiguousarray(byte.astype(np.uint8).reshape(k // 512, 16, n))


def unpack_weight(words, scales):
    g, p, n, _ = words.shape
    vals = np.ascontiguousarray(words).view(ml_dtypes.float8_e4m3fn).astype(np.float64) * np.repeat(np.exp2(scales.astype(np.float64) - 127.0), 8, axis=1)[..., None]
    return vals.transpose(0, 1, 3, 2).reshape(g * 512, n)


E2M1 = np.array([0.0, 0.5, 1.0, 1.5, 2.0, 3.0, 4.0, 6.0, -0.0, -0.5, -1.0, -1.5, -2.0, -3.0, -4.0, -6.0])


def pack_fp4(w):
    k, n = w.shape
    w = f64(np.asarray(w, np.float32).astype(ml_dtypes.bfloat16)).reshape(k // 32, 32, n)
    amax = np.abs(w).max(1)
    mant, ex = np.frexp(amax / 6.0)
    byte = np.clip(np.where(amax > 0, np.where(mant > 0.5, ex, ex - 1) + 127, 1), 1, 254)
    scaled = (w * np.exp2(127.0 - byte)[:, None, :]).reshape(k, n).astype(np.float32)
    c = np.ascontiguousarray(scaled.reshape(k // 512, 128, 4, n).transpose(0, 1, 3, 2)).astype(ml_dtypes.float4_e2m1fn).view(np.uint8) & 0xF
    words = (c[..., 0::2] | (c[..., 1::2] << 4)).reshape(k // 512, 128, 2 * n)
    return np.ascontiguousarray(words), np.ascontiguousarray(byte.astype(np.uint8).reshape(k // 512, 16, n))


def unpack_fp4(words, scales):
    g, _, n = scales.shape
    words = np.ascontiguousarray(words).reshape(g, 128, n, 2)
    nib = np.empty((g, 128, n, 4), np.uint8)
    nib[..., 0::2] = words & 0xF
    nib[..., 1::2] = words >> 4
    vals = E2M1[nib] * np.repeat(np.exp2(scales.astype(np.float64) - 127.0), 8, axis=1)[..., None]
    return vals.transpose(0, 1, 3, 2).reshape(g * 512, n)


K, T, S, H, N = 512, 4096, 1024, 512, 256


def setup_inputs():
    n = np.random.standard_normal
    s = mx_kscale(K)[:, None]
    u = mx_kscale(H)
    packed_xT = pack_weight(n((K, T)) * s)
    packed_w2 = pack_fp4(n((H, N)) / np.sqrt(H) / u[:, None])
    return {
        "x_words": packed_xT[0],
        "x_scales": packed_xT[1],
        "w1": (n((K, H)) / np.sqrt(K) / s).astype(np.float32),
        "w2_words": packed_w2[0],
        "w2_scales": packed_w2[1],
        "gamma": (np.random.uniform(0.5, 1.5, (H, 1)) * u[:, None]).astype(np.float32),
        "offs": striped(np.random.permutation(T)[:S]),
    }


def reference(x_words, x_scales, w1, w2_words, w2_scales, gamma, offs):
    xq = unpack_weight(x_words, x_scales)[:, unstriped(offs)]
    h = mxq(f64(w1), 0, "e4m3").T @ xq
    hn = (h - h.mean(axis=1, keepdims=True)) / np.sqrt(h.var(axis=1, keepdims=True) + 1e-5)
    z = f64(gamma) * hn
    return unpack_fp4(w2_words, w2_scales).T @ mxq(z, 0, "e4m3")

@@ -1,0 +1,175 @@
+from contextlib import ExitStack
+
+import concourse.mybir as mybir
+
+K, T, S, H, N = 512, 4096, 1024, 512, 256
+FLOPS = 2 * S * H * (K + N)
+EPS = 1e-5
+
+F32 = mybir.dt.float32
+BF16 = mybir.dt.bfloat16
+I32 = mybir.dt.int32
+U32 = mybir.dt.uint32
+U16 = mybir.dt.uint16
+U8 = mybir.dt.uint8
+FP8X4 = mybir.dt.float8_e4m3fn_x4
+FP4X4 = mybir.dt.float4_e2m1fn_x4
+ACT = mybir.ActivationFunctionType
+ALU = mybir.AluOpType
+
+P = 128
+PACK = 4
+HALF = 512
+CHUNK = 256
+CAST_SPLIT = 88
+
+
+def tile_picked_inorm_none_p_kernel(tc, x_words, x_scales, w1, w2_words, w2_scales, gamma, offs, out):
+    nc = tc.nc
+    with ExitStack() as ctx:
+        held = ctx.enter_context(tc.tile_pool(name="held", bufs=1))
+        late = ctx.enter_context(tc.tile_pool(name="late", bufs=1))
+        psum = ctx.enter_context(tc.psum_pool(name="psum", bufs=1))
+
+        offsets = held.tile([P, S // 16], U16, name="offsets")
+        nc.sync.dma_start(offsets[:], offs)
+        x_table = held.tile([P, T], U32, name="x_table", align_bytes=64)
+        nc.sync.dma_start(x_table[:].bitcast(I32), x_words[0].rearrange("p n r -> p (n r)").bitcast(I32))
+        w_raw = held.tile([P, PACK, H], F32, name="w_raw", align_bytes=64)
+        nc.sync.dma_start(w_raw[:], w1.rearrange("(p j) c -> p j c", j=PACK))
+
+        gain = held.tile([P, PACK], F32, name="gain", align_bytes=64)
+        nc.sync.dma_start(gain[:], gamma.rearrange("(p t) o -> p (t o)", t=PACK))
+        w2_codes = held.tile([P, 2 * N], U8, name="w2_codes", align_bytes=64)
+        nc.sync.dma_start(w2_codes[:].bitcast(I32), w2_words[0].bitcast(I32))
+
+        s_table = late.tile([P, T], U8, name="s_table", offset=0, align_bytes=64)
+        nc.vector.memset(s_table[:].bitcast(I32), 0)
+        nc.scalar.dma_start(s_table[0:P:8, :].bitcast(I32), x_scales[0].bitcast(I32))
+
+        x_plane = held.tile([P, S], U8, name="x_plane", align_bytes=64)
+        nc.vector.memset(x_plane[:].bitcast(I32), 0)
+        warm_in = held.tile([P, 1], F32, name="warm_in")
+        nc.vector.memset(warm_in[:], 1.0)
+        warm_out = held.tile([P, 1], F32, name="warm_out")
+        nc.scalar.activation(warm_out[:], warm_in[:], ACT.Abs_reciprocal_sqrt)
+
+        s_picked = late.tile([P, S], U8, name="s_picked", offset=T, align_bytes=64)
+        nc.vector.tensor_copy(s_picked[:], s_table[:].indirect(offsets[:]))
+        for r in range(4):
+            nc.scalar.dma_start(x_plane[r:P:32, :].bitcast(I32), s_picked[8 * r : P : 32, :].bitcast(I32))
+
+        w2_plane = late.tile([P, N], U8, name="w2_plane", offset=T, align_bytes=64)
+        nc.gpsimd.memset(w2_plane[:].bitcast(I32), 0)
+        for r in range(4):
+            nc.sync.dma_start(w2_plane[r:P:32, :].bitcast(I32), w2_scales[0, r:16:4, :].bitcast(I32))
+
+        x_picked = []
+        for h in range(2):
+            xp = late.tile([P, HALF], U32, name=f"x_picked{h}", offset=4 * HALF * h, align_bytes=64)
+            nc.vector.tensor_copy(xp[:], x_table[:].indirect(offsets[:, 32 * h : 32 * (h + 1)]))
+            x_picked.append(xp)
+
+        w_bf = held.tile([P, PACK, P, PACK], BF16, name="w_bf", align_bytes=64)
+        w_dst = w_bf[:].rearrange("p t m j -> p m j t")
+        w_src = w_raw[:].rearrange("p j (m t) -> p m j t", t=PACK)
+        nc.vector.tensor_copy(w_dst[:, :CAST_SPLIT], w_src[:, :CAST_SPLIT])
+        nc.scalar.copy(w_dst[:, CAST_SPLIT:], w_src[:, CAST_SPLIT:])
+        w_codes, w_planes = [], []
+        for t in range(PACK):
+            wc = held.tile([P, P], U32, name=f"w_codes{t}", align_bytes=64)
+            wp = held.tile([P, P], U8, name=f"w_plane{t}", align_bytes=64)
+            nc.vector.quantize_mx(out=wc[:].bitcast(FP8X4), scales=wp[:], in_=w_bf[:, t].rearrange("p m j -> p (m j)"))
+            w_codes.append(wc)
+            w_planes.append(wp)
+
+        neg_gain = held.tile([P, PACK], F32, name="neg_gain")
+        nc.gpsimd.tensor_scalar(neg_gain[:], gain[:], -1.0, 0.0, ALU.mult, ALU.add)
+
+        banks = {}
+        for t in range(PACK):
+            for h in range(2):
+                bank = psum.tile([P, HALF], F32, name=f"h{t}{h}", tag=f"bank{t}{h}")
+                nc.tensor.matmul_mx(
+                    out=bank[:],
+                    lhsT=w_codes[t][:].bitcast(FP8X4),
+                    lhsT_scale=w_planes[t][:],
+                    rhs=x_picked[h][:].bitcast(FP8X4),
+                    rhs_scale=x_plane[:, HALF * h : HALF * (h + 1)],
+                    start=True,
+                    stop=True,
+                )
+                banks[t, h] = bank
+
+        z_rows = [held.tile([P, PACK, HALF], BF16, name=f"z_rows{h}", align_bytes=64) for h in range(2)]
+        affine = []
+
+        def statistics(t):
+            stats = held.tile([P, 12], F32, name=f"stats{t}")
+            for h in range(2):
+                nc.vector.bn_stats(stats[:, 6 * h : 6 * (h + 1)], banks[t, h][:])
+            moments = held.tile([P, 2], F32, name=f"moments{t}")
+            nc.vector.bn_aggr(moments[:], stats[:])
+            rstd = held.tile([P, 1], F32, name=f"rstd{t}")
+            nc.scalar.activation(rstd[:], moments[:, 1:2], ACT.Abs_reciprocal_sqrt, bias=EPS)
+            pair = held.tile([P, 2], F32, name=f"pair{t}")
+            nc.gpsimd.tensor_copy(pair[:, 0:1], gain[:, t : t + 1])
+            nc.scalar.activation(pair[:, 1:2], moments[:, 0:1], ACT.Copy, scale=neg_gain[:, t : t + 1])
+            ab = held.tile([P, 2], F32, name=f"affine{t}")
+            nc.scalar.activation(ab[:], pair[:], ACT.Copy, scale=rstd[:])
+            affine.append(ab)
+
+        def normalise(t, h, on_vector):
+            ab = affine[t]
+            if on_vector:
+                nc.vector.tensor_scalar(z_rows[h][:, t], banks[t, h][:], ab[:, 0:1], ab[:, 1:2], ALU.mult, ALU.add)
+            else:
+                nc.scalar.activation(z_rows[h][:, t], banks[t, h][:], ACT.Identity, scale=ab[:, 0:1], bias=ab[:, 1:2])
+
+        statistics(0)
+        for t in range(PACK):
+            normalise(t, 0, False)
+            if t + 1 < PACK:
+                statistics(t + 1)
+            normalise(t, 1, t == PACK - 1)
+
+        out_view = out.rearrange("(u p) s -> p u s", p=P)
+        n_chunks = S // CHUNK
+        woven = []
+        for c in range(n_chunks):
+            h, lo = divmod(c * CHUNK, HALF)
+            zw = held.tile([P, CHUNK, PACK], BF16, name=f"woven{c}", align_bytes=64)
+            dst = zw[:].rearrange("p (c i) t -> p c t i", i=4)
+            src = z_rows[h][:, :, lo : lo + CHUNK].rearrange("p t (c i) -> p c t i", i=4)
+            if c == 1:
+                nc.scalar.copy(dst, src)
+            else:
+                nc.vector.tensor_copy(dst, src)
+            woven.append(zw)
+        for c in range(n_chunks):
+            zc = held.tile([P, CHUNK], U32, name=f"z_codes{c}", align_bytes=64)
+            zp = held.tile([P, CHUNK], U8, name=f"z_plane{c}", align_bytes=64)
+            nc.vector.quantize_mx(out=zc[:].bitcast(FP8X4), scales=zp[:], in_=woven[c][:].rearrange("p n t -> p (n t)"))
+            last = c == n_chunks - 1
+            res = held.tile([P, 2, CHUNK], F32, name=f"res{c}", align_bytes=64)
+            if last:
+                accs = [psum.tile([P, CHUNK], F32, name=f"acc{c}{u}", tag=f"bank{u}1")[:] for u in range(2)]
+            else:
+                acc = psum.tile([P, 2, CHUNK], F32, name=f"acc{c}", tag=f"bank{c}0")
+                accs = [acc[:, u] for u in range(2)]
+            for u in range(2):
+                nc.tensor.matmul_mx(
+                    out=accs[u],
+                    lhsT=w2_codes[:, 2 * P * u : 2 * P * (u + 1)].bitcast(FP4X4),
+                    lhsT_scale=w2_plane[:, P * u : P * (u + 1)],
+                    rhs=zc[:].bitcast(FP8X4),
+                    rhs_scale=zp[:],
+                    start=True,
+                    stop=True,
+                )
+            if last:
+                nc.scalar.copy(res[:, 0], accs[0])
+                nc.vector.tensor_copy(res[:, 1], accs[1])
+            else:
+                nc.scalar.copy(res[:], acc[:])
+            nc.sync.dma_start(out_view[:, :, c * CHUNK : (c + 1) * CHUNK], res[:])

@@ -22,6 +22,7 @@ PACK = 4
 HALF = 512
 CHUNK = 256
 CAST_SPLIT = 88
+WARM = 3
 
 
 def tile_picked_inorm_none_p_kernel(tc, x_words, x_scales, w1, w2_words, w2_scales, gamma, offs, out):
@@ -37,11 +38,8 @@ def tile_picked_inorm_none_p_kernel(tc, x_words, x_scales, w1, w2_words, w2_scal
         nc.sync.dma_start(x_table[:].bitcast(I32), x_words[0].rearrange("p n r -> p (n r)").bitcast(I32))
         w_raw = held.tile([P, PACK, H], F32, name="w_raw", align_bytes=64)
         nc.sync.dma_start(w_raw[:], w1.rearrange("(p j) c -> p j c", j=PACK))
-
         gain = held.tile([P, PACK], F32, name="gain", align_bytes=64)
         nc.sync.dma_start(gain[:], gamma.rearrange("(p t) o -> p (t o)", t=PACK))
-        w2_codes = held.tile([P, 2 * N], U8, name="w2_codes", align_bytes=64)
-        nc.sync.dma_start(w2_codes[:].bitcast(I32), w2_words[0].bitcast(I32))
 
         s_table = late.tile([P, T], U8, name="s_table", offset=0, align_bytes=64)
         nc.vector.memset(s_table[:].bitcast(I32), 0)
@@ -59,7 +57,9 @@ def tile_picked_inorm_none_p_kernel(tc, x_words, x_scales, w1, w2_words, w2_scal
         for r in range(4):
             nc.scalar.dma_start(x_plane[r:P:32, :].bitcast(I32), s_picked[8 * r : P : 32, :].bitcast(I32))
 
-        w2_plane = late.tile([P, N], U8, name="w2_plane", offset=T, align_bytes=64)
+        w2_codes = late.tile([P, 2 * N], U8, name="w2_codes", offset=T, align_bytes=64)
+        nc.sync.dma_start(w2_codes[:].bitcast(I32), w2_words[0].bitcast(I32))
+        w2_plane = late.tile([P, N], U8, name="w2_plane", offset=T + 2 * N, align_bytes=64)
         nc.gpsimd.memset(w2_plane[:].bitcast(I32), 0)
         for r in range(4):
             nc.sync.dma_start(w2_plane[r:P:32, :].bitcast(I32), w2_scales[0, r:16:4, :].bitcast(I32))
@@ -70,7 +70,19 @@ def tile_picked_inorm_none_p_kernel(tc, x_words, x_scales, w1, w2_words, w2_scal
             nc.vector.tensor_copy(xp[:], x_table[:].indirect(offsets[:, 32 * h : 32 * (h + 1)]))
             x_picked.append(xp)
 
-        w_bf = held.tile([P, PACK, P, PACK], BF16, name="w_bf", align_bytes=64)
+        for i in range(WARM):
+            idle = psum.tile([P, HALF], F32, name=f"idle{i}", tag="bank31")
+            nc.tensor.matmul_mx(
+                out=idle[:],
+                lhsT=x_picked[0][:, :P].bitcast(FP8X4),
+                lhsT_scale=x_plane[:, :P],
+                rhs=x_picked[0][:].bitcast(FP8X4),
+                rhs_scale=x_plane[:, :HALF],
+                start=True,
+                stop=True,
+            )
+
+        w_bf = late.tile([P, PACK, P, PACK], BF16, name="w_bf", offset=T + 3 * N, align_bytes=64)
         w_dst = w_bf[:].rearrange("p t m j -> p m j t")
         w_src = w_raw[:].rearrange("p j (m t) -> p m j t", t=PACK)
         nc.vector.tensor_copy(w_dst[:, :CAST_SPLIT], w_src[:, :CAST_SPLIT])
@@ -85,91 +97,141 @@ def tile_picked_inorm_none_p_kernel(tc, x_words, x_scales, w1, w2_words, w2_scal
 
         neg_gain = held.tile([P, PACK], F32, name="neg_gain")
         nc.gpsimd.tensor_scalar(neg_gain[:], gain[:], -1.0, 0.0, ALU.mult, ALU.add)
+        pairs = [held.tile([P, 2], F32, name=f"pair{t}") for t in range(PACK)]
+        for t in range(PACK):
+            nc.gpsimd.tensor_scalar(pairs[t][:, 0:1], gain[:, t : t + 1], -float(S) if t == 0 else 1.0, 0.0, ALU.mult, ALU.add)
 
         banks = {}
-        for t in range(PACK):
-            for h in range(2):
-                bank = psum.tile([P, HALF], F32, name=f"h{t}{h}", tag=f"bank{t}{h}")
-                nc.tensor.matmul_mx(
-                    out=bank[:],
-                    lhsT=w_codes[t][:].bitcast(FP8X4),
-                    lhsT_scale=w_planes[t][:],
-                    rhs=x_picked[h][:].bitcast(FP8X4),
-                    rhs_scale=x_plane[:, HALF * h : HALF * (h + 1)],
-                    start=True,
-                    stop=True,
-                )
-                banks[t, h] = bank
+        for t, h in ((0, 0), (1, 0), (0, 1), (1, 1), (2, 0), (2, 1), (3, 0), (3, 1)):
+            bank = psum.tile([P, HALF], F32, name=f"h{t}{h}", tag=f"bank{t}{h}")
+            nc.tensor.matmul_mx(
+                out=bank[:],
+                lhsT=w_codes[t][:].bitcast(FP8X4),
+                lhsT_scale=w_planes[t][:],
+                rhs=x_picked[h][:].bitcast(FP8X4),
+                rhs_scale=x_plane[:, HALF * h : HALF * (h + 1)],
+                start=True,
+                stop=True,
+            )
+            banks[t, h] = bank
 
         z_rows = [held.tile([P, PACK, HALF], BF16, name=f"z_rows{h}", align_bytes=64) for h in range(2)]
-        affine = []
+        affine = [held.tile([P, 2], F32, name=f"affine{t}") for t in range(PACK)]
+        rstd = [held.tile([P, 1], F32, name=f"rstd{t}") for t in range(PACK)]
 
-        def statistics(t):
-            stats = held.tile([P, 12], F32, name=f"stats{t}")
-            for h in range(2):
-                nc.vector.bn_stats(stats[:, 6 * h : 6 * (h + 1)], banks[t, h][:])
+        stats = [held.tile([P, 12], F32, name=f"stats{t}") for t in range(PACK)]
+
+        def tally(t, h):
+            nc.vector.bn_stats(stats[t][:, 6 * h : 6 * (h + 1)], banks[t, h][:])
+
+        def stats_vector(t):
             moments = held.tile([P, 2], F32, name=f"moments{t}")
-            nc.vector.bn_aggr(moments[:], stats[:])
-            rstd = held.tile([P, 1], F32, name=f"rstd{t}")
-            nc.scalar.activation(rstd[:], moments[:, 1:2], ACT.Abs_reciprocal_sqrt, bias=EPS)
-            pair = held.tile([P, 2], F32, name=f"pair{t}")
-            nc.gpsimd.tensor_copy(pair[:, 0:1], gain[:, t : t + 1])
-            nc.scalar.activation(pair[:, 1:2], moments[:, 0:1], ACT.Copy, scale=neg_gain[:, t : t + 1])
-            ab = held.tile([P, 2], F32, name=f"affine{t}")
-            nc.scalar.activation(ab[:], pair[:], ACT.Copy, scale=rstd[:])
-            affine.append(ab)
+            nc.vector.bn_aggr(moments[:], stats[t][:])
+            nc.scalar.activation(rstd[t][:], moments[:, 1:2], ACT.Abs_reciprocal_sqrt, bias=EPS)
+            nc.scalar.activation(pairs[t][:, 1:2], moments[:, 0:1], ACT.Copy, scale=neg_gain[:, t : t + 1])
 
-        def normalise(t, h, on_vector):
+        def finish(t):
+            nc.scalar.activation(affine[t][:], pairs[t][:], ACT.Copy, scale=rstd[t][:])
+
+        def normalise(t, h, on_vector, src=None):
             ab = affine[t]
+            src = banks[t, h][:] if src is None else src
             if on_vector:
-                nc.vector.tensor_scalar(z_rows[h][:, t], banks[t, h][:], ab[:, 0:1], ab[:, 1:2], ALU.mult, ALU.add)
+                nc.vector.tensor_scalar(z_rows[h][:, t], src, ab[:, 0:1], ab[:, 1:2], ALU.mult, ALU.add)
             else:
-                nc.scalar.activation(z_rows[h][:, t], banks[t, h][:], ACT.Identity, scale=ab[:, 0:1], bias=ab[:, 1:2])
+                nc.scalar.activation(z_rows[h][:, t], src, ACT.Identity, scale=ab[:, 0:1], bias=ab[:, 1:2])
 
-        statistics(0)
-        for t in range(PACK):
-            normalise(t, 0, False)
-            if t + 1 < PACK:
-                statistics(t + 1)
-            normalise(t, 1, t == PACK - 1)
+        kept = held.tile([P, S], F32, name="kept", align_bytes=64)
+        sums = held.tile([P, 2], F32, name="sums")
+        for h in range(2):
+            nc.scalar.activation(kept[:, HALF * h : HALF * (h + 1)], banks[0, h][:], ACT.Copy, scale=-1.0 / S, accum_out=sums[:, h : h + 1])
+        neg_mean = held.tile([P, 1], F32, name="neg_mean")
+        nc.scalar.activation(neg_mean[:], sums[:, 0:1], ACT.Identity, bias=sums[:, 1:2])
+        tally(1, 0)
+        tally(1, 1)
+        tally(2, 0)
+        stats_vector(1)
+        squares = held.tile([P, S], BF16, name="squares", align_bytes=64)
+        sum_sq = held.tile([P, 1], F32, name="sum_sq")
+        nc.scalar.activation(squares[:], kept[:], ACT.Square, scale=-float(S), bias=neg_mean[:], accum_out=sum_sq[:])
+        finish(1)
+        nc.scalar.activation(pairs[0][:, 1:2], neg_mean[:], ACT.Copy, scale=gain[:, 0:1])
+        nc.scalar.activation(rstd[0][:], sum_sq[:], ACT.Abs_reciprocal_sqrt, scale=1.0 / S, bias=EPS)
+        tally(2, 1)
+        tally(3, 0)
+        stats_vector(2)
+        tally(3, 1)
+        finish(0)
+        finish(2)
+        normalise(1, 0, False)
+        stats_vector(3)
+        finish(3)
+        normalise(2, 0, False)
+        normalise(0, 0, True, kept[:, :HALF])
+        normalise(3, 0, True)
+        normalise(0, 1, True, kept[:, HALF:])
+        normalise(1, 1, False)
+        normalise(2, 1, False)
+        normalise(3, 1, False)
 
         out_view = out.rearrange("(u p) s -> p u s", p=P)
-        n_chunks = S // CHUNK
-        woven = []
-        for c in range(n_chunks):
-            h, lo = divmod(c * CHUNK, HALF)
-            zw = held.tile([P, CHUNK, PACK], BF16, name=f"woven{c}", align_bytes=64)
-            dst = zw[:].rearrange("p (c i) t -> p c t i", i=4)
-            src = z_rows[h][:, :, lo : lo + CHUNK].rearrange("p t (c i) -> p c t i", i=4)
-            if c == 1:
-                nc.scalar.copy(dst, src)
-            else:
+        woven, codes, planes = {}, {}, {}
+
+        def weave(c, lo, n, on_vector):
+            if c not in woven:
+                woven[c] = held.tile([P, CHUNK, PACK], BF16, name=f"woven{c}", align_bytes=64)
+            h, base = divmod(c * CHUNK, HALF)
+            dst = woven[c][:, lo : lo + n].rearrange("p (c i) t -> p c t i", i=4)
+            src = z_rows[h][:, :, base + lo : base + lo + n].rearrange("p t (c i) -> p c t i", i=4)
+            if on_vector:
                 nc.vector.tensor_copy(dst, src)
-            woven.append(zw)
-        for c in range(n_chunks):
-            zc = held.tile([P, CHUNK], U32, name=f"z_codes{c}", align_bytes=64)
-            zp = held.tile([P, CHUNK], U8, name=f"z_plane{c}", align_bytes=64)
-            nc.vector.quantize_mx(out=zc[:].bitcast(FP8X4), scales=zp[:], in_=woven[c][:].rearrange("p n t -> p (n t)"))
-            last = c == n_chunks - 1
-            res = held.tile([P, 2, CHUNK], F32, name=f"res{c}", align_bytes=64)
-            if last:
-                accs = [psum.tile([P, CHUNK], F32, name=f"acc{c}{u}", tag=f"bank{u}1")[:] for u in range(2)]
             else:
-                acc = psum.tile([P, 2, CHUNK], F32, name=f"acc{c}", tag=f"bank{c}0")
+                nc.scalar.copy(dst, src)
+
+        def quantise(c):
+            codes[c] = held.tile([P, CHUNK], U32, name=f"z_codes{c}", align_bytes=64)
+            planes[c] = held.tile([P, CHUNK], U8, name=f"z_plane{c}", align_bytes=64)
+            nc.vector.quantize_mx(out=codes[c][:].bitcast(FP8X4), scales=planes[c][:], in_=woven[c][:].rearrange("p n t -> p (n t)"))
+
+        def project(c, mode):
+            res = held.tile([P, 2, CHUNK], F32, name=f"res{c}", align_bytes=64)
+            if mode == "both":
+                accs = [psum.tile([P, CHUNK], F32, name=f"acc{c}{u}", tag=f"bank{u + 1}1")[:] for u in range(2)]
+            else:
+                acc = psum.tile([P, 2, CHUNK], F32, name=f"acc{c}", tag=("bank00", "bank01", "bank10", "bank20")[c])
                 accs = [acc[:, u] for u in range(2)]
             for u in range(2):
                 nc.tensor.matmul_mx(
                     out=accs[u],
                     lhsT=w2_codes[:, 2 * P * u : 2 * P * (u + 1)].bitcast(FP4X4),
                     lhsT_scale=w2_plane[:, P * u : P * (u + 1)],
-                    rhs=zc[:].bitcast(FP8X4),
-                    rhs_scale=zp[:],
+                    rhs=codes[c][:].bitcast(FP8X4),
+                    rhs_scale=planes[c][:],
                     start=True,
                     stop=True,
                 )
-            if last:
-                nc.scalar.copy(res[:, 0], accs[0])
-                nc.vector.tensor_copy(res[:, 1], accs[1])
+            if mode == "both":
+                cols = slice(c * CHUNK, (c + 1) * CHUNK)
+                nc.vector.tensor_copy(res[:, 0], accs[0])
+                nc.sync.dma_start(out[:P, cols], res[:, 0])
+                nc.scalar.copy(res[:, 1], accs[1])
+                nc.scalar.dma_start(out[P:, cols], res[:, 1])
+                return
+            if mode == "vector":
+                nc.vector.tensor_copy(res[:], acc[:])
             else:
                 nc.scalar.copy(res[:], acc[:])
             nc.sync.dma_start(out_view[:, :, c * CHUNK : (c + 1) * CHUNK], res[:])
+
+        weave(0, 0, 256, True)
+        weave(3, 0, 256, False)
+        weave(1, 0, 256, True)
+        quantise(0)
+        quantise(1)
+        project(0, "scalar")
+        weave(2, 0, 256, True)
+        project(1, "scalar")
+        quantise(3)
+        quantise(2)
+        project(3, "scalar")
+        project(2, "both")

@@ -34,16 +34,17 @@ def tile_picked_inorm_none_p_kernel(tc, x_words, x_scales, w1, w2_words, w2_scal
 
         offsets = held.tile([P, S // 16], U16, name="offsets")
         nc.sync.dma_start(offsets[:], offs)
+        s_table = late.tile([P, T], U8, name="s_table", offset=0, align_bytes=64)
+        for copy in range(2):
+            nc.sync.dma_start(s_table[16 * copy : 16 * (copy + 1), :].bitcast(I32), x_scales[0].bitcast(I32))
+        nc.vector.memset(s_table[32:64, :].bitcast(I32), 0)
+        nc.vector.memset(s_table[64:, :].bitcast(I32), 0)
         x_table = held.tile([P, T], U32, name="x_table", align_bytes=64)
         nc.sync.dma_start(x_table[:].bitcast(I32), x_words[0].rearrange("p n r -> p (n r)").bitcast(I32))
         w_raw = held.tile([P, PACK, H], F32, name="w_raw", align_bytes=64)
         nc.sync.dma_start(w_raw[:], w1.rearrange("(p j) c -> p j c", j=PACK))
         gain = held.tile([P, PACK], F32, name="gain", align_bytes=64)
         nc.sync.dma_start(gain[:], gamma.rearrange("(p t) o -> p (t o)", t=PACK))
-
-        s_table = late.tile([P, T], U8, name="s_table", offset=0, align_bytes=64)
-        nc.vector.memset(s_table[:].bitcast(I32), 0)
-        nc.scalar.dma_start(s_table[0:P:8, :].bitcast(I32), x_scales[0].bitcast(I32))
 
         x_plane = held.tile([P, S], U8, name="x_plane", align_bytes=64)
         nc.vector.memset(x_plane[:].bitcast(I32), 0)
@@ -55,14 +56,7 @@ def tile_picked_inorm_none_p_kernel(tc, x_words, x_scales, w1, w2_words, w2_scal
         s_picked = late.tile([P, S], U8, name="s_picked", offset=T, align_bytes=64)
         nc.vector.tensor_copy(s_picked[:], s_table[:].indirect(offsets[:]))
         for r in range(4):
-            nc.scalar.dma_start(x_plane[r:P:32, :].bitcast(I32), s_picked[8 * r : P : 32, :].bitcast(I32))
-
-        w2_codes = late.tile([P, 2 * N], U8, name="w2_codes", offset=T, align_bytes=64)
-        nc.sync.dma_start(w2_codes[:].bitcast(I32), w2_words[0].bitcast(I32))
-        w2_plane = late.tile([P, N], U8, name="w2_plane", offset=T + 2 * N, align_bytes=64)
-        nc.gpsimd.memset(w2_plane[:].bitcast(I32), 0)
-        for r in range(4):
-            nc.sync.dma_start(w2_plane[r:P:32, :].bitcast(I32), w2_scales[0, r:16:4, :].bitcast(I32))
+            nc.sync.dma_start(x_plane[r:P:32, :].bitcast(I32), s_picked[r:16:4, :].bitcast(I32))
 
         x_picked = []
         for h in range(2):
@@ -75,14 +69,21 @@ def tile_picked_inorm_none_p_kernel(tc, x_words, x_scales, w1, w2_words, w2_scal
             nc.tensor.matmul_mx(
                 out=idle[:],
                 lhsT=x_picked[0][:, :P].bitcast(FP8X4),
-                lhsT_scale=x_plane[:, :P],
+                lhsT_scale=s_picked[:, :P],
                 rhs=x_picked[0][:].bitcast(FP8X4),
-                rhs_scale=x_plane[:, :HALF],
+                rhs_scale=s_picked[:, :HALF],
                 start=True,
                 stop=True,
             )
 
-        w_bf = late.tile([P, PACK, P, PACK], BF16, name="w_bf", offset=T + 3 * N, align_bytes=64)
+        w2_codes = late.tile([P, 2 * N], U8, name="w2_codes", offset=T, align_bytes=64)
+        nc.sync.dma_start(w2_codes[:].bitcast(I32), w2_words[0].bitcast(I32))
+        w2_plane = late.tile([P, N], U8, name="w2_plane", offset=T + 2 * N, align_bytes=64)
+        nc.gpsimd.memset(w2_plane[:].bitcast(I32), 0)
+        for r in range(4):
+            nc.sync.dma_start(w2_plane[r:P:32, :].bitcast(I32), w2_scales[0, r:16:4, :].bitcast(I32))
+
+        w_bf = held.tile([P, PACK, P, PACK], BF16, name="w_bf", align_bytes=64)
         w_dst = w_bf[:].rearrange("p t m j -> p m j t")
         w_src = w_raw[:].rearrange("p j (m t) -> p m j t", t=PACK)
         nc.vector.tensor_copy(w_dst[:, :CAST_SPLIT], w_src[:, :CAST_SPLIT])
@@ -115,7 +116,7 @@ def tile_picked_inorm_none_p_kernel(tc, x_words, x_scales, w1, w2_words, w2_scal
             )
             banks[t, h] = bank
 
-        z_rows = [held.tile([P, PACK, HALF], BF16, name=f"z_rows{h}", align_bytes=64) for h in range(2)]
+        z_rows = [late.tile([P, PACK, CHUNK], BF16, name=f"z_rows{c}", offset=2 * T + 8 * CHUNK * c, align_bytes=64) for c in range(4)]
         affine = [held.tile([P, 2], F32, name=f"affine{t}") for t in range(PACK)]
         rstd = [held.tile([P, 1], F32, name=f"rstd{t}") for t in range(PACK)]
 
@@ -136,10 +137,12 @@ def tile_picked_inorm_none_p_kernel(tc, x_words, x_scales, w1, w2_words, w2_scal
         def normalise(t, h, on_vector, src=None):
             ab = affine[t]
             src = banks[t, h][:] if src is None else src
-            if on_vector:
-                nc.vector.tensor_scalar(z_rows[h][:, t], src, ab[:, 0:1], ab[:, 1:2], ALU.mult, ALU.add)
-            else:
-                nc.scalar.activation(z_rows[h][:, t], src, ACT.Identity, scale=ab[:, 0:1], bias=ab[:, 1:2])
+            for k in range(2):
+                part = src[:, CHUNK * k : CHUNK * (k + 1)]
+                if on_vector:
+                    nc.vector.tensor_scalar(z_rows[2 * h + k][:, t], part, ab[:, 0:1], ab[:, 1:2], ALU.mult, ALU.add)
+                else:
+                    nc.scalar.activation(z_rows[2 * h + k][:, t], part, ACT.Identity, scale=ab[:, 0:1], bias=ab[:, 1:2])
 
         kept = held.tile([P, S], F32, name="kept", align_bytes=64)
         sums = held.tile([P, 2], F32, name="sums")
@@ -169,7 +172,6 @@ def tile_picked_inorm_none_p_kernel(tc, x_words, x_scales, w1, w2_words, w2_scal
         normalise(2, 0, False)
         normalise(0, 0, True, kept[:, :HALF])
         normalise(3, 0, True)
-        normalise(0, 1, True, kept[:, HALF:])
         normalise(1, 1, False)
         normalise(2, 1, False)
         normalise(3, 1, False)
@@ -180,9 +182,8 @@ def tile_picked_inorm_none_p_kernel(tc, x_words, x_scales, w1, w2_words, w2_scal
         def weave(c, lo, n, on_vector):
             if c not in woven:
                 woven[c] = held.tile([P, CHUNK, PACK], BF16, name=f"woven{c}", align_bytes=64)
-            h, base = divmod(c * CHUNK, HALF)
             dst = woven[c][:, lo : lo + n].rearrange("p (c i) t -> p c t i", i=4)
-            src = z_rows[h][:, :, base + lo : base + lo + n].rearrange("p t (c i) -> p c t i", i=4)
+            src = z_rows[c][:, :, lo : lo + n].rearrange("p t (c i) -> p c t i", i=4)
             if on_vector:
                 nc.vector.tensor_copy(dst, src)
             else:
@@ -224,14 +225,16 @@ def tile_picked_inorm_none_p_kernel(tc, x_words, x_scales, w1, w2_words, w2_scal
             nc.sync.dma_start(out_view[:, :, c * CHUNK : (c + 1) * CHUNK], res[:])
 
         weave(0, 0, 256, True)
-        weave(3, 0, 256, False)
-        weave(1, 0, 256, True)
+        normalise(0, 1, True, kept[:, HALF:])
         quantise(0)
-        quantise(1)
         project(0, "scalar")
+        weave(1, 0, 256, True)
+        weave(3, 0, 128, False)
         weave(2, 0, 256, True)
+        quantise(1)
         project(1, "scalar")
-        quantise(3)
         quantise(2)
-        project(3, "scalar")
-        project(2, "both")
+        weave(3, 128, 128, True)
+        project(2, "scalar")
+        quantise(3)
+        project(3, "both")

@@ -21,7 +21,8 @@ P = 128
 PACK = 4
 HALF = 512
 CHUNK = 256
-CAST_SPLIT = 88
+CAST_SPLIT = 84
+X_FIRST = 1536
 WARM = 3
 
 
@@ -33,14 +34,14 @@ def tile_picked_inorm_none_p_kernel(tc, x_words, x_scales, w1, w2_words, w2_scal
         psum = ctx.enter_context(tc.psum_pool(name="psum", bufs=1))
 
         offsets = held.tile([P, S // 16], U16, name="offsets")
-        nc.sync.dma_start(offsets[:], offs)
         s_table = late.tile([P, T], U8, name="s_table", offset=0, align_bytes=64)
-        for copy in range(2):
-            nc.sync.dma_start(s_table[16 * copy : 16 * (copy + 1), :].bitcast(I32), x_scales[0].bitcast(I32))
-        nc.vector.memset(s_table[32:64, :].bitcast(I32), 0)
-        nc.vector.memset(s_table[64:, :].bitcast(I32), 0)
+        nc.vector.memset(s_table[:].bitcast(I32), 0)
         x_table = held.tile([P, T], U32, name="x_table", align_bytes=64)
-        nc.sync.dma_start(x_table[:].bitcast(I32), x_words[0].rearrange("p n r -> p (n r)").bitcast(I32))
+        x_rows = x_words[0].rearrange("p n r -> p (n r)").bitcast(I32)
+        nc.sync.dma_start(x_table[:, :X_FIRST].bitcast(I32), x_rows[:, :X_FIRST])
+        nc.sync.dma_start(offsets[:], offs)
+        nc.sync.dma_start(s_table[0:P:8, :].bitcast(I32), x_scales[0].bitcast(I32))
+        nc.sync.dma_start(x_table[:, X_FIRST:].bitcast(I32), x_rows[:, X_FIRST:])
         w_raw = held.tile([P, PACK, H], F32, name="w_raw", align_bytes=64)
         nc.sync.dma_start(w_raw[:], w1.rearrange("(p j) c -> p j c", j=PACK))
         gain = held.tile([P, PACK], F32, name="gain", align_bytes=64)
@@ -53,19 +54,26 @@ def tile_picked_inorm_none_p_kernel(tc, x_words, x_scales, w1, w2_words, w2_scal
         warm_out = held.tile([P, 1], F32, name="warm_out")
         nc.scalar.activation(warm_out[:], warm_in[:], ACT.Abs_reciprocal_sqrt)
 
-        s_picked = late.tile([P, S], U8, name="s_picked", offset=T, align_bytes=64)
+        s_picked = late.tile([P, S], U8, name="s_picked", offset=2 * T, align_bytes=64)
         nc.vector.tensor_copy(s_picked[:], s_table[:].indirect(offsets[:]))
         for r in range(4):
-            nc.sync.dma_start(x_plane[r:P:32, :].bitcast(I32), s_picked[r:16:4, :].bitcast(I32))
+            nc.sync.dma_start(x_plane[r:P:32, :].bitcast(I32), s_picked[8 * r : P : 32, :].bitcast(I32))
+
+        w2_codes = late.tile([P, 2 * N], U8, name="w2_codes", offset=0, align_bytes=64)
+        nc.sync.dma_start(w2_codes[:].bitcast(I32), w2_words[0].bitcast(I32))
+        w2_plane = late.tile([P, N], U8, name="w2_plane", offset=2 * N, align_bytes=64)
+        nc.vector.memset(w2_plane[:].bitcast(I32), 0)
+        for r in range(4):
+            nc.sync.dma_start(w2_plane[r:P:32, :].bitcast(I32), w2_scales[0, r:16:4, :].bitcast(I32))
 
         x_picked = []
         for h in range(2):
-            xp = late.tile([P, HALF], U32, name=f"x_picked{h}", offset=4 * HALF * h, align_bytes=64)
+            xp = late.tile([P, HALF], U32, name=f"x_picked{h}", offset=4 * N + 4 * HALF * h, align_bytes=64)
             nc.vector.tensor_copy(xp[:], x_table[:].indirect(offsets[:, 32 * h : 32 * (h + 1)]))
             x_picked.append(xp)
 
         for i in range(WARM):
-            idle = psum.tile([P, HALF], F32, name=f"idle{i}", tag="bank31")
+            idle = psum.tile([P, HALF], F32, name=f"idle{i}", tag=("bank21", "bank30", "bank31")[i])
             nc.tensor.matmul_mx(
                 out=idle[:],
                 lhsT=x_picked[0][:, :P].bitcast(FP8X4),
@@ -75,13 +83,6 @@ def tile_picked_inorm_none_p_kernel(tc, x_words, x_scales, w1, w2_words, w2_scal
                 start=True,
                 stop=True,
             )
-
-        w2_codes = late.tile([P, 2 * N], U8, name="w2_codes", offset=T, align_bytes=64)
-        nc.sync.dma_start(w2_codes[:].bitcast(I32), w2_words[0].bitcast(I32))
-        w2_plane = late.tile([P, N], U8, name="w2_plane", offset=T + 2 * N, align_bytes=64)
-        nc.gpsimd.memset(w2_plane[:].bitcast(I32), 0)
-        for r in range(4):
-            nc.sync.dma_start(w2_plane[r:P:32, :].bitcast(I32), w2_scales[0, r:16:4, :].bitcast(I32))
 
         w_bf = held.tile([P, PACK, P, PACK], BF16, name="w_bf", align_bytes=64)
         w_dst = w_bf[:].rearrange("p t m j -> p m j t")
@@ -97,10 +98,11 @@ def tile_picked_inorm_none_p_kernel(tc, x_words, x_scales, w1, w2_words, w2_scal
             w_planes.append(wp)
 
         neg_gain = held.tile([P, PACK], F32, name="neg_gain")
-        nc.gpsimd.tensor_scalar(neg_gain[:], gain[:], -1.0, 0.0, ALU.mult, ALU.add)
-        pairs = [held.tile([P, 2], F32, name=f"pair{t}") for t in range(PACK)]
-        for t in range(PACK):
-            nc.gpsimd.tensor_scalar(pairs[t][:, 0:1], gain[:, t : t + 1], -float(S) if t == 0 else 1.0, 0.0, ALU.mult, ALU.add)
+        nc.scalar.activation(neg_gain[:], gain[:], ACT.Copy, scale=-1.0)
+        pair_tile = held.tile([P, PACK, 2], F32, name="pair_tile")
+        pairs = [pair_tile[:, t] for t in range(PACK)]
+        nc.scalar.activation(pair_tile[:, 0:1, 0], gain[:, 0:1], ACT.Copy, scale=-float(S))
+        nc.scalar.activation(pair_tile[:, 1:, 0], gain[:, 1:], ACT.Copy)
 
         banks = {}
         for t, h in ((0, 0), (1, 0), (0, 1), (1, 1), (2, 0), (2, 1), (3, 0), (3, 1)):
@@ -116,7 +118,7 @@ def tile_picked_inorm_none_p_kernel(tc, x_words, x_scales, w1, w2_words, w2_scal
             )
             banks[t, h] = bank
 
-        z_rows = [late.tile([P, PACK, CHUNK], BF16, name=f"z_rows{c}", offset=2 * T + 8 * CHUNK * c, align_bytes=64) for c in range(4)]
+        z_rows = [held.tile([P, 2, PACK, CHUNK], BF16, name=f"z_rows{h}", align_bytes=64) for h in range(2)]
         affine = [held.tile([P, 2], F32, name=f"affine{t}") for t in range(PACK)]
         rstd = [held.tile([P, 1], F32, name=f"rstd{t}") for t in range(PACK)]
 
@@ -132,17 +134,19 @@ def tile_picked_inorm_none_p_kernel(tc, x_words, x_scales, w1, w2_words, w2_scal
             nc.scalar.activation(pairs[t][:, 1:2], moments[:, 0:1], ACT.Copy, scale=neg_gain[:, t : t + 1])
 
         def finish(t):
-            nc.scalar.activation(affine[t][:], pairs[t][:], ACT.Copy, scale=rstd[t][:])
+            nc.scalar.activation(affine[t][:], pairs[t], ACT.Copy, scale=rstd[t][:])
 
-        def normalise(t, h, on_vector, src=None):
+        def normalise(t, h, on_vector, src=None, parts=1):
             ab = affine[t]
             src = banks[t, h][:] if src is None else src
-            for k in range(2):
-                part = src[:, CHUNK * k : CHUNK * (k + 1)]
+            n = 2 // parts
+            for k in range(parts):
+                part = src.rearrange("p (k n) -> p k n", k=2)[:, n * k : n * (k + 1)]
+                dst = z_rows[h][:, n * k : n * (k + 1), t]
                 if on_vector:
-                    nc.vector.tensor_scalar(z_rows[2 * h + k][:, t], part, ab[:, 0:1], ab[:, 1:2], ALU.mult, ALU.add)
+                    nc.vector.tensor_scalar(dst, part, ab[:, 0:1], ab[:, 1:2], ALU.mult, ALU.add)
                 else:
-                    nc.scalar.activation(z_rows[2 * h + k][:, t], part, ACT.Identity, scale=ab[:, 0:1], bias=ab[:, 1:2])
+                    nc.scalar.activation(dst, part, ACT.Identity, scale=ab[:, 0:1], bias=ab[:, 1:2])
 
         kept = held.tile([P, S], F32, name="kept", align_bytes=64)
         sums = held.tile([P, 2], F32, name="sums")
@@ -171,35 +175,40 @@ def tile_picked_inorm_none_p_kernel(tc, x_words, x_scales, w1, w2_words, w2_scal
         finish(3)
         normalise(2, 0, False)
         normalise(0, 0, True, kept[:, :HALF])
-        normalise(3, 0, True)
+        normalise(3, 0, True, parts=2)
         normalise(1, 1, False)
         normalise(2, 1, False)
         normalise(3, 1, False)
 
         out_view = out.rearrange("(u p) s -> p u s", p=P)
+        widths = (256, 256, 256, 128, 128)
+        starts = [sum(widths[:c]) for c in range(len(widths))]
+        free_banks = ("bank00", "bank01", "bank11", "bank21", "bank10")
         woven, codes, planes = {}, {}, {}
 
-        def weave(c, lo, n, on_vector):
-            if c not in woven:
-                woven[c] = held.tile([P, CHUNK, PACK], BF16, name=f"woven{c}", align_bytes=64)
-            dst = woven[c][:, lo : lo + n].rearrange("p (c i) t -> p c t i", i=4)
-            src = z_rows[c][:, :, lo : lo + n].rearrange("p t (c i) -> p c t i", i=4)
+        def weave(c, on_vector):
+            woven[c] = held.tile([P, widths[c], PACK], BF16, name=f"woven{c}", align_bytes=64)
+            dst = woven[c][:].rearrange("p (c i) t -> p c t i", i=4)
+            h, k, lo = starts[c] // HALF, starts[c] % HALF // CHUNK, starts[c] % CHUNK
+            src = z_rows[h][:, k, :, lo : lo + widths[c]].rearrange("p t (c i) -> p c t i", i=4)
             if on_vector:
                 nc.vector.tensor_copy(dst, src)
             else:
                 nc.scalar.copy(dst, src)
 
         def quantise(c):
-            codes[c] = held.tile([P, CHUNK], U32, name=f"z_codes{c}", align_bytes=64)
-            planes[c] = held.tile([P, CHUNK], U8, name=f"z_plane{c}", align_bytes=64)
+            codes[c] = held.tile([P, widths[c]], U32, name=f"z_codes{c}", align_bytes=64)
+            planes[c] = held.tile([P, widths[c]], U8, name=f"z_plane{c}", align_bytes=64)
             nc.vector.quantize_mx(out=codes[c][:].bitcast(FP8X4), scales=planes[c][:], in_=woven[c][:].rearrange("p n t -> p (n t)"))
 
         def project(c, mode):
-            res = held.tile([P, 2, CHUNK], F32, name=f"res{c}", align_bytes=64)
+            n = widths[c]
+            cols = slice(starts[c], starts[c] + n)
+            res = held.tile([P, 2, n], F32, name=f"res{c}", align_bytes=64)
             if mode == "both":
-                accs = [psum.tile([P, CHUNK], F32, name=f"acc{c}{u}", tag=f"bank{u + 1}1")[:] for u in range(2)]
+                accs = [psum.tile([P, n], F32, name=f"acc{c}{u}", tag=free_banks[c + u])[:] for u in range(2)]
             else:
-                acc = psum.tile([P, 2, CHUNK], F32, name=f"acc{c}", tag=("bank00", "bank01", "bank10", "bank20")[c])
+                acc = psum.tile([P, 2, n], F32, name=f"acc{c}", tag="bank20" if c == 3 else free_banks[c])
                 accs = [acc[:, u] for u in range(2)]
             for u in range(2):
                 nc.tensor.matmul_mx(
@@ -212,7 +221,6 @@ def tile_picked_inorm_none_p_kernel(tc, x_words, x_scales, w1, w2_words, w2_scal
                     stop=True,
                 )
             if mode == "both":
-                cols = slice(c * CHUNK, (c + 1) * CHUNK)
                 nc.vector.tensor_copy(res[:, 0], accs[0])
                 nc.sync.dma_start(out[:P, cols], res[:, 0])
                 nc.scalar.copy(res[:, 1], accs[1])
@@ -222,19 +230,21 @@ def tile_picked_inorm_none_p_kernel(tc, x_words, x_scales, w1, w2_words, w2_scal
                 nc.vector.tensor_copy(res[:], acc[:])
             else:
                 nc.scalar.copy(res[:], acc[:])
-            nc.sync.dma_start(out_view[:, :, c * CHUNK : (c + 1) * CHUNK], res[:])
+            nc.sync.dma_start(out_view[:, :, cols], res[:])
 
-        weave(0, 0, 256, True)
+        weave(0, True)
         normalise(0, 1, True, kept[:, HALF:])
         quantise(0)
+        weave(3, False)
         project(0, "scalar")
-        weave(1, 0, 256, True)
-        weave(3, 0, 128, False)
-        weave(2, 0, 256, True)
-        quantise(1)
-        project(1, "scalar")
-        quantise(2)
-        weave(3, 128, 128, True)
-        project(2, "scalar")
+        weave(1, True)
         quantise(3)
-        project(3, "both")
+        weave(4, False)
+        quantise(1)
+        weave(2, True)
+        project(3, "scalar")
+        project(1, "scalar")
+        quantise(4)
+        quantise(2)
+        project(4, "scalar")
+        project(2, "both")

@@ -21,9 +21,9 @@ P = 128
 PACK = 4
 HALF = 512
 CHUNK = 256
-CAST_SPLIT = 84
+W_PIECES = (0, 48, 96, 128)
+CAST_SPLIT = 118
 X_FIRST = 1536
-WARM = 3
 
 
 def tile_picked_inorm_none_p_kernel(tc, x_words, x_scales, w1, w2_words, w2_scales, gamma, offs, out):
@@ -42,8 +42,12 @@ def tile_picked_inorm_none_p_kernel(tc, x_words, x_scales, w1, w2_words, w2_scal
         nc.sync.dma_start(offsets[:], offs)
         nc.sync.dma_start(s_table[0:P:8, :].bitcast(I32), x_scales[0].bitcast(I32))
         nc.sync.dma_start(x_table[:, X_FIRST:].bitcast(I32), x_rows[:, X_FIRST:])
-        w_raw = held.tile([P, PACK, H], F32, name="w_raw", align_bytes=64)
-        nc.sync.dma_start(w_raw[:], w1.rearrange("(p j) c -> p j c", j=PACK))
+        w_rows = w1.rearrange("(p j) c -> p j c", j=PACK)
+        w_src = []
+        for lo, hi in zip(W_PIECES, W_PIECES[1:]):
+            piece = held.tile([P, PACK, PACK * (hi - lo)], F32, name=f"w_raw{lo}", align_bytes=64)
+            nc.sync.dma_start(piece[:], w_rows[:, :, PACK * lo : PACK * hi])
+            w_src.append(piece[:].rearrange("p j (m t) -> p m j t", t=PACK))
         gain = held.tile([P, PACK], F32, name="gain", align_bytes=64)
         nc.sync.dma_start(gain[:], gamma.rearrange("(p t) o -> p (t o)", t=PACK))
 
@@ -53,6 +57,8 @@ def tile_picked_inorm_none_p_kernel(tc, x_words, x_scales, w1, w2_words, w2_scal
         nc.vector.memset(warm_in[:], 1.0)
         warm_out = held.tile([P, 1], F32, name="warm_out")
         nc.scalar.activation(warm_out[:], warm_in[:], ACT.Abs_reciprocal_sqrt)
+        tallies = held.tile([P, 2, 3], F32, name="tallies")
+        nc.vector.memset(tallies[:, :, 0], float(HALF))
 
         s_picked = late.tile([P, S], U8, name="s_picked", offset=2 * T, align_bytes=64)
         nc.vector.tensor_copy(s_picked[:], s_table[:].indirect(offsets[:]))
@@ -72,8 +78,8 @@ def tile_picked_inorm_none_p_kernel(tc, x_words, x_scales, w1, w2_words, w2_scal
             nc.vector.tensor_copy(xp[:], x_table[:].indirect(offsets[:, 32 * h : 32 * (h + 1)]))
             x_picked.append(xp)
 
-        for i in range(WARM):
-            idle = psum.tile([P, HALF], F32, name=f"idle{i}", tag=("bank21", "bank30", "bank31")[i])
+        def warm_up(tag):
+            idle = psum.tile([P, HALF], F32, name="idle", tag=tag)
             nc.tensor.matmul_mx(
                 out=idle[:],
                 lhsT=x_picked[0][:, :P].bitcast(FP8X4),
@@ -84,11 +90,16 @@ def tile_picked_inorm_none_p_kernel(tc, x_words, x_scales, w1, w2_words, w2_scal
                 stop=True,
             )
 
+        warm_up("bank30")
+        warm_up("bank31")
+
         w_bf = held.tile([P, PACK, P, PACK], BF16, name="w_bf", align_bytes=64)
         w_dst = w_bf[:].rearrange("p t m j -> p m j t")
-        w_src = w_raw[:].rearrange("p j (m t) -> p m j t", t=PACK)
-        nc.vector.tensor_copy(w_dst[:, :CAST_SPLIT], w_src[:, :CAST_SPLIT])
-        nc.scalar.copy(w_dst[:, CAST_SPLIT:], w_src[:, CAST_SPLIT:])
+        for i in range(2):
+            nc.scalar.copy(w_dst[:, W_PIECES[i] : W_PIECES[i + 1]], w_src[i])
+        last = W_PIECES[2]
+        nc.vector.tensor_copy(w_dst[:, last:CAST_SPLIT], w_src[2][:, : CAST_SPLIT - last])
+        nc.scalar.copy(w_dst[:, CAST_SPLIT:], w_src[2][:, CAST_SPLIT - last :])
         w_codes, w_planes = [], []
         for t in range(PACK):
             wc = held.tile([P, P], U32, name=f"w_codes{t}", align_bytes=64)
@@ -101,7 +112,7 @@ def tile_picked_inorm_none_p_kernel(tc, x_words, x_scales, w1, w2_words, w2_scal
         nc.scalar.activation(neg_gain[:], gain[:], ACT.Copy, scale=-1.0)
         pair_tile = held.tile([P, PACK, 2], F32, name="pair_tile")
         pairs = [pair_tile[:, t] for t in range(PACK)]
-        nc.scalar.activation(pair_tile[:, 0:1, 0], gain[:, 0:1], ACT.Copy, scale=-float(S))
+        nc.scalar.activation(pair_tile[:, 0:1, 0], gain[:, 0:1], ACT.Copy, scale=float(HALF))
         nc.scalar.activation(pair_tile[:, 1:, 0], gain[:, 1:], ACT.Copy)
 
         banks = {}
@@ -121,77 +132,89 @@ def tile_picked_inorm_none_p_kernel(tc, x_words, x_scales, w1, w2_words, w2_scal
         z_rows = [held.tile([P, 2, PACK, CHUNK], BF16, name=f"z_rows{h}", align_bytes=64) for h in range(2)]
         affine = [held.tile([P, 2], F32, name=f"affine{t}") for t in range(PACK)]
         rstd = [held.tile([P, 1], F32, name=f"rstd{t}") for t in range(PACK)]
-
-        stats = [held.tile([P, 12], F32, name=f"stats{t}") for t in range(PACK)]
+        moments = [held.tile([P, 2], F32, name=f"moments{t}") for t in range(PACK)]
+        stats = {t: held.tile([P, 12], F32, name=f"stats{t}") for t in range(1, PACK)}
 
         def tally(t, h):
             nc.vector.bn_stats(stats[t][:, 6 * h : 6 * (h + 1)], banks[t, h][:])
 
-        def stats_vector(t):
-            moments = held.tile([P, 2], F32, name=f"moments{t}")
-            nc.vector.bn_aggr(moments[:], stats[t][:])
-            nc.scalar.activation(rstd[t][:], moments[:, 1:2], ACT.Abs_reciprocal_sqrt, bias=EPS)
-            nc.scalar.activation(pairs[t][:, 1:2], moments[:, 0:1], ACT.Copy, scale=neg_gain[:, t : t + 1])
+        def aggregate(t):
+            src = tallies[:].rearrange("p h c -> p (h c)") if t == 0 else stats[t][:]
+            nc.vector.bn_aggr(moments[t][:], src)
+
+        def factors(t):
+            nc.scalar.activation(rstd[t][:], moments[t][:, 1:2], ACT.Abs_reciprocal_sqrt, bias=EPS)
+            nc.scalar.activation(pairs[t][:, 1:2], moments[t][:, 0:1], ACT.Copy, scale=neg_gain[:, t : t + 1])
 
         def finish(t):
             nc.scalar.activation(affine[t][:], pairs[t], ACT.Copy, scale=rstd[t][:])
 
-        def normalise(t, h, on_vector, src=None, parts=1):
+        def normalise(t, h, engine, parts=(0, 1)):
             ab = affine[t]
-            src = banks[t, h][:] if src is None else src
-            n = 2 // parts
-            for k in range(parts):
-                part = src.rearrange("p (k n) -> p k n", k=2)[:, n * k : n * (k + 1)]
-                dst = z_rows[h][:, n * k : n * (k + 1), t]
-                if on_vector:
-                    nc.vector.tensor_scalar(dst, part, ab[:, 0:1], ab[:, 1:2], ALU.mult, ALU.add)
-                else:
-                    nc.scalar.activation(dst, part, ACT.Identity, scale=ab[:, 0:1], bias=ab[:, 1:2])
+            src = kept[h][:] if t == 0 else banks[t, h][:]
+            ks = slice(parts[0], parts[-1] + 1)
+            part = src.rearrange("p (k n) -> p k n", k=2)[:, ks]
+            dst = z_rows[h][:, ks, t]
+            if engine is nc.scalar:
+                nc.scalar.activation(dst, part, ACT.Identity, scale=ab[:, 0:1], bias=ab[:, 1:2])
+            else:
+                engine.tensor_scalar(dst, part, ab[:, 0:1], ab[:, 1:2], ALU.mult, ALU.add)
 
-        kept = held.tile([P, S], F32, name="kept", align_bytes=64)
-        sums = held.tile([P, 2], F32, name="sums")
-        for h in range(2):
-            nc.scalar.activation(kept[:, HALF * h : HALF * (h + 1)], banks[0, h][:], ACT.Copy, scale=-1.0 / S, accum_out=sums[:, h : h + 1])
-        neg_mean = held.tile([P, 1], F32, name="neg_mean")
-        nc.scalar.activation(neg_mean[:], sums[:, 0:1], ACT.Identity, bias=sums[:, 1:2])
+        kept = [held.tile([P, HALF], F32, name=f"kept{h}", align_bytes=64) for h in range(2)]
+        squares = [held.tile([P, HALF], BF16, name=f"squares{h}", align_bytes=64) for h in range(2)]
+
+        def keep(h):
+            nc.scalar.activation(kept[h][:], banks[0, h][:], ACT.Copy, scale=1.0 / HALF, accum_out=tallies[:, h, 1:2])
+
+        def spread(h):
+            nc.scalar.activation(squares[h][:], kept[h][:], ACT.Square, scale=-float(HALF), bias=tallies[:, h, 1:2], accum_out=tallies[:, h, 2:3])
+
+        keep(0)
+        keep(1)
+        spread(0)
         tally(1, 0)
         tally(1, 1)
-        tally(2, 0)
-        stats_vector(1)
-        squares = held.tile([P, S], BF16, name="squares", align_bytes=64)
-        sum_sq = held.tile([P, 1], F32, name="sum_sq")
-        nc.scalar.activation(squares[:], kept[:], ACT.Square, scale=-float(S), bias=neg_mean[:], accum_out=sum_sq[:])
+        aggregate(1)
+        factors(1)
+        spread(1)
         finish(1)
-        nc.scalar.activation(pairs[0][:, 1:2], neg_mean[:], ACT.Copy, scale=gain[:, 0:1])
-        nc.scalar.activation(rstd[0][:], sum_sq[:], ACT.Abs_reciprocal_sqrt, scale=1.0 / S, bias=EPS)
+        tally(2, 0)
         tally(2, 1)
+        aggregate(0)
+        aggregate(2)
+        normalise(1, 0, nc.scalar)
+        factors(0)
+        factors(2)
         tally(3, 0)
-        stats_vector(2)
         tally(3, 1)
+        aggregate(3)
+        normalise(1, 1, nc.scalar, (0,))
         finish(0)
         finish(2)
-        normalise(1, 0, False)
-        stats_vector(3)
+        factors(3)
+        normalise(1, 1, nc.vector, (1,))
+        normalise(2, 0, nc.scalar, (0,))
         finish(3)
-        normalise(2, 0, False)
-        normalise(0, 0, True, kept[:, :HALF])
-        normalise(3, 0, True, parts=2)
-        normalise(1, 1, False)
-        normalise(2, 1, False)
-        normalise(3, 1, False)
+        normalise(0, 0, nc.vector)
+        normalise(0, 1, nc.vector)
+        normalise(3, 0, nc.vector, (0,))
+        normalise(2, 0, nc.scalar, (1,))
+        normalise(3, 0, nc.vector, (1,))
+        normalise(2, 1, nc.scalar)
+        normalise(3, 1, nc.scalar)
 
-        out_view = out.rearrange("(u p) s -> p u s", p=P)
-        widths = (256, 256, 256, 128, 128)
+        warm_up("bank31")
+        widths = (128, 128, 256, 256, 128, 128)
         starts = [sum(widths[:c]) for c in range(len(widths))]
-        free_banks = ("bank00", "bank01", "bank11", "bank21", "bank10")
         woven, codes, planes = {}, {}, {}
+        res = [[held.tile([P, CHUNK], F32, name=f"res{b}{u}", align_bytes=64) for u in range(2)] for b in range(S // CHUNK)]
 
-        def weave(c, on_vector):
+        def weave(c, engine):
             woven[c] = held.tile([P, widths[c], PACK], BF16, name=f"woven{c}", align_bytes=64)
             dst = woven[c][:].rearrange("p (c i) t -> p c t i", i=4)
             h, k, lo = starts[c] // HALF, starts[c] % HALF // CHUNK, starts[c] % CHUNK
             src = z_rows[h][:, k, :, lo : lo + widths[c]].rearrange("p t (c i) -> p c t i", i=4)
-            if on_vector:
+            if engine is nc.vector:
                 nc.vector.tensor_copy(dst, src)
             else:
                 nc.scalar.copy(dst, src)
@@ -201,18 +224,13 @@ def tile_picked_inorm_none_p_kernel(tc, x_words, x_scales, w1, w2_words, w2_scal
             planes[c] = held.tile([P, widths[c]], U8, name=f"z_plane{c}", align_bytes=64)
             nc.vector.quantize_mx(out=codes[c][:].bitcast(FP8X4), scales=planes[c][:], in_=woven[c][:].rearrange("p n t -> p (n t)"))
 
-        def project(c, mode):
-            n = widths[c]
-            cols = slice(starts[c], starts[c] + n)
-            res = held.tile([P, 2, n], F32, name=f"res{c}", align_bytes=64)
-            if mode == "both":
-                accs = [psum.tile([P, n], F32, name=f"acc{c}{u}", tag=free_banks[c + u])[:] for u in range(2)]
-            else:
-                acc = psum.tile([P, 2, n], F32, name=f"acc{c}", tag="bank20" if c == 3 else free_banks[c])
-                accs = [acc[:, u] for u in range(2)]
-            for u in range(2):
+        def project(chunks, u, engine, tag):
+            first = starts[chunks[0]]
+            n = sum(widths[c] for c in chunks)
+            acc = psum.tile([P, n], F32, name=f"acc{chunks[0]}{u}", tag=tag)
+            for c in chunks:
                 nc.tensor.matmul_mx(
-                    out=accs[u],
+                    out=acc[:, starts[c] - first : starts[c] - first + widths[c]],
                     lhsT=w2_codes[:, 2 * P * u : 2 * P * (u + 1)].bitcast(FP4X4),
                     lhsT_scale=w2_plane[:, P * u : P * (u + 1)],
                     rhs=codes[c][:].bitcast(FP8X4),
@@ -220,31 +238,38 @@ def tile_picked_inorm_none_p_kernel(tc, x_words, x_scales, w1, w2_words, w2_scal
                     start=True,
                     stop=True,
                 )
-            if mode == "both":
-                nc.vector.tensor_copy(res[:, 0], accs[0])
-                nc.sync.dma_start(out[:P, cols], res[:, 0])
-                nc.scalar.copy(res[:, 1], accs[1])
-                nc.scalar.dma_start(out[P:, cols], res[:, 1])
-                return
-            if mode == "vector":
-                nc.vector.tensor_copy(res[:], acc[:])
+            dst = res[first // CHUNK][u][:, first % CHUNK : first % CHUNK + n]
+            if engine is nc.vector:
+                nc.vector.tensor_copy(dst, acc[:])
             else:
-                nc.scalar.copy(res[:], acc[:])
-            nc.sync.dma_start(out_view[:, :, cols], res[:])
+                nc.scalar.copy(dst, acc[:])
 
-        weave(0, True)
-        normalise(0, 1, True, kept[:, HALF:])
+        def store(b, u):
+            nc.sync.dma_start(out[P * u : P * (u + 1), CHUNK * b : CHUNK * (b + 1)], res[b][u][:])
+
+        weave(0, nc.vector)
+        weave(1, nc.vector)
         quantise(0)
-        weave(3, False)
-        project(0, "scalar")
-        weave(1, True)
-        quantise(3)
-        weave(4, False)
         quantise(1)
-        weave(2, True)
-        project(3, "scalar")
-        project(1, "scalar")
-        quantise(4)
+        weave(3, nc.scalar)
+        for u in range(2):
+            project((0, 1), u, nc.scalar, f"bank0{u}")
+            store(0, u)
+        weave(2, nc.vector)
+        weave(4, nc.vector)
         quantise(2)
-        project(4, "scalar")
-        project(2, "both")
+        quantise(3)
+        for u in range(2):
+            project((2,), u, nc.scalar, f"bank1{u}")
+            store(1, u)
+        weave(5, nc.vector)
+        quantise(4)
+        quantise(5)
+        for u, engine in enumerate((nc.scalar, nc.vector)):
+            project((3,), u, engine, f"bank2{u}")
+            store(2, u)
+        for u, engine in enumerate((nc.scalar, nc.vector)):
+            project((4,), u, engine, f"bank0{u}")
+        for u, engine in enumerate((nc.scalar, nc.vector)):
+            project((5,), u, engine, f"bank3{u}")
+            store(3, u)

@@ -21,8 +21,7 @@ P = 128
 PACK = 4
 HALF = 512
 CHUNK = 256
-W_PIECES = (0, 48, 96, 128)
-CAST_SPLIT = 118
+CAST_SPLIT = 84
 X_FIRST = 1536
 
 
@@ -43,11 +42,8 @@ def tile_picked_inorm_none_p_kernel(tc, x_words, x_scales, w1, w2_words, w2_scal
         nc.sync.dma_start(s_table[0:P:8, :].bitcast(I32), x_scales[0].bitcast(I32))
         nc.sync.dma_start(x_table[:, X_FIRST:].bitcast(I32), x_rows[:, X_FIRST:])
         w_rows = w1.rearrange("(p j) c -> p j c", j=PACK)
-        w_src = []
-        for lo, hi in zip(W_PIECES, W_PIECES[1:]):
-            piece = held.tile([P, PACK, PACK * (hi - lo)], F32, name=f"w_raw{lo}", align_bytes=64)
-            nc.sync.dma_start(piece[:], w_rows[:, :, PACK * lo : PACK * hi])
-            w_src.append(piece[:].rearrange("p j (m t) -> p m j t", t=PACK))
+        w_raw = held.tile([P, PACK, H], F32, name="w_raw", align_bytes=64)
+        nc.sync.dma_start(w_raw[:], w_rows)
         gain = held.tile([P, PACK], F32, name="gain", align_bytes=64)
         nc.sync.dma_start(gain[:], gamma.rearrange("(p t) o -> p (t o)", t=PACK))
 
@@ -63,7 +59,7 @@ def tile_picked_inorm_none_p_kernel(tc, x_words, x_scales, w1, w2_words, w2_scal
         s_picked = late.tile([P, S], U8, name="s_picked", offset=2 * T, align_bytes=64)
         nc.vector.tensor_copy(s_picked[:], s_table[:].indirect(offsets[:]))
         for r in range(4):
-            nc.sync.dma_start(x_plane[r:P:32, :].bitcast(I32), s_picked[8 * r : P : 32, :].bitcast(I32))
+            nc.scalar.dma_start(x_plane[r:P:32, :].bitcast(I32), s_picked[8 * r : P : 32, :].bitcast(I32))
 
         w2_codes = late.tile([P, 2 * N], U8, name="w2_codes", offset=0, align_bytes=64)
         nc.sync.dma_start(w2_codes[:].bitcast(I32), w2_words[0].bitcast(I32))
@@ -90,16 +86,15 @@ def tile_picked_inorm_none_p_kernel(tc, x_words, x_scales, w1, w2_words, w2_scal
                 stop=True,
             )
 
+        warm_up("bank21")
         warm_up("bank30")
         warm_up("bank31")
 
         w_bf = held.tile([P, PACK, P, PACK], BF16, name="w_bf", align_bytes=64)
         w_dst = w_bf[:].rearrange("p t m j -> p m j t")
-        for i in range(2):
-            nc.scalar.copy(w_dst[:, W_PIECES[i] : W_PIECES[i + 1]], w_src[i])
-        last = W_PIECES[2]
-        nc.vector.tensor_copy(w_dst[:, last:CAST_SPLIT], w_src[2][:, : CAST_SPLIT - last])
-        nc.scalar.copy(w_dst[:, CAST_SPLIT:], w_src[2][:, CAST_SPLIT - last :])
+        w_src = w_raw[:].rearrange("p j (m t) -> p m j t", t=PACK)
+        nc.vector.tensor_copy(w_dst[:, :CAST_SPLIT], w_src[:, :CAST_SPLIT])
+        nc.scalar.copy(w_dst[:, CAST_SPLIT:], w_src[:, CAST_SPLIT:])
         w_codes, w_planes = [], []
         for t in range(PACK):
             wc = held.tile([P, P], U32, name=f"w_codes{t}", align_bytes=64)
@@ -203,7 +198,6 @@ def tile_picked_inorm_none_p_kernel(tc, x_words, x_scales, w1, w2_words, w2_scal
         normalise(2, 1, nc.scalar)
         normalise(3, 1, nc.scalar)
 
-        warm_up("bank31")
         widths = (128, 128, 256, 256, 128, 128)
         starts = [sum(widths[:c]) for c in range(len(widths))]
         woven, codes, planes = {}, {}, {}

@@ -21,8 +21,7 @@ P = 128
 PACK = 4
 HALF = 512
 CHUNK = 256
-CAST_SPLIT = 84
-X_FIRST = 1536
+CAST_SPLIT = 64
 
 
 def tile_picked_inorm_none_p_kernel(tc, x_words, x_scales, w1, w2_words, w2_scales, gamma, offs, out):
@@ -32,18 +31,17 @@ def tile_picked_inorm_none_p_kernel(tc, x_words, x_scales, w1, w2_words, w2_scal
         late = ctx.enter_context(tc.tile_pool(name="late", bufs=1))
         psum = ctx.enter_context(tc.psum_pool(name="psum", bufs=1))
 
-        offsets = held.tile([P, S // 16], U16, name="offsets")
-        s_table = late.tile([P, T], U8, name="s_table", offset=0, align_bytes=64)
+        s_table = held.tile([P, T], U8, name="s_table", align_bytes=64)
         nc.vector.memset(s_table[:].bitcast(I32), 0)
-        x_table = held.tile([P, T], U32, name="x_table", align_bytes=64)
-        x_rows = x_words[0].rearrange("p n r -> p (n r)").bitcast(I32)
-        nc.sync.dma_start(x_table[:, :X_FIRST].bitcast(I32), x_rows[:, :X_FIRST])
+        w_raw = held.tile([P, PACK, H], F32, name="w_raw", align_bytes=64)
+        w_rows = w1.rearrange("(p j) c -> p j c", j=PACK)
+        nc.sync.dma_start(w_raw[:, :2], w_rows[:, :2])
+        offsets = held.tile([P, S // 16], U16, name="offsets")
         nc.sync.dma_start(offsets[:], offs)
         nc.sync.dma_start(s_table[0:P:8, :].bitcast(I32), x_scales[0].bitcast(I32))
-        nc.sync.dma_start(x_table[:, X_FIRST:].bitcast(I32), x_rows[:, X_FIRST:])
-        w_rows = w1.rearrange("(p j) c -> p j c", j=PACK)
-        w_raw = held.tile([P, PACK, H], F32, name="w_raw", align_bytes=64)
-        nc.sync.dma_start(w_raw[:], w_rows)
+        nc.sync.dma_start(w_raw[:, 2:], w_rows[:, 2:])
+        x_table = late.tile([P, T], U32, name="x_table", offset=0, align_bytes=64)
+        nc.sync.dma_start(x_table[:].bitcast(I32), x_words[0].rearrange("p n r -> p (n r)").bitcast(I32))
         gain = held.tile([P, PACK], F32, name="gain", align_bytes=64)
         nc.sync.dma_start(gain[:], gamma.rearrange("(p t) o -> p (t o)", t=PACK))
 
@@ -53,13 +51,61 @@ def tile_picked_inorm_none_p_kernel(tc, x_words, x_scales, w1, w2_words, w2_scal
         nc.vector.memset(warm_in[:], 1.0)
         warm_out = held.tile([P, 1], F32, name="warm_out")
         nc.scalar.activation(warm_out[:], warm_in[:], ACT.Abs_reciprocal_sqrt)
-        tallies = held.tile([P, 2, 3], F32, name="tallies")
-        nc.vector.memset(tallies[:, :, 0], float(HALF))
+        KEPT = ((0, 0), (1, 0), (3, 0))
+        stats = [held.tile([P, 12], F32, name=f"stats{t}") for t in range(PACK)]
+        for t, h in KEPT:
+            nc.vector.memset(stats[t][:, 3:4], float(HALF))
 
-        s_picked = late.tile([P, S], U8, name="s_picked", offset=2 * T, align_bytes=64)
+        s_picked = held.tile([P, S], U8, name="s_picked", align_bytes=64)
         nc.vector.tensor_copy(s_picked[:], s_table[:].indirect(offsets[:]))
         for r in range(4):
-            nc.scalar.dma_start(x_plane[r:P:32, :].bitcast(I32), s_picked[8 * r : P : 32, :].bitcast(I32))
+            nc.sync.dma_start(x_plane[r:P:32, :].bitcast(I32), s_picked[8 * r : P : 32, :].bitcast(I32))
+
+        w_bf = held.tile([P, PACK, P, PACK], BF16, name="w_bf", align_bytes=64)
+        w_dst = w_bf[:].rearrange("p t m j -> p m j t")
+        w_src = w_raw[:].rearrange("p j (m t) -> p m j t", t=PACK)
+        nc.scalar.copy(w_dst[:, :CAST_SPLIT], w_src[:, :CAST_SPLIT])
+        nc.vector.tensor_copy(w_dst[:, CAST_SPLIT:], w_src[:, CAST_SPLIT:])
+
+
+        w_codes = held.tile([P, H], U32, name="w_codes", align_bytes=64)
+        w_plane = held.tile([P, H], U8, name="w_plane", align_bytes=64)
+        nc.vector.quantize_mx(out=w_codes[:].bitcast(FP8X4), scales=w_plane[:], in_=w_bf[:].rearrange("p t m j -> p (t m j)"))
+
+        for tag in ("bank11", "bank21", "bank31"):
+            idle = psum.tile([P, HALF], F32, name="idle", tag=tag)
+            nc.tensor.matmul_mx(
+                out=idle[:],
+                lhsT=w_codes[:, :P].bitcast(FP8X4),
+                lhsT_scale=w_plane[:, :P],
+                rhs=w_codes[:].bitcast(FP8X4),
+                rhs_scale=w_plane[:],
+                start=True,
+                stop=True,
+            )
+
+        neg_gain = held.tile([P, PACK], F32, name="neg_gain")
+        nc.scalar.activation(neg_gain[:], gain[:], ACT.Copy, scale=-1.0)
+        pairs = held.tile([P, PACK, 3], F32, name="pairs")
+        nc.scalar.activation(pairs[:, :, 0], gain[:], ACT.Copy)
+        nc.scalar.activation(pairs[:, :, 2], gain[:], ACT.Copy, scale=float(HALF))
+
+        banks = {}
+        for h in range(2):
+            picked = held.tile([P, HALF], U32, name=f"x_picked{h}", align_bytes=64)
+            nc.vector.tensor_copy(picked[:], x_table[:].indirect(offsets[:, 32 * h : 32 * (h + 1)]))
+            for t in (0, 1, 3, 2) if h == 0 else range(PACK):
+                bank = psum.tile([P, HALF], F32, name=f"h{t}{h}", tag=f"bank{t}{h}")
+                nc.tensor.matmul_mx(
+                    out=bank[:],
+                    lhsT=w_codes[:, P * t : P * (t + 1)].bitcast(FP8X4),
+                    lhsT_scale=w_plane[:, P * t : P * (t + 1)],
+                    rhs=picked[:].bitcast(FP8X4),
+                    rhs_scale=x_plane[:, HALF * h : HALF * (h + 1)],
+                    start=True,
+                    stop=True,
+                )
+                banks[t, h] = bank
 
         w2_codes = late.tile([P, 2 * N], U8, name="w2_codes", offset=0, align_bytes=64)
         nc.sync.dma_start(w2_codes[:].bitcast(I32), w2_words[0].bitcast(I32))
@@ -68,135 +114,70 @@ def tile_picked_inorm_none_p_kernel(tc, x_words, x_scales, w1, w2_words, w2_scal
         for r in range(4):
             nc.sync.dma_start(w2_plane[r:P:32, :].bitcast(I32), w2_scales[0, r:16:4, :].bitcast(I32))
 
-        x_picked = []
-        for h in range(2):
-            xp = late.tile([P, HALF], U32, name=f"x_picked{h}", offset=4 * N + 4 * HALF * h, align_bytes=64)
-            nc.vector.tensor_copy(xp[:], x_table[:].indirect(offsets[:, 32 * h : 32 * (h + 1)]))
-            x_picked.append(xp)
-
-        def warm_up(tag):
-            idle = psum.tile([P, HALF], F32, name="idle", tag=tag)
-            nc.tensor.matmul_mx(
-                out=idle[:],
-                lhsT=x_picked[0][:, :P].bitcast(FP8X4),
-                lhsT_scale=s_picked[:, :P],
-                rhs=x_picked[0][:].bitcast(FP8X4),
-                rhs_scale=s_picked[:, :HALF],
-                start=True,
-                stop=True,
-            )
-
-        warm_up("bank21")
-        warm_up("bank30")
-        warm_up("bank31")
-
-        w_bf = held.tile([P, PACK, P, PACK], BF16, name="w_bf", align_bytes=64)
-        w_dst = w_bf[:].rearrange("p t m j -> p m j t")
-        w_src = w_raw[:].rearrange("p j (m t) -> p m j t", t=PACK)
-        nc.vector.tensor_copy(w_dst[:, :CAST_SPLIT], w_src[:, :CAST_SPLIT])
-        nc.scalar.copy(w_dst[:, CAST_SPLIT:], w_src[:, CAST_SPLIT:])
-        w_codes, w_planes = [], []
-        for t in range(PACK):
-            wc = held.tile([P, P], U32, name=f"w_codes{t}", align_bytes=64)
-            wp = held.tile([P, P], U8, name=f"w_plane{t}", align_bytes=64)
-            nc.vector.quantize_mx(out=wc[:].bitcast(FP8X4), scales=wp[:], in_=w_bf[:, t].rearrange("p m j -> p (m j)"))
-            w_codes.append(wc)
-            w_planes.append(wp)
-
-        neg_gain = held.tile([P, PACK], F32, name="neg_gain")
-        nc.scalar.activation(neg_gain[:], gain[:], ACT.Copy, scale=-1.0)
-        pair_tile = held.tile([P, PACK, 2], F32, name="pair_tile")
-        pairs = [pair_tile[:, t] for t in range(PACK)]
-        nc.scalar.activation(pair_tile[:, 0:1, 0], gain[:, 0:1], ACT.Copy, scale=float(HALF))
-        nc.scalar.activation(pair_tile[:, 1:, 0], gain[:, 1:], ACT.Copy)
-
-        banks = {}
-        for t, h in ((0, 0), (1, 0), (0, 1), (1, 1), (2, 0), (2, 1), (3, 0), (3, 1)):
-            bank = psum.tile([P, HALF], F32, name=f"h{t}{h}", tag=f"bank{t}{h}")
-            nc.tensor.matmul_mx(
-                out=bank[:],
-                lhsT=w_codes[t][:].bitcast(FP8X4),
-                lhsT_scale=w_planes[t][:],
-                rhs=x_picked[h][:].bitcast(FP8X4),
-                rhs_scale=x_plane[:, HALF * h : HALF * (h + 1)],
-                start=True,
-                stop=True,
-            )
-            banks[t, h] = bank
-
         z_rows = [held.tile([P, 2, PACK, CHUNK], BF16, name=f"z_rows{h}", align_bytes=64) for h in range(2)]
-        affine = [held.tile([P, 2], F32, name=f"affine{t}") for t in range(PACK)]
+        affine = [held.tile([P, 3], F32, name=f"affine{t}") for t in range(PACK)]
         rstd = [held.tile([P, 1], F32, name=f"rstd{t}") for t in range(PACK)]
         moments = [held.tile([P, 2], F32, name=f"moments{t}") for t in range(PACK)]
-        stats = {t: held.tile([P, 12], F32, name=f"stats{t}") for t in range(1, PACK)}
+        kept = {th: held.tile([P, HALF], F32, name=f"kept{th[0]}", align_bytes=64) for th in KEPT}
+        squares = {th: held.tile([P, HALF], BF16, name=f"squares{th[0]}", align_bytes=64) for th in KEPT}
+
+        def keep(t, h):
+            nc.scalar.activation(kept[t, h][:], banks[t, h][:], ACT.Copy, scale=1.0 / HALF, accum_out=stats[t][:, 4:5])
+
+        def spread(t, h):
+            nc.scalar.activation(squares[t, h][:], kept[t, h][:], ACT.Square, scale=-float(HALF), bias=stats[t][:, 4:5], accum_out=stats[t][:, 5:6])
 
         def tally(t, h):
             nc.vector.bn_stats(stats[t][:, 6 * h : 6 * (h + 1)], banks[t, h][:])
 
         def aggregate(t):
-            src = tallies[:].rearrange("p h c -> p (h c)") if t == 0 else stats[t][:]
-            nc.vector.bn_aggr(moments[t][:], src)
+            nc.vector.bn_aggr(moments[t][:], stats[t][:, 3:] if (t, 0) in KEPT else stats[t][:])
 
         def factors(t):
             nc.scalar.activation(rstd[t][:], moments[t][:, 1:2], ACT.Abs_reciprocal_sqrt, bias=EPS)
-            nc.scalar.activation(pairs[t][:, 1:2], moments[t][:, 0:1], ACT.Copy, scale=neg_gain[:, t : t + 1])
+            nc.scalar.activation(pairs[:, t, 1:2], moments[t][:, 0:1], ACT.Copy, scale=neg_gain[:, t : t + 1])
 
         def finish(t):
-            nc.scalar.activation(affine[t][:], pairs[t], ACT.Copy, scale=rstd[t][:])
+            nc.scalar.activation(affine[t][:], pairs[:, t], ACT.Copy, scale=rstd[t][:])
 
-        def normalise(t, h, engine, parts=(0, 1)):
+        def normalise(t, h, engine):
             ab = affine[t]
-            src = kept[h][:] if t == 0 else banks[t, h][:]
-            ks = slice(parts[0], parts[-1] + 1)
-            part = src.rearrange("p (k n) -> p k n", k=2)[:, ks]
-            dst = z_rows[h][:, ks, t]
+            src, scale = (kept[t, h], ab[:, 2:3]) if (t, h) in KEPT else (banks[t, h], ab[:, 0:1])
+            part = src[:].rearrange("p (k n) -> p k n", k=2)
+            dst = z_rows[h][:, :, t]
             if engine is nc.scalar:
-                nc.scalar.activation(dst, part, ACT.Identity, scale=ab[:, 0:1], bias=ab[:, 1:2])
+                nc.scalar.activation(dst, part, ACT.Identity, scale=scale, bias=ab[:, 1:2])
             else:
-                engine.tensor_scalar(dst, part, ab[:, 0:1], ab[:, 1:2], ALU.mult, ALU.add)
+                engine.tensor_scalar(dst, part, scale, ab[:, 1:2], ALU.mult, ALU.add)
 
-        kept = [held.tile([P, HALF], F32, name=f"kept{h}", align_bytes=64) for h in range(2)]
-        squares = [held.tile([P, HALF], BF16, name=f"squares{h}", align_bytes=64) for h in range(2)]
-
-        def keep(h):
-            nc.scalar.activation(kept[h][:], banks[0, h][:], ACT.Copy, scale=1.0 / HALF, accum_out=tallies[:, h, 1:2])
-
-        def spread(h):
-            nc.scalar.activation(squares[h][:], kept[h][:], ACT.Square, scale=-float(HALF), bias=tallies[:, h, 1:2], accum_out=tallies[:, h, 2:3])
-
-        keep(0)
-        keep(1)
-        spread(0)
-        tally(1, 0)
-        tally(1, 1)
-        aggregate(1)
-        factors(1)
-        spread(1)
-        finish(1)
+        for th in KEPT:
+            keep(*th)
+        spread(0, 0)
+        spread(1, 0)
         tally(2, 0)
-        tally(2, 1)
+        tally(0, 1)
+        tally(1, 1)
         aggregate(0)
-        aggregate(2)
-        normalise(1, 0, nc.scalar)
+        aggregate(1)
         factors(0)
+        factors(1)
+        spread(3, 0)
+        tally(2, 1)
+        aggregate(2)
+        finish(0)
+        finish(1)
         factors(2)
-        tally(3, 0)
         tally(3, 1)
         aggregate(3)
-        normalise(1, 1, nc.scalar, (0,))
-        finish(0)
         finish(2)
         factors(3)
-        normalise(1, 1, nc.vector, (1,))
-        normalise(2, 0, nc.scalar, (0,))
+        normalise(2, 0, nc.scalar)
         finish(3)
         normalise(0, 0, nc.vector)
-        normalise(0, 1, nc.vector)
-        normalise(3, 0, nc.vector, (0,))
-        normalise(2, 0, nc.scalar, (1,))
-        normalise(3, 0, nc.vector, (1,))
-        normalise(2, 1, nc.scalar)
-        normalise(3, 1, nc.scalar)
+        normalise(1, 0, nc.vector)
+        normalise(3, 0, nc.vector)
+        for t in range(PACK):
+            normalise(t, 1, nc.scalar)
 
         widths = (128, 128, 256, 256, 128, 128)
         starts = [sum(widths[:c]) for c in range(len(widths))]
@@ -245,25 +226,23 @@ def tile_picked_inorm_none_p_kernel(tc, x_words, x_scales, w1, w2_words, w2_scal
         weave(1, nc.vector)
         quantise(0)
         quantise(1)
-        weave(3, nc.scalar)
-        for u in range(2):
-            project((0, 1), u, nc.scalar, f"bank0{u}")
-            store(0, u)
         weave(2, nc.vector)
-        weave(4, nc.vector)
+        for u in range(2):
+            project((0, 1), u, nc.scalar, f"bank{u}0")
+            store(0, u)
+        weave(3, nc.vector)
         quantise(2)
         quantise(3)
         for u in range(2):
-            project((2,), u, nc.scalar, f"bank1{u}")
+            project((2,), u, nc.scalar, f"bank{u + 2}0")
             store(1, u)
+        weave(4, nc.vector)
         weave(5, nc.vector)
         quantise(4)
         quantise(5)
-        for u, engine in enumerate((nc.scalar, nc.vector)):
-            project((3,), u, engine, f"bank2{u}")
+        for u in range(2):
+            project((3,), u, nc.scalar, f"bank{u}1")
             store(2, u)
         for u, engine in enumerate((nc.scalar, nc.vector)):
-            project((4,), u, engine, f"bank0{u}")
-        for u, engine in enumerate((nc.scalar, nc.vector)):
-            project((5,), u, engine, f"bank3{u}")
+            project((4, 5), u, engine, f"bank{u + 2}1")
             store(3, u)

@@ -158,25 +158,27 @@ def tile_picked_inorm_none_p_kernel(tc, x_words, x_scales, w1, w2_words, w2_scal
         tally(0, 1)
         tally(1, 1)
         aggregate(0)
-        aggregate(1)
         factors(0)
-        factors(1)
-        spread(3, 0)
         tally(2, 1)
+        aggregate(1)
         aggregate(2)
+        spread(3, 0)
         finish(0)
-        finish(1)
+        factors(1)
         factors(2)
         tally(3, 1)
         aggregate(3)
+        finish(1)
         finish(2)
         factors(3)
         normalise(2, 0, nc.scalar)
         finish(3)
-        normalise(0, 0, nc.vector)
+        normalise(0, 0, nc.gpsimd)
+        normalise(0, 1, nc.vector)
+        normalise(1, 1, nc.vector)
         normalise(1, 0, nc.vector)
         normalise(3, 0, nc.vector)
-        for t in range(PACK):
+        for t in range(2, PACK):
             normalise(t, 1, nc.scalar)
 
         widths = (128, 128, 256, 256, 128, 128)
@@ -226,23 +228,25 @@ def tile_picked_inorm_none_p_kernel(tc, x_words, x_scales, w1, w2_words, w2_scal
         weave(1, nc.vector)
         quantise(0)
         quantise(1)
-        weave(2, nc.vector)
+        weave(3, nc.scalar)
         for u in range(2):
             project((0, 1), u, nc.scalar, f"bank{u}0")
             store(0, u)
-        weave(3, nc.vector)
-        quantise(2)
+        weave(2, nc.vector)
         quantise(3)
+        quantise(2)
         for u in range(2):
-            project((2,), u, nc.scalar, f"bank{u + 2}0")
-            store(1, u)
+            project((3,), u, nc.scalar, f"bank{u + 2}0")
+            store(2, u)
         weave(4, nc.vector)
         weave(5, nc.vector)
         quantise(4)
         quantise(5)
-        for u in range(2):
-            project((3,), u, nc.scalar, f"bank{u}1")
-            store(2, u)
-        for u, engine in enumerate((nc.scalar, nc.vector)):
-            project((4, 5), u, engine, f"bank{u + 2}1")
+        for u, engine in enumerate((nc.scalar, nc.scalar)):
+            project((2,), u, engine, f"bank{u}1")
+            store(1, u)
+        for u, engine in enumerate((nc.vector, nc.vector)):
+            project((4,), u, engine, f"bank{u + 2}1")
+        for u, engine in enumerate((nc.vector, nc.scalar)):
+            project((5,), u, engine, f"bank{u}0")
             store(3, u)

@@ -21,7 +21,7 @@ P = 128
 PACK = 4
 HALF = 512
 CHUNK = 256
-CAST_SPLIT = 64
+X_LAST = 512
 
 
 def tile_picked_inorm_none_p_kernel(tc, x_words, x_scales, w1, w2_words, w2_scales, gamma, offs, out):
@@ -41,7 +41,11 @@ def tile_picked_inorm_none_p_kernel(tc, x_words, x_scales, w1, w2_words, w2_scal
         nc.sync.dma_start(s_table[0:P:8, :].bitcast(I32), x_scales[0].bitcast(I32))
         nc.sync.dma_start(w_raw[:, 2:], w_rows[:, 2:])
         x_table = late.tile([P, T], U32, name="x_table", offset=0, align_bytes=64)
-        nc.sync.dma_start(x_table[:].bitcast(I32), x_words[0].rearrange("p n r -> p (n r)").bitcast(I32))
+        x_rows = x_words[0].rearrange("p n r -> p (n r)").bitcast(I32)
+        nc.sync.dma_start(x_table[:, : T - X_LAST].bitcast(I32), x_rows[:, : T - X_LAST])
+        w2_codes = held.tile([P, 2 * N], U8, name="w2_codes", align_bytes=64)
+        nc.sync.dma_start(w2_codes[:].bitcast(I32), w2_words[0].bitcast(I32))
+        nc.sync.dma_start(x_table[:, T - X_LAST :].bitcast(I32), x_rows[:, T - X_LAST :])
         gain = held.tile([P, PACK], F32, name="gain", align_bytes=64)
         nc.sync.dma_start(gain[:], gamma.rearrange("(p t) o -> p (t o)", t=PACK))
 
@@ -59,24 +63,23 @@ def tile_picked_inorm_none_p_kernel(tc, x_words, x_scales, w1, w2_words, w2_scal
         s_picked = held.tile([P, S], U8, name="s_picked", align_bytes=64)
         nc.vector.tensor_copy(s_picked[:], s_table[:].indirect(offsets[:]))
         for r in range(4):
-            nc.sync.dma_start(x_plane[r:P:32, :].bitcast(I32), s_picked[8 * r : P : 32, :].bitcast(I32))
+            nc.scalar.dma_start(x_plane[r:P:32, :].bitcast(I32), s_picked[8 * r : P : 32, :].bitcast(I32))
 
         w_bf = held.tile([P, PACK, P, PACK], BF16, name="w_bf", align_bytes=64)
-        w_dst = w_bf[:].rearrange("p t m j -> p m j t")
-        w_src = w_raw[:].rearrange("p j (m t) -> p m j t", t=PACK)
-        nc.scalar.copy(w_dst[:, :CAST_SPLIT], w_src[:, :CAST_SPLIT])
-        nc.vector.tensor_copy(w_dst[:, CAST_SPLIT:], w_src[:, CAST_SPLIT:])
-
+        nc.vector.tensor_copy(
+            w_bf[:].rearrange("p (u v) m j -> p u m j v", v=2),
+            w_raw[:].rearrange("p j (m u v) -> p u m j v", u=2, v=2),
+        )
 
         w_codes = held.tile([P, H], U32, name="w_codes", align_bytes=64)
         w_plane = held.tile([P, H], U8, name="w_plane", align_bytes=64)
         nc.vector.quantize_mx(out=w_codes[:].bitcast(FP8X4), scales=w_plane[:], in_=w_bf[:].rearrange("p t m j -> p (t m j)"))
 
-        for tag in ("bank11", "bank21", "bank31"):
+        for tag in ("bank21", "bank31"):
             idle = psum.tile([P, HALF], F32, name="idle", tag=tag)
             nc.tensor.matmul_mx(
                 out=idle[:],
-                lhsT=w_codes[:, :P].bitcast(FP8X4),
+                lhsT=w2_codes[:, : 2 * P].bitcast(FP4X4),
                 lhsT_scale=w_plane[:, :P],
                 rhs=w_codes[:].bitcast(FP8X4),
                 rhs_scale=w_plane[:],
@@ -107,8 +110,6 @@ def tile_picked_inorm_none_p_kernel(tc, x_words, x_scales, w1, w2_words, w2_scal
                 )
                 banks[t, h] = bank
 
-        w2_codes = late.tile([P, 2 * N], U8, name="w2_codes", offset=0, align_bytes=64)
-        nc.sync.dma_start(w2_codes[:].bitcast(I32), w2_words[0].bitcast(I32))
         w2_plane = late.tile([P, N], U8, name="w2_plane", offset=2 * N, align_bytes=64)
         nc.vector.memset(w2_plane[:].bitcast(I32), 0)
         for r in range(4):
@@ -175,16 +176,15 @@ def tile_picked_inorm_none_p_kernel(tc, x_words, x_scales, w1, w2_words, w2_scal
         finish(3)
         normalise(0, 0, nc.gpsimd)
         normalise(0, 1, nc.vector)
-        normalise(1, 1, nc.vector)
         normalise(1, 0, nc.vector)
         normalise(3, 0, nc.vector)
-        for t in range(2, PACK):
+        for t in range(1, PACK):
             normalise(t, 1, nc.scalar)
 
-        widths = (128, 128, 256, 256, 128, 128)
+        widths = (128,) * 8
         starts = [sum(widths[:c]) for c in range(len(widths))]
         woven, codes, planes = {}, {}, {}
-        res = [[held.tile([P, CHUNK], F32, name=f"res{b}{u}", align_bytes=64) for u in range(2)] for b in range(S // CHUNK)]
+        res = [held.tile([P, 2, CHUNK], F32, name=f"res{b}", align_bytes=64) for b in range(S // CHUNK)]
 
         def weave(c, engine):
             woven[c] = held.tile([P, widths[c], PACK], BF16, name=f"woven{c}", align_bytes=64)
@@ -201,52 +201,60 @@ def tile_picked_inorm_none_p_kernel(tc, x_words, x_scales, w1, w2_words, w2_scal
             planes[c] = held.tile([P, widths[c]], U8, name=f"z_plane{c}", align_bytes=64)
             nc.vector.quantize_mx(out=codes[c][:].bitcast(FP8X4), scales=planes[c][:], in_=woven[c][:].rearrange("p n t -> p (n t)"))
 
-        def project(chunks, u, engine, tag):
+        def project(chunks, us, engine, tag):
             first = starts[chunks[0]]
             n = sum(widths[c] for c in chunks)
-            acc = psum.tile([P, n], F32, name=f"acc{chunks[0]}{u}", tag=tag)
+            acc = psum.tile([P, len(us), n], F32, name=f"acc{chunks[0]}{us[0]}", tag=tag)
             for c in chunks:
-                nc.tensor.matmul_mx(
-                    out=acc[:, starts[c] - first : starts[c] - first + widths[c]],
-                    lhsT=w2_codes[:, 2 * P * u : 2 * P * (u + 1)].bitcast(FP4X4),
-                    lhsT_scale=w2_plane[:, P * u : P * (u + 1)],
-                    rhs=codes[c][:].bitcast(FP8X4),
-                    rhs_scale=planes[c][:],
-                    start=True,
-                    stop=True,
-                )
-            dst = res[first // CHUNK][u][:, first % CHUNK : first % CHUNK + n]
+                for i, u in enumerate(us):
+                    nc.tensor.matmul_mx(
+                        out=acc[:, i, starts[c] - first : starts[c] - first + widths[c]],
+                        lhsT=w2_codes[:, 2 * P * u : 2 * P * (u + 1)].bitcast(FP4X4),
+                        lhsT_scale=w2_plane[:, P * u : P * (u + 1)],
+                        rhs=codes[c][:].bitcast(FP8X4),
+                        rhs_scale=planes[c][:],
+                        start=True,
+                        stop=True,
+                    )
+            dst = res[first // CHUNK][:, us[0] : us[-1] + 1, first % CHUNK : first % CHUNK + n]
             if engine is nc.vector:
                 nc.vector.tensor_copy(dst, acc[:])
             else:
                 nc.scalar.copy(dst, acc[:])
 
-        def store(b, u):
-            nc.sync.dma_start(out[P * u : P * (u + 1), CHUNK * b : CHUNK * (b + 1)], res[b][u][:])
+        out_rows = out.rearrange("(u p) s -> p u s", p=P)
+
+        def store(lo, hi, us):
+            rows = slice(us[0], us[-1] + 1)
+            nc.sync.dma_start(out_rows[:, rows, lo:hi], res[lo // CHUNK][:, rows, lo % CHUNK : lo % CHUNK + hi - lo])
 
         weave(0, nc.vector)
         weave(1, nc.vector)
         quantise(0)
         quantise(1)
-        weave(3, nc.scalar)
+        weave(4, nc.scalar)
         for u in range(2):
-            project((0, 1), u, nc.scalar, f"bank{u}0")
-            store(0, u)
+            project((0, 1), (u,), nc.scalar, f"bank{u}0")
+            store(0, CHUNK, (u,))
         weave(2, nc.vector)
-        quantise(3)
+        weave(3, nc.vector)
         quantise(2)
+        quantise(3)
         for u in range(2):
-            project((3,), u, nc.scalar, f"bank{u + 2}0")
-            store(2, u)
-        weave(4, nc.vector)
+            project((2, 3), (u,), nc.scalar, f"bank{u + 2}0")
+            store(CHUNK, 2 * CHUNK, (u,))
         weave(5, nc.vector)
         quantise(4)
+        weave(6, nc.vector)
         quantise(5)
-        for u, engine in enumerate((nc.scalar, nc.scalar)):
-            project((2,), u, engine, f"bank{u}1")
-            store(1, u)
-        for u, engine in enumerate((nc.vector, nc.vector)):
-            project((4,), u, engine, f"bank{u + 2}1")
-        for u, engine in enumerate((nc.vector, nc.scalar)):
-            project((5,), u, engine, f"bank{u}0")
-            store(3, u)
+        for u in range(2):
+            project((4, 5), (u,), nc.scalar, f"bank{u}1")
+            store(2 * CHUNK, 3 * CHUNK, (u,))
+        weave(7, nc.vector)
+        quantise(6)
+        quantise(7)
+        project((6,), (0, 1), nc.vector, "bank21")
+        store(6 * P, 7 * P, (0, 1))
+        for u, engine in enumerate((nc.scalar, nc.vector)):
+            project((7,), (u,), engine, f"bank{u}0")
+        store(7 * P, S, (0, 1))

@@ -21,7 +21,7 @@ P = 128
 PACK = 4
 HALF = 512
 CHUNK = 256
-X_LAST = 512
+X_LAST = 448
 
 
 def tile_picked_inorm_none_p_kernel(tc, x_words, x_scales, w1, w2_words, w2_scales, gamma, offs, out):
@@ -93,22 +93,24 @@ def tile_picked_inorm_none_p_kernel(tc, x_words, x_scales, w1, w2_words, w2_scal
         nc.scalar.activation(pairs[:, :, 0], gain[:], ACT.Copy)
         nc.scalar.activation(pairs[:, :, 2], gain[:], ACT.Copy, scale=float(HALF))
 
-        banks = {}
+        picked = []
         for h in range(2):
-            picked = held.tile([P, HALF], U32, name=f"x_picked{h}", align_bytes=64)
-            nc.vector.tensor_copy(picked[:], x_table[:].indirect(offsets[:, 32 * h : 32 * (h + 1)]))
-            for t in (0, 1, 3, 2) if h == 0 else range(PACK):
-                bank = psum.tile([P, HALF], F32, name=f"h{t}{h}", tag=f"bank{t}{h}")
-                nc.tensor.matmul_mx(
-                    out=bank[:],
-                    lhsT=w_codes[:, P * t : P * (t + 1)].bitcast(FP8X4),
-                    lhsT_scale=w_plane[:, P * t : P * (t + 1)],
-                    rhs=picked[:].bitcast(FP8X4),
-                    rhs_scale=x_plane[:, HALF * h : HALF * (h + 1)],
-                    start=True,
-                    stop=True,
-                )
-                banks[t, h] = bank
+            half = held.tile([P, HALF], U32, name=f"x_picked{h}", align_bytes=64)
+            nc.vector.tensor_copy(half[:], x_table[:].indirect(offsets[:, 32 * h : 32 * (h + 1)]))
+            picked.append(half)
+        banks = {}
+        for t, h in ((0, 0), (2, 0), (1, 0), (3, 0), (0, 1), (2, 1), (1, 1), (3, 1)):
+            bank = psum.tile([P, HALF], F32, name=f"h{t}{h}", tag=f"bank{t}{h}")
+            nc.tensor.matmul_mx(
+                out=bank[:],
+                lhsT=w_codes[:, P * t : P * (t + 1)].bitcast(FP8X4),
+                lhsT_scale=w_plane[:, P * t : P * (t + 1)],
+                rhs=picked[h][:].bitcast(FP8X4),
+                rhs_scale=x_plane[:, HALF * h : HALF * (h + 1)],
+                start=True,
+                stop=True,
+            )
+            banks[t, h] = bank
 
         w2_plane = late.tile([P, N], U8, name="w2_plane", offset=2 * N, align_bytes=64)
         nc.vector.memset(w2_plane[:].bitcast(I32), 0)

@@ -21,7 +21,6 @@ P = 128
 PACK = 4
 HALF = 512
 CHUNK = 256
-X_LAST = 448
 
 
 def tile_picked_inorm_none_p_kernel(tc, x_words, x_scales, w1, w2_words, w2_scales, gamma, offs, out):
@@ -38,14 +37,13 @@ def tile_picked_inorm_none_p_kernel(tc, x_words, x_scales, w1, w2_words, w2_scal
         nc.sync.dma_start(w_raw[:, :2], w_rows[:, :2])
         offsets = held.tile([P, S // 16], U16, name="offsets")
         nc.sync.dma_start(offsets[:], offs)
-        nc.sync.dma_start(s_table[0:P:8, :].bitcast(I32), x_scales[0].bitcast(I32))
+        nc.sync.dma_start(s_table[32:96:4, :].bitcast(I32), x_scales[0].bitcast(I32))
         nc.sync.dma_start(w_raw[:, 2:], w_rows[:, 2:])
         x_table = late.tile([P, T], U32, name="x_table", offset=0, align_bytes=64)
         x_rows = x_words[0].rearrange("p n r -> p (n r)").bitcast(I32)
-        nc.sync.dma_start(x_table[:, : T - X_LAST].bitcast(I32), x_rows[:, : T - X_LAST])
+        nc.sync.dma_start(x_table[:].bitcast(I32), x_rows)
         w2_codes = held.tile([P, 2 * N], U8, name="w2_codes", align_bytes=64)
         nc.sync.dma_start(w2_codes[:].bitcast(I32), w2_words[0].bitcast(I32))
-        nc.sync.dma_start(x_table[:, T - X_LAST :].bitcast(I32), x_rows[:, T - X_LAST :])
         gain = held.tile([P, PACK], F32, name="gain", align_bytes=64)
         nc.sync.dma_start(gain[:], gamma.rearrange("(p t) o -> p (t o)", t=PACK))
 
@@ -55,15 +53,16 @@ def tile_picked_inorm_none_p_kernel(tc, x_words, x_scales, w1, w2_words, w2_scal
         nc.vector.memset(warm_in[:], 1.0)
         warm_out = held.tile([P, 1], F32, name="warm_out")
         nc.scalar.activation(warm_out[:], warm_in[:], ACT.Abs_reciprocal_sqrt)
-        KEPT = ((0, 0), (1, 0), (3, 0))
-        stats = [held.tile([P, 12], F32, name=f"stats{t}") for t in range(PACK)]
-        for t, h in KEPT:
-            nc.vector.memset(stats[t][:, 3:4], float(HALF))
+        stats = [held.tile([P, 12 if t < 2 else 15], F32, name=f"stats{t}")[:] for t in range(PACK)]
+        slot = {(0, 0): 0, (0, 1): 3, (0, 2): 6, (1, 0): 0, (1, 1): 3, (1, 2): 6, (2, 2): 0, (2, 1): 6, (2, 0): 12, (3, 2): 0, (3, 1): 6, (3, 0): 12}
+        KEPT = ((0, 0), (1, 0), (0, 1), (1, 1), (2, 0), (3, 0))
+        for t, q in KEPT:
+            nc.vector.memset(stats[t][:, slot[t, q] : slot[t, q] + 1], float(CHUNK))
 
         s_picked = held.tile([P, S], U8, name="s_picked", align_bytes=64)
         nc.vector.tensor_copy(s_picked[:], s_table[:].indirect(offsets[:]))
         for r in range(4):
-            nc.scalar.dma_start(x_plane[r:P:32, :].bitcast(I32), s_picked[8 * r : P : 32, :].bitcast(I32))
+            nc.scalar.dma_start(x_plane[r:P:32, :].bitcast(I32), s_picked[32 + 4 * r : 96 : 16, :].bitcast(I32))
 
         w_bf = held.tile([P, PACK, P, PACK], BF16, name="w_bf", align_bytes=64)
         nc.vector.tensor_copy(
@@ -75,113 +74,149 @@ def tile_picked_inorm_none_p_kernel(tc, x_words, x_scales, w1, w2_words, w2_scal
         w_plane = held.tile([P, H], U8, name="w_plane", align_bytes=64)
         nc.vector.quantize_mx(out=w_codes[:].bitcast(FP8X4), scales=w_plane[:], in_=w_bf[:].rearrange("p t m j -> p (t m j)"))
 
-        for tag in ("bank21", "bank31"):
-            idle = psum.tile([P, HALF], F32, name="idle", tag=tag)
-            nc.tensor.matmul_mx(
-                out=idle[:],
-                lhsT=w2_codes[:, : 2 * P].bitcast(FP4X4),
-                lhsT_scale=w_plane[:, :P],
-                rhs=w_codes[:].bitcast(FP8X4),
-                rhs_scale=w_plane[:],
-                start=True,
-                stop=True,
-            )
-
         neg_gain = held.tile([P, PACK], F32, name="neg_gain")
         nc.scalar.activation(neg_gain[:], gain[:], ACT.Copy, scale=-1.0)
-        pairs = held.tile([P, PACK, 3], F32, name="pairs")
-        nc.scalar.activation(pairs[:, :, 0], gain[:], ACT.Copy)
-        nc.scalar.activation(pairs[:, :, 2], gain[:], ACT.Copy, scale=float(HALF))
+        triples = [held.tile([P, 2, 3], F32, name=f"triples{i}") for i in range(2)]
+        for i in range(2):
+            nc.scalar.activation(triples[i][:, :, 0], gain[:, 2 * i : 2 * i + 2], ACT.Copy)
+            nc.scalar.activation(triples[i][:, :, 2], gain[:, 2 * i : 2 * i + 2], ACT.Copy, scale=float(CHUNK))
 
+        pieces = ((0, CHUNK), (CHUNK, CHUNK), (HALF, HALF))
         picked = []
-        for h in range(2):
-            half = held.tile([P, HALF], U32, name=f"x_picked{h}", align_bytes=64)
-            nc.vector.tensor_copy(half[:], x_table[:].indirect(offsets[:, 32 * h : 32 * (h + 1)]))
-            picked.append(half)
-        banks = {}
-        for t, h in ((0, 0), (2, 0), (1, 0), (3, 0), (0, 1), (2, 1), (1, 1), (3, 1)):
-            bank = psum.tile([P, HALF], F32, name=f"h{t}{h}", tag=f"bank{t}{h}")
-            nc.tensor.matmul_mx(
-                out=bank[:],
-                lhsT=w_codes[:, P * t : P * (t + 1)].bitcast(FP8X4),
-                lhsT_scale=w_plane[:, P * t : P * (t + 1)],
-                rhs=picked[h][:].bitcast(FP8X4),
-                rhs_scale=x_plane[:, HALF * h : HALF * (h + 1)],
-                start=True,
-                stop=True,
-            )
-            banks[t, h] = bank
+        for i, (lo, n) in enumerate(pieces):
+            piece = held.tile([P, n], U32, name=f"x_picked{i}", align_bytes=64)
+            nc.vector.tensor_copy(piece[:], x_table[:].indirect(offsets[:, lo // 16 : (lo + n) // 16]))
+            picked.append(piece)
+        sums = {}
+        groups = (((0, 1), 0), ((0, 1), 1), ((2, 3), 1), ((0,), 2), ((1,), 2), ((2, 3), 0), ((2,), 2), ((3,), 2))
+        for b, (ts, i) in enumerate(groups):
+            bank = psum.tile([P, HALF], F32, name=f"h{b}", tag=f"bank{b}")
+            lo, n = pieces[i]
+            for a, t in enumerate(ts):
+                sums[t, i] = bank[:, n * a : n * (a + 1)]
+                nc.tensor.matmul_mx(
+                    out=sums[t, i],
+                    lhsT=w_codes[:, P * t : P * (t + 1)].bitcast(FP8X4),
+                    lhsT_scale=w_plane[:, P * t : P * (t + 1)],
+                    rhs=picked[i][:].bitcast(FP8X4),
+                    rhs_scale=x_plane[:, lo : lo + n],
+                    start=True,
+                    stop=True,
+                )
 
         w2_plane = late.tile([P, N], U8, name="w2_plane", offset=2 * N, align_bytes=64)
         nc.vector.memset(w2_plane[:].bitcast(I32), 0)
         for r in range(4):
             nc.sync.dma_start(w2_plane[r:P:32, :].bitcast(I32), w2_scales[0, r:16:4, :].bitcast(I32))
 
-        z_rows = [held.tile([P, 2, PACK, CHUNK], BF16, name=f"z_rows{h}", align_bytes=64) for h in range(2)]
         affine = [held.tile([P, 3], F32, name=f"affine{t}") for t in range(PACK)]
-        rstd = [held.tile([P, 1], F32, name=f"rstd{t}") for t in range(PACK)]
-        moments = [held.tile([P, 2], F32, name=f"moments{t}") for t in range(PACK)]
-        kept = {th: held.tile([P, HALF], F32, name=f"kept{th[0]}", align_bytes=64) for th in KEPT}
-        squares = {th: held.tile([P, HALF], BF16, name=f"squares{th[0]}", align_bytes=64) for th in KEPT}
+        rstd = [held.tile([P, 1], F32, name=f"rstd{t}")[:] for t in range(2)]
+        last_roots = held.tile([P, 2], F32, name="last_roots")
+        rstd.extend(last_roots[:, i : i + 1] for i in range(2))
+        moments = [held.tile([P, 2], F32, name=f"moments{t}")[:] for t in range(2)]
+        last_moments = held.tile([P, 2, 2], F32, name="last_moments")
+        moments.extend(last_moments[:, i] for i in range(2))
+        z_first = held.tile([P, 2, PACK, CHUNK], BF16, name="z_first", align_bytes=64)
+        z_last = [held.tile([P, 1, PACK, CHUNK], BF16, name=f"z_last{i}", align_bytes=64) for i in range(2)]
+        wide_gain = held.tile([P, PACK], F32, name="wide_gain")
+        nc.scalar.activation(wide_gain[:], gain[:], ACT.Copy, scale=float(CHUNK))
+        gained = {t: held.tile([P, CHUNK], F32, name=f"gained{t}", align_bytes=64) for t in (2, 3)}
+        kept = [held.tile([P, HALF if t < 2 else CHUNK], F32, name=f"kept{t}", align_bytes=64) for t in range(PACK)]
+        squares = [held.tile([P, CHUNK], BF16, name=f"squares{i}", align_bytes=64) for i in range(2)]
 
-        def keep(t, h):
-            nc.scalar.activation(kept[t, h][:], banks[t, h][:], ACT.Copy, scale=1.0 / HALF, accum_out=stats[t][:, 4:5])
+        def keep(t, q):
+            at = slot[t, q]
+            nc.scalar.activation(kept[t][:, CHUNK * q : CHUNK * (q + 1)], sums[t, q], ACT.Copy, scale=1.0 / CHUNK, accum_out=stats[t][:, at + 1 : at + 2])
 
-        def spread(t, h):
-            nc.scalar.activation(squares[t, h][:], kept[t, h][:], ACT.Square, scale=-float(HALF), bias=stats[t][:, 4:5], accum_out=stats[t][:, 5:6])
+        def spread(t, q):
+            at = slot[t, q]
+            nc.scalar.activation(
+                squares[t % 2][:], kept[t][:, CHUNK * q : CHUNK * (q + 1)], ACT.Square, scale=-float(CHUNK), bias=stats[t][:, at + 1 : at + 2], accum_out=stats[t][:, at + 2 : at + 3]
+            )
 
-        def tally(t, h):
-            nc.vector.bn_stats(stats[t][:, 6 * h : 6 * (h + 1)], banks[t, h][:])
+        def tally(t, i):
+            nc.vector.bn_stats(stats[t][:, slot[t, i] : slot[t, i] + 6], sums[t, i])
 
         def aggregate(t):
-            nc.vector.bn_aggr(moments[t][:], stats[t][:, 3:] if (t, 0) in KEPT else stats[t][:])
+            nc.vector.bn_aggr(moments[t], stats[t])
 
-        def factors(t):
-            nc.scalar.activation(rstd[t][:], moments[t][:, 1:2], ACT.Abs_reciprocal_sqrt, bias=EPS)
-            nc.scalar.activation(pairs[:, t, 1:2], moments[t][:, 0:1], ACT.Copy, scale=neg_gain[:, t : t + 1])
+        def root(dst, variance):
+            nc.scalar.activation(dst, variance, ACT.Abs_reciprocal_sqrt, bias=EPS)
+
+        def shift(t, engine):
+            dst = triples[t // 2][:, t % 2, 1:2]
+            if engine is nc.scalar:
+                nc.scalar.activation(dst, moments[t][:, 0:1], ACT.Copy, scale=neg_gain[:, t : t + 1])
+            else:
+                nc.vector.tensor_scalar(dst, moments[t][:, 0:1], neg_gain[:, t : t + 1], 0.0, ALU.mult, ALU.add)
 
         def finish(t):
-            nc.scalar.activation(affine[t][:], pairs[:, t], ACT.Copy, scale=rstd[t][:])
+            nc.scalar.activation(affine[t][:], triples[t // 2][:, t % 2], ACT.Copy, scale=rstd[t])
 
-        def normalise(t, h, engine):
+        def amplify(t):
+            nc.gpsimd.tensor_scalar(gained[t][:], kept[t][:], wide_gain[:, t : t + 1], 0.0, ALU.mult, ALU.add)
+
+        def centre(t):
+            nc.vector.tensor_scalar(z_first[:, 0, t], gained[t][:], triples[1][:, t % 2, 1:2], rstd[t], ALU.add, ALU.mult)
+
+        def normalise(t, q, n, engine):
             ab = affine[t]
-            src, scale = (kept[t, h], ab[:, 2:3]) if (t, h) in KEPT else (banks[t, h], ab[:, 0:1])
-            part = src[:].rearrange("p (k n) -> p k n", k=2)
-            dst = z_rows[h][:, :, t]
+            if (t, q) in KEPT:
+                src, scale = kept[t][:, CHUNK * q : CHUNK * (q + n)], ab[:, 2:3]
+            elif q == 1:
+                src, scale = sums[t, 1], ab[:, 0:1]
+            else:
+                src, scale = sums[t, 2][:, CHUNK * (q - 2) : CHUNK * (q - 2 + n)], ab[:, 0:1]
+            part = src.rearrange("p (k n) -> p k n", k=n)
+            dst = z_first[:, q : q + n, t] if q < 2 else z_last[q - 2][:, :, t]
             if engine is nc.scalar:
                 nc.scalar.activation(dst, part, ACT.Identity, scale=scale, bias=ab[:, 1:2])
             else:
                 engine.tensor_scalar(dst, part, scale, ab[:, 1:2], ALU.mult, ALU.add)
 
-        for th in KEPT:
-            keep(*th)
-        spread(0, 0)
-        spread(1, 0)
-        tally(2, 0)
-        tally(0, 1)
-        tally(1, 1)
-        aggregate(0)
-        factors(0)
+        for q in range(2):
+            keep(0, q)
+            keep(1, q)
+            spread(0, q)
+            spread(1, q)
         tally(2, 1)
-        aggregate(1)
-        aggregate(2)
-        spread(3, 0)
-        finish(0)
-        factors(1)
-        factors(2)
         tally(3, 1)
-        aggregate(3)
+        tally(0, 2)
+        tally(1, 2)
+        aggregate(0)
+        tally(2, 2)
+        aggregate(1)
+        tally(3, 2)
+        shift(1, nc.vector)
+        keep(2, 0)
+        keep(3, 0)
+        root(rstd[0], moments[0][:, 1:2])
+        shift(0, nc.scalar)
+        spread(2, 0)
+        finish(0)
+        root(rstd[1], moments[1][:, 1:2])
+        spread(3, 0)
         finish(1)
+        amplify(2)
+        amplify(3)
+        normalise(0, 0, 1, nc.gpsimd)
+        normalise(1, 0, 1, nc.gpsimd)
+        normalise(0, 1, 1, nc.gpsimd)
+        aggregate(2)
+        aggregate(3)
+        shift(2, nc.vector)
+        shift(3, nc.vector)
+        root(last_roots[:], last_moments[:, :, 1])
         finish(2)
-        factors(3)
-        normalise(2, 0, nc.scalar)
         finish(3)
-        normalise(0, 0, nc.gpsimd)
-        normalise(0, 1, nc.vector)
-        normalise(1, 0, nc.vector)
-        normalise(3, 0, nc.vector)
-        for t in range(1, PACK):
-            normalise(t, 1, nc.scalar)
+        centre(2)
+        centre(3)
+        normalise(1, 1, 1, nc.vector)
+        normalise(2, 1, 1, nc.scalar)
+        normalise(3, 1, 1, nc.scalar)
+        for q in (2, 3):
+            for t in range(PACK):
+                normalise(t, q, 1, nc.scalar)
 
         widths = (128,) * 8
         starts = [sum(widths[:c]) for c in range(len(widths))]
@@ -191,8 +226,9 @@ def tile_picked_inorm_none_p_kernel(tc, x_words, x_scales, w1, w2_words, w2_scal
         def weave(c, engine):
             woven[c] = held.tile([P, widths[c], PACK], BF16, name=f"woven{c}", align_bytes=64)
             dst = woven[c][:].rearrange("p (c i) t -> p c t i", i=4)
-            h, k, lo = starts[c] // HALF, starts[c] % HALF // CHUNK, starts[c] % CHUNK
-            src = z_rows[h][:, k, :, lo : lo + widths[c]].rearrange("p t (c i) -> p c t i", i=4)
+            q, lo = divmod(starts[c], CHUNK)
+            rows = z_first[:, q] if q < 2 else z_last[q - 2][:, 0]
+            src = rows[:, :, lo : lo + widths[c]].rearrange("p t (c i) -> p c t i", i=4)
             if engine is nc.vector:
                 nc.vector.tensor_copy(dst, src)
             else:
@@ -230,33 +266,21 @@ def tile_picked_inorm_none_p_kernel(tc, x_words, x_scales, w1, w2_words, w2_scal
             rows = slice(us[0], us[-1] + 1)
             nc.sync.dma_start(out_rows[:, rows, lo:hi], res[lo // CHUNK][:, rows, lo % CHUNK : lo % CHUNK + hi - lo])
 
-        weave(0, nc.vector)
-        weave(1, nc.vector)
-        quantise(0)
-        quantise(1)
-        weave(4, nc.scalar)
-        for u in range(2):
-            project((0, 1), (u,), nc.scalar, f"bank{u}0")
-            store(0, CHUNK, (u,))
-        weave(2, nc.vector)
-        weave(3, nc.vector)
-        quantise(2)
-        quantise(3)
-        for u in range(2):
-            project((2, 3), (u,), nc.scalar, f"bank{u + 2}0")
-            store(CHUNK, 2 * CHUNK, (u,))
-        weave(5, nc.vector)
-        quantise(4)
+        banks = ((0, 1), (5, 2), (0, 1))
+        for b in range(3):
+            weave(2 * b, nc.vector)
+            weave(2 * b + 1, nc.vector)
+            quantise(2 * b)
+            quantise(2 * b + 1)
+            for u in range(2):
+                project((2 * b, 2 * b + 1), (u,), nc.scalar, f"bank{banks[b][u]}")
+                store(CHUNK * b, CHUNK * (b + 1), (u,))
         weave(6, nc.vector)
-        quantise(5)
-        for u in range(2):
-            project((4, 5), (u,), nc.scalar, f"bank{u}1")
-            store(2 * CHUNK, 3 * CHUNK, (u,))
         weave(7, nc.vector)
         quantise(6)
         quantise(7)
-        project((6,), (0, 1), nc.vector, "bank21")
+        project((6,), (0, 1), nc.scalar, "bank5")
         store(6 * P, 7 * P, (0, 1))
         for u, engine in enumerate((nc.scalar, nc.vector)):
-            project((7,), (u,), engine, f"bank{u}0")
+            project((7,), (u,), engine, f"bank{u + 3}")
         store(7 * P, S, (0, 1))

@@ -27,7 +27,7 @@ def tile_picked_inorm_none_p_kernel(tc, x_words, x_scales, w1, w2_words, w2_scal
     nc = tc.nc
     with ExitStack() as ctx:
         held = ctx.enter_context(tc.tile_pool(name="held", bufs=1))
-        late = ctx.enter_context(tc.tile_pool(name="late", bufs=1))
+        early = ctx.enter_context(tc.tile_pool(name="early", bufs=1))
         psum = ctx.enter_context(tc.psum_pool(name="psum", bufs=1))
 
         s_table = held.tile([P, T], U8, name="s_table", align_bytes=64)
@@ -39,7 +39,7 @@ def tile_picked_inorm_none_p_kernel(tc, x_words, x_scales, w1, w2_words, w2_scal
         nc.sync.dma_start(offsets[:], offs)
         nc.sync.dma_start(s_table[32:96:4, :].bitcast(I32), x_scales[0].bitcast(I32))
         nc.sync.dma_start(w_raw[:, 2:], w_rows[:, 2:])
-        x_table = late.tile([P, T], U32, name="x_table", offset=0, align_bytes=64)
+        x_table = early.tile([P, T], U32, name="x_table", offset=0, align_bytes=64)
         x_rows = x_words[0].rearrange("p n r -> p (n r)").bitcast(I32)
         nc.sync.dma_start(x_table[:].bitcast(I32), x_rows)
         w2_codes = held.tile([P, 2 * N], U8, name="w2_codes", align_bytes=64)
@@ -53,9 +53,9 @@ def tile_picked_inorm_none_p_kernel(tc, x_words, x_scales, w1, w2_words, w2_scal
         nc.vector.memset(warm_in[:], 1.0)
         warm_out = held.tile([P, 1], F32, name="warm_out")
         nc.scalar.activation(warm_out[:], warm_in[:], ACT.Abs_reciprocal_sqrt)
-        stats = [held.tile([P, 12 if t < 2 else 15], F32, name=f"stats{t}")[:] for t in range(PACK)]
-        slot = {(0, 0): 0, (0, 1): 3, (0, 2): 6, (1, 0): 0, (1, 1): 3, (1, 2): 6, (2, 2): 0, (2, 1): 6, (2, 0): 12, (3, 2): 0, (3, 1): 6, (3, 0): 12}
-        KEPT = ((0, 0), (1, 0), (0, 1), (1, 1), (2, 0), (3, 0))
+        KEPT = ((0, 0), (1, 0), (0, 1), (2, 0), (3, 0), (3, 3))
+        slot = {(0, 0): 0, (0, 1): 3, (0, 2): 6, (1, 0): 0, (1, 1): 3, (1, 2): 9, (2, 0): 0, (2, 1): 3, (2, 2): 9, (3, 0): 0, (3, 3): 3, (3, 1): 6, (3, 2): 12}
+        stats = [held.tile([P, n], F32, name=f"stats{t}")[:] for t, n in enumerate((12, 15, 15, 18))]
         for t, q in KEPT:
             nc.vector.memset(stats[t][:, slot[t, q] : slot[t, q] + 1], float(CHUNK))
 
@@ -87,27 +87,29 @@ def tile_picked_inorm_none_p_kernel(tc, x_words, x_scales, w1, w2_words, w2_scal
             piece = held.tile([P, n], U32, name=f"x_picked{i}", align_bytes=64)
             nc.vector.tensor_copy(piece[:], x_table[:].indirect(offsets[:, lo // 16 : (lo + n) // 16]))
             picked.append(piece)
-        sums = {}
-        groups = (((0, 1), 0), ((0, 1), 1), ((2, 3), 1), ((0,), 2), ((1,), 2), ((2, 3), 0), ((2,), 2), ((3,), 2))
-        for b, (ts, i) in enumerate(groups):
-            bank = psum.tile([P, HALF], F32, name=f"h{b}", tag=f"bank{b}")
-            lo, n = pieces[i]
-            for a, t in enumerate(ts):
-                sums[t, i] = bank[:, n * a : n * (a + 1)]
-                nc.tensor.matmul_mx(
-                    out=sums[t, i],
-                    lhsT=w_codes[:, P * t : P * (t + 1)].bitcast(FP8X4),
-                    lhsT_scale=w_plane[:, P * t : P * (t + 1)],
-                    rhs=picked[i][:].bitcast(FP8X4),
-                    rhs_scale=x_plane[:, lo : lo + n],
-                    start=True,
-                    stop=True,
-                )
-
-        w2_plane = late.tile([P, N], U8, name="w2_plane", offset=2 * N, align_bytes=64)
+        w2_plane = early.tile([P, N], U8, name="w2_plane", offset=0, align_bytes=64)
         nc.vector.memset(w2_plane[:].bitcast(I32), 0)
         for r in range(4):
             nc.sync.dma_start(w2_plane[r:P:32, :].bitcast(I32), w2_scales[0, r:16:4, :].bitcast(I32))
+
+        banks = {}
+        sums = {}
+
+        def multiply(t, i, b, side):
+            lo, n = pieces[i]
+            if side == 0:
+                banks[b] = psum.tile([P, HALF], F32, name=f"h{t}{i}", tag=f"bank{b}")
+            for k in range(n // CHUNK):
+                sums[t, i + k] = banks[b][:, CHUNK * (side + k) : CHUNK * (side + k + 1)]
+            nc.tensor.matmul_mx(
+                out=banks[b][:, CHUNK * side : CHUNK * side + n],
+                lhsT=w_codes[:, P * t : P * (t + 1)].bitcast(FP8X4),
+                lhsT_scale=w_plane[:, P * t : P * (t + 1)],
+                rhs=picked[i][:].bitcast(FP8X4),
+                rhs_scale=x_plane[:, lo : lo + n],
+                start=True,
+                stop=True,
+            )
 
         affine = [held.tile([P, 3], F32, name=f"affine{t}") for t in range(PACK)]
         rstd = [held.tile([P, 1], F32, name=f"rstd{t}")[:] for t in range(2)]
@@ -121,21 +123,21 @@ def tile_picked_inorm_none_p_kernel(tc, x_words, x_scales, w1, w2_words, w2_scal
         wide_gain = held.tile([P, PACK], F32, name="wide_gain")
         nc.scalar.activation(wide_gain[:], gain[:], ACT.Copy, scale=float(CHUNK))
         gained = {t: held.tile([P, CHUNK], F32, name=f"gained{t}", align_bytes=64) for t in (2, 3)}
-        kept = [held.tile([P, HALF if t < 2 else CHUNK], F32, name=f"kept{t}", align_bytes=64) for t in range(PACK)]
+        kept = {(t, q): held.tile([P, CHUNK], F32, name=f"kept{t}{q}", align_bytes=64) for t, q in KEPT}
         squares = [held.tile([P, CHUNK], BF16, name=f"squares{i}", align_bytes=64) for i in range(2)]
 
         def keep(t, q):
             at = slot[t, q]
-            nc.scalar.activation(kept[t][:, CHUNK * q : CHUNK * (q + 1)], sums[t, q], ACT.Copy, scale=1.0 / CHUNK, accum_out=stats[t][:, at + 1 : at + 2])
+            nc.scalar.activation(kept[t, q][:], sums[t, q], ACT.Copy, scale=1.0 / CHUNK, accum_out=stats[t][:, at + 1 : at + 2])
 
         def spread(t, q):
             at = slot[t, q]
             nc.scalar.activation(
-                squares[t % 2][:], kept[t][:, CHUNK * q : CHUNK * (q + 1)], ACT.Square, scale=-float(CHUNK), bias=stats[t][:, at + 1 : at + 2], accum_out=stats[t][:, at + 2 : at + 3]
+                squares[KEPT.index((t, q)) % 2][:], kept[t, q][:], ACT.Square, scale=-float(CHUNK), bias=stats[t][:, at + 1 : at + 2], accum_out=stats[t][:, at + 2 : at + 3]
             )
 
-        def tally(t, i):
-            nc.vector.bn_stats(stats[t][:, slot[t, i] : slot[t, i] + 6], sums[t, i])
+        def tally(t, q, src):
+            nc.vector.bn_stats(stats[t][:, slot[t, q] : slot[t, q] + 6], src)
 
         def aggregate(t):
             nc.vector.bn_aggr(moments[t], stats[t])
@@ -154,54 +156,64 @@ def tile_picked_inorm_none_p_kernel(tc, x_words, x_scales, w1, w2_words, w2_scal
             nc.scalar.activation(affine[t][:], triples[t // 2][:, t % 2], ACT.Copy, scale=rstd[t])
 
         def amplify(t):
-            nc.gpsimd.tensor_scalar(gained[t][:], kept[t][:], wide_gain[:, t : t + 1], 0.0, ALU.mult, ALU.add)
+            nc.gpsimd.tensor_scalar(gained[t][:], kept[t, 0][:], wide_gain[:, t : t + 1], 0.0, ALU.mult, ALU.add)
 
         def centre(t):
             nc.vector.tensor_scalar(z_first[:, 0, t], gained[t][:], triples[1][:, t % 2, 1:2], rstd[t], ALU.add, ALU.mult)
 
-        def normalise(t, q, n, engine):
+        def normalise(t, q, engine):
             ab = affine[t]
-            if (t, q) in KEPT:
-                src, scale = kept[t][:, CHUNK * q : CHUNK * (q + n)], ab[:, 2:3]
-            elif q == 1:
-                src, scale = sums[t, 1], ab[:, 0:1]
-            else:
-                src, scale = sums[t, 2][:, CHUNK * (q - 2) : CHUNK * (q - 2 + n)], ab[:, 0:1]
-            part = src.rearrange("p (k n) -> p k n", k=n)
-            dst = z_first[:, q : q + n, t] if q < 2 else z_last[q - 2][:, :, t]
+            src, scale = (kept[t, q][:], ab[:, 2:3]) if (t, q) in KEPT else (sums[t, q], ab[:, 0:1])
+            dst = z_first[:, q, t] if q < 2 else z_last[q - 2][:, 0, t]
             if engine is nc.scalar:
-                nc.scalar.activation(dst, part, ACT.Identity, scale=scale, bias=ab[:, 1:2])
+                nc.scalar.activation(dst, src, ACT.Identity, scale=scale, bias=ab[:, 1:2])
             else:
-                engine.tensor_scalar(dst, part, scale, ab[:, 1:2], ALU.mult, ALU.add)
+                engine.tensor_scalar(dst, src, scale, ab[:, 1:2], ALU.mult, ALU.add)
 
-        for q in range(2):
-            keep(0, q)
-            keep(1, q)
-            spread(0, q)
-            spread(1, q)
-        tally(2, 1)
-        tally(3, 1)
-        tally(0, 2)
-        tally(1, 2)
-        aggregate(0)
-        tally(2, 2)
-        aggregate(1)
-        tally(3, 2)
-        shift(1, nc.vector)
+        multiply(0, 0, 0, 0)
+        multiply(1, 0, 1, 0)
+        multiply(1, 1, 2, 0)
+        multiply(0, 1, 3, 0)
+        multiply(2, 1, 4, 0)
+        multiply(3, 1, 4, 1)
+        keep(0, 0)
+        keep(1, 0)
+        spread(0, 0)
+        keep(0, 1)
+        spread(1, 0)
+        spread(0, 1)
+        tally(1, 1, sums[1, 1])
+        tally(2, 1, sums[2, 1])
+        tally(3, 1, sums[3, 1])
+        multiply(0, 2, 0, 0)
+        multiply(2, 0, 5, 0)
+        multiply(3, 0, 2, 1)
+        multiply(1, 2, 1, 0)
+        multiply(3, 2, 7, 0)
+        multiply(2, 2, 6, 0)
         keep(2, 0)
         keep(3, 0)
+        spread(2, 0)
+        keep(3, 3)
+        tally(0, 2, banks[0][:])
+        tally(1, 2, banks[1][:])
+        aggregate(0)
+        tally(2, 2, banks[6][:])
+        aggregate(1)
+        tally(3, 2, sums[3, 2])
+        shift(1, nc.vector)
+        spread(3, 0)
         root(rstd[0], moments[0][:, 1:2])
         shift(0, nc.scalar)
-        spread(2, 0)
+        spread(3, 3)
         finish(0)
         root(rstd[1], moments[1][:, 1:2])
-        spread(3, 0)
         finish(1)
         amplify(2)
         amplify(3)
-        normalise(0, 0, 1, nc.gpsimd)
-        normalise(1, 0, 1, nc.gpsimd)
-        normalise(0, 1, 1, nc.gpsimd)
+        normalise(0, 0, nc.gpsimd)
+        normalise(1, 0, nc.gpsimd)
+        normalise(0, 1, nc.gpsimd)
         aggregate(2)
         aggregate(3)
         shift(2, nc.vector)
@@ -211,12 +223,7 @@ def tile_picked_inorm_none_p_kernel(tc, x_words, x_scales, w1, w2_words, w2_scal
         finish(3)
         centre(2)
         centre(3)
-        normalise(1, 1, 1, nc.vector)
-        normalise(2, 1, 1, nc.scalar)
-        normalise(3, 1, 1, nc.scalar)
-        for q in (2, 3):
-            for t in range(PACK):
-                normalise(t, q, 1, nc.scalar)
+        normalise(3, 3, nc.vector)
 
         widths = (128,) * 8
         starts = [sum(widths[:c]) for c in range(len(widths))]
@@ -266,21 +273,30 @@ def tile_picked_inorm_none_p_kernel(tc, x_words, x_scales, w1, w2_words, w2_scal
             rows = slice(us[0], us[-1] + 1)
             nc.sync.dma_start(out_rows[:, rows, lo:hi], res[lo // CHUNK][:, rows, lo % CHUNK : lo % CHUNK + hi - lo])
 
-        banks = ((0, 1), (5, 2), (0, 1))
+        free = ((3, 5), (2, 4), (3, 5))
+        for t in range(1, PACK):
+            normalise(t, 1, nc.scalar)
         for b in range(3):
             weave(2 * b, nc.vector)
             weave(2 * b + 1, nc.vector)
             quantise(2 * b)
             quantise(2 * b + 1)
             for u in range(2):
-                project((2 * b, 2 * b + 1), (u,), nc.scalar, f"bank{banks[b][u]}")
-                store(CHUNK * b, CHUNK * (b + 1), (u,))
+                if b == 0:
+                    project((u,), (0, 1), nc.scalar, f"bank{free[b][u]}")
+                    store(P * u, P * (u + 1), (0, 1))
+                else:
+                    project((2 * b, 2 * b + 1), (u,), nc.scalar, f"bank{free[b][u]}")
+                    store(CHUNK * b, CHUNK * (b + 1), (u,))
+            for t in range(PACK):
+                if b < 2 and (t, b + 2) not in KEPT:
+                    normalise(t, b + 2, nc.scalar)
         weave(6, nc.vector)
         weave(7, nc.vector)
         quantise(6)
         quantise(7)
-        project((6,), (0, 1), nc.scalar, "bank5")
+        project((6,), (0, 1), nc.scalar, "bank7")
         store(6 * P, 7 * P, (0, 1))
         for u, engine in enumerate((nc.scalar, nc.vector)):
-            project((7,), (u,), engine, f"bank{u + 3}")
+            project((7,), (u,), engine, f"bank{(2, 4)[u]}")
         store(7 * P, S, (0, 1))

@@ -213,7 +213,6 @@ def tile_picked_inorm_none_p_kernel(tc, x_words, x_scales, w1, w2_words, w2_scal
         amplify(3)
         normalise(0, 0, nc.gpsimd)
         normalise(1, 0, nc.gpsimd)
-        normalise(0, 1, nc.gpsimd)
         aggregate(2)
         aggregate(3)
         shift(2, nc.vector)
@@ -223,7 +222,7 @@ def tile_picked_inorm_none_p_kernel(tc, x_words, x_scales, w1, w2_words, w2_scal
         finish(3)
         centre(2)
         centre(3)
-        normalise(3, 3, nc.vector)
+        normalise(0, 1, nc.vector)
 
         widths = (128,) * 8
         starts = [sum(widths[:c]) for c in range(len(widths))]
@@ -289,7 +288,7 @@ def tile_picked_inorm_none_p_kernel(tc, x_words, x_scales, w1, w2_words, w2_scal
                     project((2 * b, 2 * b + 1), (u,), nc.scalar, f"bank{free[b][u]}")
                     store(CHUNK * b, CHUNK * (b + 1), (u,))
             for t in range(PACK):
-                if b < 2 and (t, b + 2) not in KEPT:
+                if b < 2:
                     normalise(t, b + 2, nc.scalar)
         weave(6, nc.vector)
         weave(7, nc.vector)

@@ -28,9 +28,10 @@ def tile_picked_inorm_none_p_kernel(tc, x_words, x_scales, w1, w2_words, w2_scal
     with ExitStack() as ctx:
         held = ctx.enter_context(tc.tile_pool(name="held", bufs=1))
         early = ctx.enter_context(tc.tile_pool(name="early", bufs=1))
+        late = ctx.enter_context(tc.tile_pool(name="late", bufs=1))
         psum = ctx.enter_context(tc.psum_pool(name="psum", bufs=1))
 
-        s_table = held.tile([P, T], U8, name="s_table", align_bytes=64)
+        s_table = early.tile([P, T], U8, name="s_table", offset=4 * T, align_bytes=64)
         nc.vector.memset(s_table[:].bitcast(I32), 0)
         w_raw = held.tile([P, PACK, H], F32, name="w_raw", align_bytes=64)
         w_rows = w1.rearrange("(p j) c -> p j c", j=PACK)
@@ -54,8 +55,9 @@ def tile_picked_inorm_none_p_kernel(tc, x_words, x_scales, w1, w2_words, w2_scal
         warm_out = held.tile([P, 1], F32, name="warm_out")
         nc.scalar.activation(warm_out[:], warm_in[:], ACT.Abs_reciprocal_sqrt)
         KEPT = ((0, 0), (1, 0), (0, 1), (2, 0), (3, 0), (3, 3))
-        slot = {(0, 0): 0, (0, 1): 3, (0, 2): 6, (1, 0): 0, (1, 1): 3, (1, 2): 9, (2, 0): 0, (2, 1): 3, (2, 2): 9, (3, 0): 0, (3, 3): 3, (3, 1): 6, (3, 2): 12}
-        stats = [held.tile([P, n], F32, name=f"stats{t}")[:] for t, n in enumerate((12, 15, 15, 18))]
+        slot = {(0, 0): 0, (0, 1): 3, (0, 2): 6, (1, 0): 0, (1, 1): 3, (1, 2): 9, (1, 3): 15, (2, 0): 0, (2, 1): 3, (2, 2): 9, (3, 0): 0, (3, 3): 3, (3, 1): 6, (3, 2): 12}
+        stats = [held.tile([P, n], F32, name=f"stats{t}")[:] for t, n in enumerate((12, 21, 15))]
+        stats.append(late.tile([P, 18], F32, name="stats3", offset=0)[:])
         for t, q in KEPT:
             nc.vector.memset(stats[t][:, slot[t, q] : slot[t, q] + 1], float(CHUNK))
 
@@ -69,6 +71,11 @@ def tile_picked_inorm_none_p_kernel(tc, x_words, x_scales, w1, w2_words, w2_scal
             w_bf[:].rearrange("p (u v) m j -> p u m j v", v=2),
             w_raw[:].rearrange("p j (m u v) -> p u m j v", u=2, v=2),
         )
+
+        w2_plane = early.tile([P, N], U8, name="w2_plane", offset=4 * T, align_bytes=64)
+        nc.vector.memset(w2_plane[:].bitcast(I32), 0)
+        for r in range(4):
+            nc.sync.dma_start(w2_plane[r:P:32, :].bitcast(I32), w2_scales[0, r:16:4, :].bitcast(I32))
 
         w_codes = held.tile([P, H], U32, name="w_codes", align_bytes=64)
         w_plane = held.tile([P, H], U8, name="w_plane", align_bytes=64)
@@ -87,10 +94,6 @@ def tile_picked_inorm_none_p_kernel(tc, x_words, x_scales, w1, w2_words, w2_scal
             piece = held.tile([P, n], U32, name=f"x_picked{i}", align_bytes=64)
             nc.vector.tensor_copy(piece[:], x_table[:].indirect(offsets[:, lo // 16 : (lo + n) // 16]))
             picked.append(piece)
-        w2_plane = early.tile([P, N], U8, name="w2_plane", offset=0, align_bytes=64)
-        nc.vector.memset(w2_plane[:].bitcast(I32), 0)
-        for r in range(4):
-            nc.sync.dma_start(w2_plane[r:P:32, :].bitcast(I32), w2_scales[0, r:16:4, :].bitcast(I32))
 
         banks = {}
         sums = {}
@@ -111,7 +114,7 @@ def tile_picked_inorm_none_p_kernel(tc, x_words, x_scales, w1, w2_words, w2_scal
                 stop=True,
             )
 
-        affine = [held.tile([P, 3], F32, name=f"affine{t}") for t in range(PACK)]
+        affine = {t: held.tile([P, 3], F32, name=f"affine{t}") for t in (0, 2, 3)}
         rstd = [held.tile([P, 1], F32, name=f"rstd{t}")[:] for t in range(2)]
         last_roots = held.tile([P, 2], F32, name="last_roots")
         rstd.extend(last_roots[:, i : i + 1] for i in range(2))
@@ -119,21 +122,26 @@ def tile_picked_inorm_none_p_kernel(tc, x_words, x_scales, w1, w2_words, w2_scal
         last_moments = held.tile([P, 2, 2], F32, name="last_moments")
         moments.extend(last_moments[:, i] for i in range(2))
         z_first = held.tile([P, 2, PACK, CHUNK], BF16, name="z_first", align_bytes=64)
-        z_last = [held.tile([P, 1, PACK, CHUNK], BF16, name=f"z_last{i}", align_bytes=64) for i in range(2)]
+        z_last = [held.tile([P, 1, PACK, CHUNK], BF16, name="z_last0", align_bytes=64)]
         wide_gain = held.tile([P, PACK], F32, name="wide_gain")
         nc.scalar.activation(wide_gain[:], gain[:], ACT.Copy, scale=float(CHUNK))
-        gained = {t: held.tile([P, CHUNK], F32, name=f"gained{t}", align_bytes=64) for t in (2, 3)}
-        kept = {(t, q): held.tile([P, CHUNK], F32, name=f"kept{t}{q}", align_bytes=64) for t, q in KEPT}
-        squares = [held.tile([P, CHUNK], BF16, name=f"squares{i}", align_bytes=64) for i in range(2)]
+        gained = {t: held.tile([P, CHUNK], F32, name=f"gained{t}", align_bytes=64) for t in (1, 2, 3)}
+        gained_half = held.tile([P, 2, CHUNK], F32, name="gained_half", align_bytes=64)
+        kept_half = held.tile([P, 2, CHUNK], F32, name="kept_half", align_bytes=64)
+        kept = {(0, q): kept_half[:, q] for q in range(2)}
+        for t, q in KEPT:
+            if t > 0:
+                kept[t, q] = held.tile([P, CHUNK], F32, name=f"kept{t}{q}", align_bytes=64)[:]
+        squares = [held.tile([P, CHUNK], BF16, name="squares0", align_bytes=64), late.tile([P, CHUNK], BF16, name="squares1", offset=128, align_bytes=64)]
 
         def keep(t, q):
             at = slot[t, q]
-            nc.scalar.activation(kept[t, q][:], sums[t, q], ACT.Copy, scale=1.0 / CHUNK, accum_out=stats[t][:, at + 1 : at + 2])
+            nc.scalar.activation(kept[t, q], sums[t, q], ACT.Copy, scale=1.0 / CHUNK, accum_out=stats[t][:, at + 1 : at + 2])
 
         def spread(t, q):
             at = slot[t, q]
             nc.scalar.activation(
-                squares[KEPT.index((t, q)) % 2][:], kept[t, q][:], ACT.Square, scale=-float(CHUNK), bias=stats[t][:, at + 1 : at + 2], accum_out=stats[t][:, at + 2 : at + 3]
+                squares[KEPT.index((t, q)) % 2][:], kept[t, q], ACT.Square, scale=-float(CHUNK), bias=stats[t][:, at + 1 : at + 2], accum_out=stats[t][:, at + 2 : at + 3]
             )
 
         def tally(t, q, src):
@@ -156,14 +164,15 @@ def tile_picked_inorm_none_p_kernel(tc, x_words, x_scales, w1, w2_words, w2_scal
             nc.scalar.activation(affine[t][:], triples[t // 2][:, t % 2], ACT.Copy, scale=rstd[t])
 
         def amplify(t):
-            nc.gpsimd.tensor_scalar(gained[t][:], kept[t, 0][:], wide_gain[:, t : t + 1], 0.0, ALU.mult, ALU.add)
+            nc.gpsimd.tensor_scalar(gained[t][:], kept[t, 0], wide_gain[:, t : t + 1], 0.0, ALU.mult, ALU.add)
 
-        def centre(t):
-            nc.vector.tensor_scalar(z_first[:, 0, t], gained[t][:], triples[1][:, t % 2, 1:2], rstd[t], ALU.add, ALU.mult)
+        def centre(t, half):
+            cols = slice(P * half, P * (half + 1))
+            nc.vector.tensor_scalar(z_first[:, 0, t, cols], gained[t][:, cols], triples[1][:, t % 2, 1:2], rstd[t], ALU.add, ALU.mult)
 
         def normalise(t, q, engine):
             ab = affine[t]
-            src, scale = (kept[t, q][:], ab[:, 2:3]) if (t, q) in KEPT else (sums[t, q], ab[:, 0:1])
+            src, scale = (kept[t, q], ab[:, 2:3]) if (t, q) in KEPT else (sums[t, q], ab[:, 0:1])
             dst = z_first[:, q, t] if q < 2 else z_last[q - 2][:, 0, t]
             if engine is nc.scalar:
                 nc.scalar.activation(dst, src, ACT.Identity, scale=scale, bias=ab[:, 1:2])
@@ -191,38 +200,46 @@ def tile_picked_inorm_none_p_kernel(tc, x_words, x_scales, w1, w2_words, w2_scal
         multiply(1, 2, 1, 0)
         multiply(3, 2, 7, 0)
         multiply(2, 2, 6, 0)
+        amplify(1)
+        nc.gpsimd.tensor_scalar(gained_half[:], kept_half[:], wide_gain[:, 0:1], 0.0, ALU.mult, ALU.add)
         keep(2, 0)
         keep(3, 0)
         spread(2, 0)
         keep(3, 3)
+        amplify(2)
+        amplify(3)
         tally(0, 2, banks[0][:])
-        tally(1, 2, banks[1][:])
+        tally(1, 2, sums[1, 2])
         aggregate(0)
+        tally(1, 3, sums[1, 3])
         tally(2, 2, banks[6][:])
         aggregate(1)
         tally(3, 2, sums[3, 2])
-        shift(1, nc.vector)
-        spread(3, 0)
         root(rstd[0], moments[0][:, 1:2])
         shift(0, nc.scalar)
+        spread(3, 0)
         spread(3, 3)
-        finish(0)
         root(rstd[1], moments[1][:, 1:2])
-        finish(1)
-        amplify(2)
-        amplify(3)
-        normalise(0, 0, nc.gpsimd)
-        normalise(1, 0, nc.gpsimd)
+        shift(1, nc.scalar)
+        finish(0)
+        normalise(0, 2, nc.scalar)
+        nc.gpsimd.tensor_scalar(z_first[:, :, 0], gained_half[:], triples[0][:, 0, 1:2], rstd[0], ALU.add, ALU.mult)
+        nc.gpsimd.tensor_scalar(z_first[:, 0, 1], gained[1][:], triples[0][:, 1, 1:2], rstd[1], ALU.add, ALU.mult)
         aggregate(2)
         aggregate(3)
         shift(2, nc.vector)
+        affine[1] = late.tile([P, 3], F32, name="affine1", offset=0)
+        z_last.append(late.tile([P, 1, PACK, CHUNK], BF16, name="z_last1", offset=128, align_bytes=64))
+        normalise(0, 3, nc.vector)
         shift(3, nc.vector)
         root(last_roots[:], last_moments[:, :, 1])
+        for half in range(2):
+            centre(2, half)
+            centre(3, half)
+        finish(1)
         finish(2)
+        normalise(1, 1, nc.scalar)
         finish(3)
-        centre(2)
-        centre(3)
-        normalise(0, 1, nc.vector)
 
         widths = (128,) * 8
         starts = [sum(widths[:c]) for c in range(len(widths))]
@@ -273,8 +290,10 @@ def tile_picked_inorm_none_p_kernel(tc, x_words, x_scales, w1, w2_words, w2_scal
             nc.sync.dma_start(out_rows[:, rows, lo:hi], res[lo // CHUNK][:, rows, lo % CHUNK : lo % CHUNK + hi - lo])
 
         free = ((3, 5), (2, 4), (3, 5))
-        for t in range(1, PACK):
+        for t in range(2, PACK):
             normalise(t, 1, nc.scalar)
+        for t in range(1, PACK):
+            normalise(t, 2, nc.scalar)
         for b in range(3):
             weave(2 * b, nc.vector)
             weave(2 * b + 1, nc.vector)
@@ -284,17 +303,17 @@ def tile_picked_inorm_none_p_kernel(tc, x_words, x_scales, w1, w2_words, w2_scal
                 if b == 0:
                     project((u,), (0, 1), nc.scalar, f"bank{free[b][u]}")
                     store(P * u, P * (u + 1), (0, 1))
+                    for t in range(1, PACK):
+                        if u == 0:
+                            normalise(t, 3, nc.scalar)
                 else:
                     project((2 * b, 2 * b + 1), (u,), nc.scalar, f"bank{free[b][u]}")
                     store(CHUNK * b, CHUNK * (b + 1), (u,))
-            for t in range(PACK):
-                if b < 2:
-                    normalise(t, b + 2, nc.scalar)
         weave(6, nc.vector)
         weave(7, nc.vector)
         quantise(6)
         quantise(7)
-        project((6,), (0, 1), nc.scalar, "bank7")
+        project((6,), (0, 1), nc.vector, "bank7")
         store(6 * P, 7 * P, (0, 1))
         for u, engine in enumerate((nc.scalar, nc.vector)):
             project((7,), (u,), engine, f"bank{(2, 4)[u]}")

@@ -35,11 +35,11 @@ def tile_picked_inorm_none_p_kernel(tc, x_words, x_scales, w1, w2_words, w2_scal
         nc.vector.memset(s_table[:].bitcast(I32), 0)
         w_raw = held.tile([P, PACK, H], F32, name="w_raw", align_bytes=64)
         w_rows = w1.rearrange("(p j) c -> p j c", j=PACK)
-        nc.sync.dma_start(w_raw[:, :2], w_rows[:, :2])
+        nc.sync.dma_start(w_raw[:, :3], w_rows[:, :3])
         offsets = held.tile([P, S // 16], U16, name="offsets")
         nc.sync.dma_start(offsets[:], offs)
         nc.sync.dma_start(s_table[32:96:4, :].bitcast(I32), x_scales[0].bitcast(I32))
-        nc.sync.dma_start(w_raw[:, 2:], w_rows[:, 2:])
+        nc.sync.dma_start(w_raw[:, 3:], w_rows[:, 3:])
         x_table = early.tile([P, T], U32, name="x_table", offset=0, align_bytes=64)
         x_rows = x_words[0].rearrange("p n r -> p (n r)").bitcast(I32)
         nc.sync.dma_start(x_table[:].bitcast(I32), x_rows)

@@ -100,7 +100,7 @@ def tile_picked_inorm_none_p_kernel(tc, x_words, x_scales, w1, w2_words, w2_scal
 
         def multiply(t, i, b, side):
             lo, n = pieces[i]
-            if side == 0:
+            if side == 0 and (t, i) != (0, 0):
                 banks[b] = psum.tile([P, HALF], F32, name=f"h{t}{i}", tag=f"bank{b}")
             for k in range(n // CHUNK):
                 sums[t, i + k] = banks[b][:, CHUNK * (side + k) : CHUNK * (side + k + 1)]
@@ -179,6 +179,16 @@ def tile_picked_inorm_none_p_kernel(tc, x_words, x_scales, w1, w2_words, w2_scal
             else:
                 engine.tensor_scalar(dst, src, scale, ab[:, 1:2], ALU.mult, ALU.add)
 
+        banks[0] = psum.tile([P, HALF], F32, name="h00", tag="bank0")
+        nc.tensor.matmul_mx(
+            out=banks[0][:],
+            lhsT=w_codes[:, :P].bitcast(FP8X4),
+            lhsT_scale=w_plane[:, :P],
+            rhs=w_codes[:].bitcast(FP8X4),
+            rhs_scale=w_plane[:],
+            start=True,
+            stop=True,
+        )
         multiply(0, 0, 0, 0)
         multiply(1, 0, 1, 0)
         multiply(1, 1, 2, 0)

@@ -55,8 +55,8 @@ def tile_picked_inorm_none_p_kernel(tc, x_words, x_scales, w1, w2_words, w2_scal
         warm_out = held.tile([P, 1], F32, name="warm_out")
         nc.scalar.activation(warm_out[:], warm_in[:], ACT.Abs_reciprocal_sqrt)
         KEPT = ((0, 0), (1, 0), (0, 1), (2, 0), (3, 0), (3, 3))
-        slot = {(0, 0): 0, (0, 1): 3, (0, 2): 6, (1, 0): 0, (1, 1): 3, (1, 2): 9, (1, 3): 15, (2, 0): 0, (2, 1): 3, (2, 2): 9, (3, 0): 0, (3, 3): 3, (3, 1): 6, (3, 2): 12}
-        stats = [held.tile([P, n], F32, name=f"stats{t}")[:] for t, n in enumerate((12, 21, 15))]
+        slot = {(0, 0): 0, (0, 1): 3, (0, 2): 6, (0, 3): 12, (1, 0): 0, (1, 1): 3, (1, 2): 9, (1, 3): 15, (2, 0): 0, (2, 1): 3, (2, 2): 9, (3, 0): 0, (3, 3): 3, (3, 1): 6, (3, 2): 12}
+        stats = [held.tile([P, n], F32, name=f"stats{t}")[:] for t, n in enumerate((18, 21, 15))]
         stats.append(late.tile([P, 18], F32, name="stats3", offset=0)[:])
         for t, q in KEPT:
             nc.vector.memset(stats[t][:, slot[t, q] : slot[t, q] + 1], float(CHUNK))
@@ -88,18 +88,15 @@ def tile_picked_inorm_none_p_kernel(tc, x_words, x_scales, w1, w2_words, w2_scal
             nc.scalar.activation(triples[i][:, :, 0], gain[:, 2 * i : 2 * i + 2], ACT.Copy)
             nc.scalar.activation(triples[i][:, :, 2], gain[:, 2 * i : 2 * i + 2], ACT.Copy, scale=float(CHUNK))
 
-        pieces = ((0, CHUNK), (CHUNK, CHUNK), (HALF, HALF))
-        picked = []
-        for i, (lo, n) in enumerate(pieces):
-            piece = held.tile([P, n], U32, name=f"x_picked{i}", align_bytes=64)
-            nc.vector.tensor_copy(piece[:], x_table[:].indirect(offsets[:, lo // 16 : (lo + n) // 16]))
-            picked.append(piece)
+        picked = held.tile([P, S], U32, name="x_picked", align_bytes=64)
+        for lo in range(0, S, CHUNK):
+            nc.vector.tensor_copy(picked[:, lo : lo + CHUNK], x_table[:].indirect(offsets[:, lo // 16 : (lo + CHUNK) // 16]))
 
         banks = {}
         sums = {}
 
-        def multiply(t, i, b, side):
-            lo, n = pieces[i]
+        def multiply(t, i, b, side, n=CHUNK):
+            lo = CHUNK * i
             if side == 0 and (t, i) != (0, 0):
                 banks[b] = psum.tile([P, HALF], F32, name=f"h{t}{i}", tag=f"bank{b}")
             for k in range(n // CHUNK):
@@ -108,7 +105,7 @@ def tile_picked_inorm_none_p_kernel(tc, x_words, x_scales, w1, w2_words, w2_scal
                 out=banks[b][:, CHUNK * side : CHUNK * side + n],
                 lhsT=w_codes[:, P * t : P * (t + 1)].bitcast(FP8X4),
                 lhsT_scale=w_plane[:, P * t : P * (t + 1)],
-                rhs=picked[i][:].bitcast(FP8X4),
+                rhs=picked[:, lo : lo + n].bitcast(FP8X4),
                 rhs_scale=x_plane[:, lo : lo + n],
                 start=True,
                 stop=True,
@@ -204,25 +201,29 @@ def tile_picked_inorm_none_p_kernel(tc, x_words, x_scales, w1, w2_words, w2_scal
         tally(1, 1, sums[1, 1])
         tally(2, 1, sums[2, 1])
         tally(3, 1, sums[3, 1])
-        multiply(0, 2, 0, 0)
-        multiply(2, 0, 5, 0)
+        multiply(0, 2, 5, 0)
+        multiply(2, 0, 6, 0)
+        multiply(0, 3, 7, 0)
+        multiply(1, 2, 0, 0)
         multiply(3, 0, 2, 1)
-        multiply(1, 2, 1, 0)
-        multiply(3, 2, 7, 0)
-        multiply(2, 2, 6, 0)
+        multiply(1, 3, 1, 0)
         amplify(1)
         nc.gpsimd.tensor_scalar(gained_half[:], kept_half[:], wide_gain[:, 0:1], 0.0, ALU.mult, ALU.add)
         keep(2, 0)
+        multiply(3, 3, 6, 1)
+        multiply(2, 2, 3, 0, HALF)
         keep(3, 0)
         spread(2, 0)
-        keep(3, 3)
         amplify(2)
         amplify(3)
-        tally(0, 2, banks[0][:])
+        tally(0, 2, sums[0, 2])
+        tally(0, 3, sums[0, 3])
+        multiply(3, 2, 5, 1)
+        keep(3, 3)
         tally(1, 2, sums[1, 2])
         aggregate(0)
         tally(1, 3, sums[1, 3])
-        tally(2, 2, banks[6][:])
+        tally(2, 2, banks[3][:])
         aggregate(1)
         tally(3, 2, sums[3, 2])
         root(rstd[0], moments[0][:, 1:2])
@@ -299,15 +300,17 @@ def tile_picked_inorm_none_p_kernel(tc, x_words, x_scales, w1, w2_words, w2_scal
             rows = slice(us[0], us[-1] + 1)
             nc.sync.dma_start(out_rows[:, rows, lo:hi], res[lo // CHUNK][:, rows, lo % CHUNK : lo % CHUNK + hi - lo])
 
-        free = ((3, 5), (2, 4), (3, 5))
+        free = ((6, 7), (2, 4), (0, 5))
         for t in range(2, PACK):
             normalise(t, 1, nc.scalar)
         for t in range(1, PACK):
             normalise(t, 2, nc.scalar)
+        weave(0, nc.vector)
         for b in range(3):
-            weave(2 * b, nc.vector)
             weave(2 * b + 1, nc.vector)
             quantise(2 * b)
+            if b < 2:
+                weave(2 * b + 2, nc.vector)
             quantise(2 * b + 1)
             for u in range(2):
                 if b == 0:
@@ -323,7 +326,8 @@ def tile_picked_inorm_none_p_kernel(tc, x_words, x_scales, w1, w2_words, w2_scal
         weave(7, nc.vector)
         quantise(6)
         quantise(7)
-        project((6,), (0, 1), nc.vector, "bank7")
+        for u, engine in enumerate((nc.scalar, nc.vector)):
+            project((6,), (u,), engine, f"bank{(6, 7)[u]}")
         store(6 * P, 7 * P, (0, 1))
         for u, engine in enumerate((nc.scalar, nc.vector)):
             project((7,), (u,), engine, f"bank{(2, 4)[u]}")

@@ -155,7 +155,7 @@ def tile_picked_inorm_none_p_kernel(tc, x_words, x_scales, w1, w2_words, w2_scal
             if engine is nc.scalar:
                 nc.scalar.activation(dst, moments[t][:, 0:1], ACT.Copy, scale=neg_gain[:, t : t + 1])
             else:
-                nc.vector.tensor_scalar(dst, moments[t][:, 0:1], neg_gain[:, t : t + 1], 0.0, ALU.mult, ALU.add)
+                engine.tensor_scalar(dst, moments[t][:, 0:1], neg_gain[:, t : t + 1], 0.0, ALU.mult, ALU.add)
 
         def finish(t):
             nc.scalar.activation(affine[t][:], triples[t // 2][:, t % 2], ACT.Copy, scale=rstd[t])
@@ -227,7 +227,7 @@ def tile_picked_inorm_none_p_kernel(tc, x_words, x_scales, w1, w2_words, w2_scal
         aggregate(1)
         tally(3, 2, sums[3, 2])
         root(rstd[0], moments[0][:, 1:2])
-        shift(0, nc.scalar)
+        shift(0, nc.gpsimd)
         spread(3, 0)
         spread(3, 3)
         root(rstd[1], moments[1][:, 1:2])

@@ -119,7 +119,7 @@ def tile_picked_inorm_none_p_kernel(tc, x_words, x_scales, w1, w2_words, w2_scal
         last_moments = held.tile([P, 2, 2], F32, name="last_moments")
         moments.extend(last_moments[:, i] for i in range(2))
         z_first = held.tile([P, 2, PACK, CHUNK], BF16, name="z_first", align_bytes=64)
-        z_last = [held.tile([P, 1, PACK, CHUNK], BF16, name="z_last0", align_bytes=64)]
+        z_last = []
         wide_gain = held.tile([P, PACK], F32, name="wide_gain")
         nc.scalar.activation(wide_gain[:], gain[:], ACT.Copy, scale=float(CHUNK))
         gained = {t: held.tile([P, CHUNK], F32, name=f"gained{t}", align_bytes=64) for t in (1, 2, 3)}
@@ -233,17 +233,18 @@ def tile_picked_inorm_none_p_kernel(tc, x_words, x_scales, w1, w2_words, w2_scal
         root(rstd[1], moments[1][:, 1:2])
         shift(1, nc.scalar)
         finish(0)
+        z_second = late.tile([P, 2, PACK, CHUNK], BF16, name="z_second", offset=128, align_bytes=64)
+        z_last.extend(z_second[:, i : i + 1] for i in range(2))
         normalise(0, 2, nc.scalar)
         nc.gpsimd.tensor_scalar(z_first[:, :, 0], gained_half[:], triples[0][:, 0, 1:2], rstd[0], ALU.add, ALU.mult)
-        nc.gpsimd.tensor_scalar(z_first[:, 0, 1], gained[1][:], triples[0][:, 1, 1:2], rstd[1], ALU.add, ALU.mult)
         aggregate(2)
         aggregate(3)
-        shift(2, nc.vector)
         affine[1] = late.tile([P, 3], F32, name="affine1", offset=0)
-        z_last.append(late.tile([P, 1, PACK, CHUNK], BF16, name="z_last1", offset=128, align_bytes=64))
         normalise(0, 3, nc.vector)
-        shift(3, nc.vector)
+        nc.vector.tensor_scalar(z_first[:, 0, 1], gained[1][:], triples[0][:, 1, 1:2], rstd[1], ALU.add, ALU.mult)
         root(last_roots[:], last_moments[:, :, 1])
+        shift(2, nc.scalar)
+        shift(3, nc.scalar)
         for half in range(2):
             centre(2, half)
             centre(3, half)
@@ -303,8 +304,9 @@ def tile_picked_inorm_none_p_kernel(tc, x_words, x_scales, w1, w2_words, w2_scal
         free = ((6, 7), (2, 4), (0, 5))
         for t in range(2, PACK):
             normalise(t, 1, nc.scalar)
-        for t in range(1, PACK):
+        for t in (1, 3):
             normalise(t, 2, nc.scalar)
+        nc.scalar.activation(z_second[:, :, 2], banks[3][:].rearrange("p (q n) -> p q n", q=2), ACT.Identity, scale=affine[2][:, 0:1], bias=affine[2][:, 1:2])
         weave(0, nc.vector)
         for b in range(3):
             weave(2 * b + 1, nc.vector)
@@ -316,7 +318,7 @@ def tile_picked_inorm_none_p_kernel(tc, x_words, x_scales, w1, w2_words, w2_scal
                 if b == 0:
                     project((u,), (0, 1), nc.scalar, f"bank{free[b][u]}")
                     store(P * u, P * (u + 1), (0, 1))
-                    for t in range(1, PACK):
+                    for t in (1, 3):
                         if u == 0:
                             normalise(t, 3, nc.scalar)
                 else:

@@ -19,8 +19,11 @@ ALU = mybir.AluOpType
 
 P = 128
 PACK = 4
-HALF = 512
-CHUNK = 256
+BANK = 512
+QUARTER = 256
+W_FIRST = 3
+KEPT = ((0, 0), (1, 0), (0, 1), (2, 0), (3, 0), (3, 3))
+TALLIED = ((0, 2), (0, 3), (1, 1), (1, 2), (1, 3), (2, 1), (2, 2), (3, 1), (3, 2))
 
 
 def tile_picked_inorm_none_p_kernel(tc, x_words, x_scales, w1, w2_words, w2_scales, gamma, offs, out):
@@ -35,11 +38,11 @@ def tile_picked_inorm_none_p_kernel(tc, x_words, x_scales, w1, w2_words, w2_scal
         nc.vector.memset(s_table[:].bitcast(I32), 0)
         w_raw = held.tile([P, PACK, H], F32, name="w_raw", align_bytes=64)
         w_rows = w1.rearrange("(p j) c -> p j c", j=PACK)
-        nc.sync.dma_start(w_raw[:, :3], w_rows[:, :3])
+        nc.sync.dma_start(w_raw[:, :W_FIRST], w_rows[:, :W_FIRST])
         offsets = held.tile([P, S // 16], U16, name="offsets")
         nc.sync.dma_start(offsets[:], offs)
         nc.sync.dma_start(s_table[32:96:4, :].bitcast(I32), x_scales[0].bitcast(I32))
-        nc.sync.dma_start(w_raw[:, 3:], w_rows[:, 3:])
+        nc.sync.dma_start(w_raw[:, W_FIRST:], w_rows[:, W_FIRST:])
         x_table = early.tile([P, T], U32, name="x_table", offset=0, align_bytes=64)
         x_rows = x_words[0].rearrange("p n r -> p (n r)").bitcast(I32)
         nc.sync.dma_start(x_table[:].bitcast(I32), x_rows)
@@ -54,12 +57,16 @@ def tile_picked_inorm_none_p_kernel(tc, x_words, x_scales, w1, w2_words, w2_scal
         nc.vector.memset(warm_in[:], 1.0)
         warm_out = held.tile([P, 1], F32, name="warm_out")
         nc.scalar.activation(warm_out[:], warm_in[:], ACT.Abs_reciprocal_sqrt)
-        KEPT = ((0, 0), (1, 0), (0, 1), (2, 0), (3, 0), (3, 3))
-        slot = {(0, 0): 0, (0, 1): 3, (0, 2): 6, (0, 3): 12, (1, 0): 0, (1, 1): 3, (1, 2): 9, (1, 3): 15, (2, 0): 0, (2, 1): 3, (2, 2): 9, (3, 0): 0, (3, 3): 3, (3, 1): 6, (3, 2): 12}
-        stats = [held.tile([P, n], F32, name=f"stats{t}")[:] for t, n in enumerate((18, 21, 15))]
-        stats.append(late.tile([P, 18], F32, name="stats3", offset=0)[:])
+
+        slot, used = {}, [0] * PACK
+        for runs, width in ((KEPT, 3), (TALLIED, 6)):
+            for t, q in runs:
+                slot[t, q] = used[t]
+                used[t] = used[t] + width
+        stats = [held.tile([P, used[t]], F32, name=f"stats{t}")[:] for t in range(PACK - 1)]
+        stats.append(late.tile([P, used[3]], F32, name="stats3", offset=0)[:])
         for t, q in KEPT:
-            nc.vector.memset(stats[t][:, slot[t, q] : slot[t, q] + 1], float(CHUNK))
+            nc.vector.memset(stats[t][:, slot[t, q] : slot[t, q] + 1], float(QUARTER))
 
         s_picked = held.tile([P, S], U8, name="s_picked", align_bytes=64)
         nc.vector.tensor_copy(s_picked[:], s_table[:].indirect(offsets[:]))
@@ -83,26 +90,26 @@ def tile_picked_inorm_none_p_kernel(tc, x_words, x_scales, w1, w2_words, w2_scal
 
         neg_gain = held.tile([P, PACK], F32, name="neg_gain")
         nc.scalar.activation(neg_gain[:], gain[:], ACT.Copy, scale=-1.0)
-        triples = [held.tile([P, 2, 3], F32, name=f"triples{i}") for i in range(2)]
+        raw_factors = [held.tile([P, 2, 2], F32, name=f"raw_factors{i}") for i in range(2)]
         for i in range(2):
-            nc.scalar.activation(triples[i][:, :, 0], gain[:, 2 * i : 2 * i + 2], ACT.Copy)
-            nc.scalar.activation(triples[i][:, :, 2], gain[:, 2 * i : 2 * i + 2], ACT.Copy, scale=float(CHUNK))
+            nc.scalar.activation(raw_factors[i][:, :, 0], gain[:, 2 * i : 2 * i + 2], ACT.Copy)
 
         picked = held.tile([P, S], U32, name="x_picked", align_bytes=64)
-        for lo in range(0, S, CHUNK):
-            nc.vector.tensor_copy(picked[:, lo : lo + CHUNK], x_table[:].indirect(offsets[:, lo // 16 : (lo + CHUNK) // 16]))
+        for lo in range(0, S, QUARTER):
+            nc.vector.tensor_copy(picked[:, lo : lo + QUARTER], x_table[:].indirect(offsets[:, lo // 16 : (lo + QUARTER) // 16]))
 
         banks = {}
         sums = {}
 
-        def multiply(t, i, b, side, n=CHUNK):
-            lo = CHUNK * i
-            if side == 0 and (t, i) != (0, 0):
-                banks[b] = psum.tile([P, HALF], F32, name=f"h{t}{i}", tag=f"bank{b}")
-            for k in range(n // CHUNK):
-                sums[t, i + k] = banks[b][:, CHUNK * (side + k) : CHUNK * (side + k + 1)]
+        def open_bank(b, name):
+            banks[b] = psum.tile([P, BANK], F32, name=name, tag=f"bank{b}")
+
+        def multiply(t, q, b, side, n=QUARTER):
+            lo = QUARTER * q
+            for k in range(n // QUARTER):
+                sums[t, q + k] = banks[b][:, QUARTER * (side + k) : QUARTER * (side + k + 1)]
             nc.tensor.matmul_mx(
-                out=banks[b][:, CHUNK * side : CHUNK * side + n],
+                out=banks[b][:, QUARTER * side : QUARTER * side + n],
                 lhsT=w_codes[:, P * t : P * (t + 1)].bitcast(FP8X4),
                 lhsT_scale=w_plane[:, P * t : P * (t + 1)],
                 rhs=picked[:, lo : lo + n].bitcast(FP8X4),
@@ -111,34 +118,47 @@ def tile_picked_inorm_none_p_kernel(tc, x_words, x_scales, w1, w2_words, w2_scal
                 stop=True,
             )
 
-        affine = {t: held.tile([P, 3], F32, name=f"affine{t}") for t in (0, 2, 3)}
+        def multiply_fresh(t, q, b, n=QUARTER):
+            open_bank(b, f"h{t}{q}")
+            multiply(t, q, b, 0, n)
+
+        affine = {t: held.tile([P, 2], F32, name=f"affine{t}") for t in (0, 2, 3)}
         rstd = [held.tile([P, 1], F32, name=f"rstd{t}")[:] for t in range(2)]
         last_roots = held.tile([P, 2], F32, name="last_roots")
         rstd.extend(last_roots[:, i : i + 1] for i in range(2))
         moments = [held.tile([P, 2], F32, name=f"moments{t}")[:] for t in range(2)]
         last_moments = held.tile([P, 2, 2], F32, name="last_moments")
         moments.extend(last_moments[:, i] for i in range(2))
-        z_first = held.tile([P, 2, PACK, CHUNK], BF16, name="z_first", align_bytes=64)
-        z_last = []
+        z_first = held.tile([P, 2, PACK, QUARTER], BF16, name="z_first", align_bytes=64)
+        z_rows = [z_first[:, q] for q in range(2)]
         wide_gain = held.tile([P, PACK], F32, name="wide_gain")
-        nc.scalar.activation(wide_gain[:], gain[:], ACT.Copy, scale=float(CHUNK))
-        gained = {t: held.tile([P, CHUNK], F32, name=f"gained{t}", align_bytes=64) for t in (1, 2, 3)}
-        gained_half = held.tile([P, 2, CHUNK], F32, name="gained_half", align_bytes=64)
-        kept_half = held.tile([P, 2, CHUNK], F32, name="kept_half", align_bytes=64)
+        nc.scalar.activation(wide_gain[:], gain[:], ACT.Copy, scale=float(QUARTER))
+        gained = {t: held.tile([P, QUARTER], F32, name=f"gained{t}", align_bytes=64) for t in (1, 2, 3)}
+        gained_half = held.tile([P, 2, QUARTER], F32, name="gained_half", align_bytes=64)
+        kept_half = held.tile([P, 2, QUARTER], F32, name="kept_half", align_bytes=64)
         kept = {(0, q): kept_half[:, q] for q in range(2)}
         for t, q in KEPT:
             if t > 0:
-                kept[t, q] = held.tile([P, CHUNK], F32, name=f"kept{t}{q}", align_bytes=64)[:]
-        squares = [held.tile([P, CHUNK], BF16, name="squares0", align_bytes=64), late.tile([P, CHUNK], BF16, name="squares1", offset=128, align_bytes=64)]
+                kept[t, q] = held.tile([P, QUARTER], F32, name=f"kept{t}{q}", align_bytes=64)[:]
+        after_stats3 = 128
+        squares = [
+            held.tile([P, QUARTER], BF16, name="squares0", align_bytes=64),
+            late.tile([P, QUARTER], BF16, name="squares1", offset=after_stats3, align_bytes=64),
+        ]
 
         def keep(t, q):
             at = slot[t, q]
-            nc.scalar.activation(kept[t, q], sums[t, q], ACT.Copy, scale=1.0 / CHUNK, accum_out=stats[t][:, at + 1 : at + 2])
+            nc.scalar.activation(kept[t, q], sums[t, q], ACT.Copy, scale=1.0 / QUARTER, accum_out=stats[t][:, at + 1 : at + 2])
 
         def spread(t, q):
             at = slot[t, q]
             nc.scalar.activation(
-                squares[KEPT.index((t, q)) % 2][:], kept[t, q], ACT.Square, scale=-float(CHUNK), bias=stats[t][:, at + 1 : at + 2], accum_out=stats[t][:, at + 2 : at + 3]
+                squares[KEPT.index((t, q)) % 2][:],
+                kept[t, q],
+                ACT.Square,
+                scale=-float(QUARTER),
+                bias=stats[t][:, at + 1 : at + 2],
+                accum_out=stats[t][:, at + 2 : at + 3],
             )
 
         def tally(t, q, src):
@@ -150,33 +170,35 @@ def tile_picked_inorm_none_p_kernel(tc, x_words, x_scales, w1, w2_words, w2_scal
         def root(dst, variance):
             nc.scalar.activation(dst, variance, ACT.Abs_reciprocal_sqrt, bias=EPS)
 
+        def shifted(t):
+            return raw_factors[t // 2][:, t % 2, 1:2]
+
         def shift(t, engine):
-            dst = triples[t // 2][:, t % 2, 1:2]
             if engine is nc.scalar:
-                nc.scalar.activation(dst, moments[t][:, 0:1], ACT.Copy, scale=neg_gain[:, t : t + 1])
+                nc.scalar.activation(shifted(t), moments[t][:, 0:1], ACT.Copy, scale=neg_gain[:, t : t + 1])
             else:
-                engine.tensor_scalar(dst, moments[t][:, 0:1], neg_gain[:, t : t + 1], 0.0, ALU.mult, ALU.add)
+                engine.tensor_scalar(shifted(t), moments[t][:, 0:1], neg_gain[:, t : t + 1], 0.0, ALU.mult, ALU.add)
 
         def finish(t):
-            nc.scalar.activation(affine[t][:], triples[t // 2][:, t % 2], ACT.Copy, scale=rstd[t])
+            nc.scalar.activation(affine[t][:], raw_factors[t // 2][:, t % 2], ACT.Copy, scale=rstd[t])
 
-        def amplify(t):
-            nc.gpsimd.tensor_scalar(gained[t][:], kept[t, 0], wide_gain[:, t : t + 1], 0.0, ALU.mult, ALU.add)
+        def amplify(t, dst, src):
+            nc.gpsimd.tensor_scalar(dst, src, wide_gain[:, t : t + 1], 0.0, ALU.mult, ALU.add)
 
-        def centre(t, half):
-            cols = slice(P * half, P * (half + 1))
-            nc.vector.tensor_scalar(z_first[:, 0, t, cols], gained[t][:, cols], triples[1][:, t % 2, 1:2], rstd[t], ALU.add, ALU.mult)
+        def centre(t, dst, src, engine):
+            engine.tensor_scalar(dst, src, shifted(t), rstd[t], ALU.add, ALU.mult)
 
-        def normalise(t, q, engine):
-            ab = affine[t]
-            src, scale = (kept[t, q], ab[:, 2:3]) if (t, q) in KEPT else (sums[t, q], ab[:, 0:1])
-            dst = z_first[:, q, t] if q < 2 else z_last[q - 2][:, 0, t]
+        def normalise(t, dst, src, engine):
+            scale, bias = affine[t][:, 0:1], affine[t][:, 1:2]
             if engine is nc.scalar:
-                nc.scalar.activation(dst, src, ACT.Identity, scale=scale, bias=ab[:, 1:2])
+                nc.scalar.activation(dst, src, ACT.Identity, scale=scale, bias=bias)
             else:
-                engine.tensor_scalar(dst, src, scale, ab[:, 1:2], ALU.mult, ALU.add)
+                engine.tensor_scalar(dst, src, scale, bias, ALU.mult, ALU.add)
 
-        banks[0] = psum.tile([P, HALF], F32, name="h00", tag="bank0")
+        def normalise_unit(t, q, engine):
+            normalise(t, z_rows[q][:, t], sums[t, q], engine)
+
+        open_bank(0, "h00")
         nc.tensor.matmul_mx(
             out=banks[0][:],
             lhsT=w_codes[:, :P].bitcast(FP8X4),
@@ -186,11 +208,12 @@ def tile_picked_inorm_none_p_kernel(tc, x_words, x_scales, w1, w2_words, w2_scal
             start=True,
             stop=True,
         )
+
         multiply(0, 0, 0, 0)
-        multiply(1, 0, 1, 0)
-        multiply(1, 1, 2, 0)
-        multiply(0, 1, 3, 0)
-        multiply(2, 1, 4, 0)
+        multiply_fresh(1, 0, 1)
+        multiply_fresh(1, 1, 2)
+        multiply_fresh(0, 1, 3)
+        multiply_fresh(2, 1, 4)
         multiply(3, 1, 4, 1)
         keep(0, 0)
         keep(1, 0)
@@ -198,90 +221,84 @@ def tile_picked_inorm_none_p_kernel(tc, x_words, x_scales, w1, w2_words, w2_scal
         keep(0, 1)
         spread(1, 0)
         spread(0, 1)
-        tally(1, 1, sums[1, 1])
-        tally(2, 1, sums[2, 1])
-        tally(3, 1, sums[3, 1])
-        multiply(0, 2, 5, 0)
-        multiply(2, 0, 6, 0)
-        multiply(0, 3, 7, 0)
-        multiply(1, 2, 0, 0)
+        for t in range(1, PACK):
+            tally(t, 1, sums[t, 1])
+        multiply_fresh(0, 2, 5)
+        multiply_fresh(2, 0, 6)
+        multiply_fresh(0, 3, 7)
+        multiply_fresh(1, 2, 0)
         multiply(3, 0, 2, 1)
-        multiply(1, 3, 1, 0)
-        amplify(1)
-        nc.gpsimd.tensor_scalar(gained_half[:], kept_half[:], wide_gain[:, 0:1], 0.0, ALU.mult, ALU.add)
+        multiply_fresh(1, 3, 1)
+        amplify(1, gained[1][:], kept[1, 0])
+        amplify(0, gained_half[:], kept_half[:])
         keep(2, 0)
         multiply(3, 3, 6, 1)
-        multiply(2, 2, 3, 0, HALF)
+        multiply_fresh(2, 2, 3, BANK)
         keep(3, 0)
         spread(2, 0)
-        amplify(2)
-        amplify(3)
+        amplify(2, gained[2][:], kept[2, 0])
         tally(0, 2, sums[0, 2])
         tally(0, 3, sums[0, 3])
         multiply(3, 2, 5, 1)
         keep(3, 3)
         tally(1, 2, sums[1, 2])
         aggregate(0)
+        shift(0, nc.gpsimd)
+        amplify(3, gained[3][:], kept[3, 0])
         tally(1, 3, sums[1, 3])
         tally(2, 2, banks[3][:])
         aggregate(1)
         tally(3, 2, sums[3, 2])
         root(rstd[0], moments[0][:, 1:2])
-        shift(0, nc.gpsimd)
         spread(3, 0)
         spread(3, 3)
+
+        finish(0)
         root(rstd[1], moments[1][:, 1:2])
         shift(1, nc.scalar)
-        finish(0)
-        z_second = late.tile([P, 2, PACK, CHUNK], BF16, name="z_second", offset=128, align_bytes=64)
-        z_last.extend(z_second[:, i : i + 1] for i in range(2))
-        normalise(0, 2, nc.scalar)
-        nc.gpsimd.tensor_scalar(z_first[:, :, 0], gained_half[:], triples[0][:, 0, 1:2], rstd[0], ALU.add, ALU.mult)
+        z_second = late.tile([P, 2, PACK, QUARTER], BF16, name="z_second", offset=after_stats3, align_bytes=64)
+        z_rows.extend(z_second[:, q] for q in range(2))
+        normalise_unit(0, 2, nc.scalar)
+        centre(0, z_first[:, :, 0], gained_half[:], nc.gpsimd)
         aggregate(2)
         aggregate(3)
-        affine[1] = late.tile([P, 3], F32, name="affine1", offset=0)
-        normalise(0, 3, nc.vector)
-        nc.vector.tensor_scalar(z_first[:, 0, 1], gained[1][:], triples[0][:, 1, 1:2], rstd[1], ALU.add, ALU.mult)
+        affine[1] = late.tile([P, 2], F32, name="affine1", offset=0)
+        normalise_unit(0, 3, nc.vector)
+        shift(3, nc.vector)
+        centre(1, z_rows[0][:, 1], gained[1][:], nc.vector)
         root(last_roots[:], last_moments[:, :, 1])
         shift(2, nc.scalar)
-        shift(3, nc.scalar)
-        for half in range(2):
-            centre(2, half)
-            centre(3, half)
+        centre(2, z_rows[0][:, 2], gained[2][:], nc.vector)
+        for lo in (0, P):
+            centre(3, z_rows[0][:, 3, lo : lo + P], gained[3][:, lo : lo + P], nc.vector)
         finish(1)
         finish(2)
-        normalise(1, 1, nc.scalar)
+        normalise_unit(1, 1, nc.scalar)
         finish(3)
 
-        widths = (128,) * 8
-        starts = [sum(widths[:c]) for c in range(len(widths))]
         woven, codes, planes = {}, {}, {}
-        res = [held.tile([P, 2, CHUNK], F32, name=f"res{b}", align_bytes=64) for b in range(S // CHUNK)]
+        res = [held.tile([P, 2, QUARTER], F32, name=f"res{q}", align_bytes=64) for q in range(S // QUARTER)]
 
-        def weave(c, engine):
-            woven[c] = held.tile([P, widths[c], PACK], BF16, name=f"woven{c}", align_bytes=64)
-            dst = woven[c][:].rearrange("p (c i) t -> p c t i", i=4)
-            q, lo = divmod(starts[c], CHUNK)
-            rows = z_first[:, q] if q < 2 else z_last[q - 2][:, 0]
-            src = rows[:, :, lo : lo + widths[c]].rearrange("p t (c i) -> p c t i", i=4)
-            if engine is nc.vector:
-                nc.vector.tensor_copy(dst, src)
-            else:
-                nc.scalar.copy(dst, src)
+        def weave(c):
+            woven[c] = held.tile([P, P, PACK], BF16, name=f"woven{c}", align_bytes=64)
+            q, lo = divmod(P * c, QUARTER)
+            nc.vector.tensor_copy(
+                woven[c][:].rearrange("p (g i) t -> p g t i", i=4),
+                z_rows[q][:, :, lo : lo + P].rearrange("p t (g i) -> p g t i", i=4),
+            )
 
         def quantise(c):
-            codes[c] = held.tile([P, widths[c]], U32, name=f"z_codes{c}", align_bytes=64)
-            planes[c] = held.tile([P, widths[c]], U8, name=f"z_plane{c}", align_bytes=64)
+            codes[c] = held.tile([P, P], U32, name=f"z_codes{c}", align_bytes=64)
+            planes[c] = held.tile([P, P], U8, name=f"z_plane{c}", align_bytes=64)
             nc.vector.quantize_mx(out=codes[c][:].bitcast(FP8X4), scales=planes[c][:], in_=woven[c][:].rearrange("p n t -> p (n t)"))
 
-        def project(chunks, us, engine, tag):
-            first = starts[chunks[0]]
-            n = sum(widths[c] for c in chunks)
-            acc = psum.tile([P, len(us), n], F32, name=f"acc{chunks[0]}{us[0]}", tag=tag)
+        def project(chunks, us, engine, b):
+            first, n = P * chunks[0], P * len(chunks)
+            acc = psum.tile([P, len(us), n], F32, name=f"acc{chunks[0]}{us[0]}", tag=f"bank{b}")
             for c in chunks:
                 for i, u in enumerate(us):
                     nc.tensor.matmul_mx(
-                        out=acc[:, i, starts[c] - first : starts[c] - first + widths[c]],
+                        out=acc[:, i, P * c - first : P * (c + 1) - first],
                         lhsT=w2_codes[:, 2 * P * u : 2 * P * (u + 1)].bitcast(FP4X4),
                         lhsT_scale=w2_plane[:, P * u : P * (u + 1)],
                         rhs=codes[c][:].bitcast(FP8X4),
@@ -289,7 +306,7 @@ def tile_picked_inorm_none_p_kernel(tc, x_words, x_scales, w1, w2_words, w2_scal
                         start=True,
                         stop=True,
                     )
-            dst = res[first // CHUNK][:, us[0] : us[-1] + 1, first % CHUNK : first % CHUNK + n]
+            dst = res[first // QUARTER][:, us[0] : us[-1] + 1, first % QUARTER : first % QUARTER + n]
             if engine is nc.vector:
                 nc.vector.tensor_copy(dst, acc[:])
             else:
@@ -297,40 +314,36 @@ def tile_picked_inorm_none_p_kernel(tc, x_words, x_scales, w1, w2_words, w2_scal
 
         out_rows = out.rearrange("(u p) s -> p u s", p=P)
 
-        def store(lo, hi, us):
+        def store(lo, n, us):
             rows = slice(us[0], us[-1] + 1)
-            nc.sync.dma_start(out_rows[:, rows, lo:hi], res[lo // CHUNK][:, rows, lo % CHUNK : lo % CHUNK + hi - lo])
+            nc.sync.dma_start(out_rows[:, rows, lo : lo + n], res[lo // QUARTER][:, rows, lo % QUARTER : lo % QUARTER + n])
 
-        free = ((6, 7), (2, 4), (0, 5))
-        for t in range(2, PACK):
-            normalise(t, 1, nc.scalar)
+        free = ((7, 5), (2, 4), (0, 3))
+        for t in (2, 3):
+            normalise_unit(t, 1, nc.scalar)
         for t in (1, 3):
-            normalise(t, 2, nc.scalar)
-        nc.scalar.activation(z_second[:, :, 2], banks[3][:].rearrange("p (q n) -> p q n", q=2), ACT.Identity, scale=affine[2][:, 0:1], bias=affine[2][:, 1:2])
-        weave(0, nc.vector)
-        for b in range(3):
-            weave(2 * b + 1, nc.vector)
-            quantise(2 * b)
-            if b < 2:
-                weave(2 * b + 2, nc.vector)
-            quantise(2 * b + 1)
-            for u in range(2):
-                if b == 0:
-                    project((u,), (0, 1), nc.scalar, f"bank{free[b][u]}")
-                    store(P * u, P * (u + 1), (0, 1))
-                    for t in (1, 3):
-                        if u == 0:
-                            normalise(t, 3, nc.scalar)
+            normalise_unit(t, 2, nc.scalar)
+        normalise(2, z_second[:, :, 2], banks[3][:].rearrange("p (q n) -> p q n", q=2), nc.scalar)
+        weave(0)
+        for q in range(3):
+            weave(2 * q + 1)
+            quantise(2 * q)
+            if q < 2:
+                weave(2 * q + 2)
+            quantise(2 * q + 1)
+            for i in range(2):
+                if q == 0:
+                    project((i,), (0, 1), nc.scalar, free[q][i])
+                    store(P * i, P, (0, 1))
+                    normalise_unit(1 + 2 * i, 3, nc.scalar)
                 else:
-                    project((2 * b, 2 * b + 1), (u,), nc.scalar, f"bank{free[b][u]}")
-                    store(CHUNK * b, CHUNK * (b + 1), (u,))
-        weave(6, nc.vector)
-        weave(7, nc.vector)
+                    project((2 * q, 2 * q + 1), (i,), nc.scalar, free[q][i])
+                    store(QUARTER * q, QUARTER, (i,))
+        weave(6)
+        weave(7)
         quantise(6)
         quantise(7)
-        for u, engine in enumerate((nc.scalar, nc.vector)):
-            project((6,), (u,), engine, f"bank{(6, 7)[u]}")
-        store(6 * P, 7 * P, (0, 1))
-        for u, engine in enumerate((nc.scalar, nc.vector)):
-            project((7,), (u,), engine, f"bank{(2, 4)[u]}")
-        store(7 * P, S, (0, 1))
+        for c in (6, 7):
+            for u, engine in enumerate((nc.scalar, nc.vector)):
+                project((c,), (u,), engine, free[c - 6][u])
+            store(P * c, P, (0, 1))

@@ -22,6 +22,7 @@ PACK = 4
 BANK = 512
 QUARTER = 256
 W_FIRST = 3
+WARM_PASSES, WARM_ROWS = 2, 64
 KEPT = ((0, 0), (1, 0), (0, 1), (2, 0), (3, 0), (3, 3))
 TALLIED = ((0, 2), (0, 3), (1, 1), (1, 2), (1, 3), (2, 1), (2, 2), (3, 1), (3, 2))
 
@@ -199,15 +200,16 @@ def tile_picked_inorm_none_p_kernel(tc, x_words, x_scales, w1, w2_words, w2_scal
             normalise(t, z_rows[q][:, t], sums[t, q], engine)
 
         open_bank(0, "h00")
-        nc.tensor.matmul_mx(
-            out=banks[0][:],
-            lhsT=w_codes[:, :P].bitcast(FP8X4),
-            lhsT_scale=w_plane[:, :P],
-            rhs=w_codes[:].bitcast(FP8X4),
-            rhs_scale=w_plane[:],
-            start=True,
-            stop=True,
-        )
+        for lo in range(0, WARM_PASSES * WARM_ROWS, WARM_ROWS):
+            nc.tensor.matmul_mx(
+                out=banks[0][:WARM_ROWS],
+                lhsT=w_codes[:, lo : lo + WARM_ROWS].bitcast(FP8X4),
+                lhsT_scale=w_plane[:, lo : lo + WARM_ROWS],
+                rhs=w_codes[:].bitcast(FP8X4),
+                rhs_scale=w_plane[:],
+                start=True,
+                stop=True,
+            )
 
         multiply(0, 0, 0, 0)
         multiply_fresh(1, 0, 1)

@@ -23,6 +23,7 @@ BANK = 512
 QUARTER = 256
 W_FIRST = 3
 WARM_PASSES, WARM_ROWS = 2, 64
+M_VECTOR = 48
 KEPT = ((0, 0), (1, 0), (0, 1), (2, 0), (3, 0), (3, 3))
 TALLIED = ((0, 2), (0, 3), (1, 1), (1, 2), (1, 3), (2, 1), (2, 2), (3, 1), (3, 2))
 
@@ -75,10 +76,10 @@ def tile_picked_inorm_none_p_kernel(tc, x_words, x_scales, w1, w2_words, w2_scal
             nc.scalar.dma_start(x_plane[r:P:32, :].bitcast(I32), s_picked[32 + 4 * r : 96 : 16, :].bitcast(I32))
 
         w_bf = held.tile([P, PACK, P, PACK], BF16, name="w_bf", align_bytes=64)
-        nc.vector.tensor_copy(
-            w_bf[:].rearrange("p (u v) m j -> p u m j v", v=2),
-            w_raw[:].rearrange("p j (m u v) -> p u m j v", u=2, v=2),
-        )
+        w_dealt = w_bf[:].rearrange("p (u v) m j -> p u m j v", v=2)
+        w_pairs = w_raw[:].rearrange("p j (m u v) -> p u m j v", u=2, v=2)
+        nc.scalar.copy(w_dealt[:, :, M_VECTOR:], w_pairs[:, :, M_VECTOR:])
+        nc.vector.tensor_copy(w_dealt[:, :, :M_VECTOR], w_pairs[:, :, :M_VECTOR])
 
         w2_plane = early.tile([P, N], U8, name="w2_plane", offset=4 * T, align_bytes=64)
         nc.vector.memset(w2_plane[:].bitcast(I32), 0)

from contextlib import ExitStack

import concourse.mybir as mybir

K, T, S, H, N = 512, 4096, 1024, 512, 256
FLOPS = 2 * S * H * (K + N)
EPS = 1e-5

F32 = mybir.dt.float32
BF16 = mybir.dt.bfloat16
I32 = mybir.dt.int32
U32 = mybir.dt.uint32
U16 = mybir.dt.uint16
U8 = mybir.dt.uint8
FP8X4 = mybir.dt.float8_e4m3fn_x4
FP4X4 = mybir.dt.float4_e2m1fn_x4
ACT = mybir.ActivationFunctionType
ALU = mybir.AluOpType

P = 128
PACK = 4
BANK = 512
QUARTER = 256
W_FIRST = 3
WARM_PASSES, WARM_ROWS = 2, 64
M_VECTOR = 48
KEPT = ((0, 0), (1, 0), (0, 1), (2, 0), (3, 0), (3, 3))
TALLIED = ((0, 2), (0, 3), (1, 1), (1, 2), (1, 3), (2, 1), (2, 2), (3, 1), (3, 2))


def tile_picked_inorm_none_p_kernel(tc, x_words, x_scales, w1, w2_words, w2_scales, gamma, offs, out):
    nc = tc.nc
    with ExitStack() as ctx:
        held = ctx.enter_context(tc.tile_pool(name="held", bufs=1))
        early = ctx.enter_context(tc.tile_pool(name="early", bufs=1))
        late = ctx.enter_context(tc.tile_pool(name="late", bufs=1))
        psum = ctx.enter_context(tc.psum_pool(name="psum", bufs=1))

        s_table = early.tile([P, T], U8, name="s_table", offset=4 * T, align_bytes=64)
        nc.vector.memset(s_table[:].bitcast(I32), 0)
        w_raw = held.tile([P, PACK, H], F32, name="w_raw", align_bytes=64)
        w_rows = w1.rearrange("(p j) c -> p j c", j=PACK)
        nc.sync.dma_start(w_raw[:, :W_FIRST], w_rows[:, :W_FIRST])
        offsets = held.tile([P, S // 16], U16, name="offsets")
        nc.sync.dma_start(offsets[:], offs)
        nc.sync.dma_start(s_table[32:96:4, :].bitcast(I32), x_scales[0].bitcast(I32))
        nc.sync.dma_start(w_raw[:, W_FIRST:], w_rows[:, W_FIRST:])
        x_table = early.tile([P, T], U32, name="x_table", offset=0, align_bytes=64)
        x_rows = x_words[0].rearrange("p n r -> p (n r)").bitcast(I32)
        nc.sync.dma_start(x_table[:].bitcast(I32), x_rows)
        w2_codes = held.tile([P, 2 * N], U8, name="w2_codes", align_bytes=64)
        nc.sync.dma_start(w2_codes[:].bitcast(I32), w2_words[0].bitcast(I32))
        gain = held.tile([P, PACK], F32, name="gain", align_bytes=64)
        nc.sync.dma_start(gain[:], gamma.rearrange("(p t) o -> p (t o)", t=PACK))

        x_plane = held.tile([P, S], U8, name="x_plane", align_bytes=64)
        nc.vector.memset(x_plane[:].bitcast(I32), 0)
        warm_in = held.tile([P, 1], F32, name="warm_in")
        nc.vector.memset(warm_in[:], 1.0)
        warm_out = held.tile([P, 1], F32, name="warm_out")
        nc.scalar.activation(warm_out[:], warm_in[:], ACT.Abs_reciprocal_sqrt)

        slot, used = {}, [0] * PACK
        for runs, width in ((KEPT, 3), (TALLIED, 6)):
            for t, q in runs:
                slot[t, q] = used[t]
                used[t] = used[t] + width
        stats = [held.tile([P, used[t]], F32, name=f"stats{t}")[:] for t in range(PACK - 1)]
        stats.append(late.tile([P, used[3]], F32, name="stats3", offset=0)[:])
        for t, q in KEPT:
            nc.vector.memset(stats[t][:, slot[t, q] : slot[t, q] + 1], float(QUARTER))

        s_picked = held.tile([P, S], U8, name="s_picked", align_bytes=64)
        nc.vector.tensor_copy(s_picked[:], s_table[:].indirect(offsets[:]))
        for r in range(4):
            nc.scalar.dma_start(x_plane[r:P:32, :].bitcast(I32), s_picked[32 + 4 * r : 96 : 16, :].bitcast(I32))

        w_bf = held.tile([P, PACK, P, PACK], BF16, name="w_bf", align_bytes=64)
        w_dealt = w_bf[:].rearrange("p (u v) m j -> p u m j v", v=2)
        w_pairs = w_raw[:].rearrange("p j (m u v) -> p u m j v", u=2, v=2)
        nc.scalar.copy(w_dealt[:, :, M_VECTOR:], w_pairs[:, :, M_VECTOR:])
        nc.vector.tensor_copy(w_dealt[:, :, :M_VECTOR], w_pairs[:, :, :M_VECTOR])

        w2_plane = early.tile([P, N], U8, name="w2_plane", offset=4 * T, align_bytes=64)
        nc.vector.memset(w2_plane[:].bitcast(I32), 0)
        for r in range(4):
            nc.sync.dma_start(w2_plane[r:P:32, :].bitcast(I32), w2_scales[0, r:16:4, :].bitcast(I32))

        w_codes = held.tile([P, H], U32, name="w_codes", align_bytes=64)
        w_plane = held.tile([P, H], U8, name="w_plane", align_bytes=64)
        nc.vector.quantize_mx(out=w_codes[:].bitcast(FP8X4), scales=w_plane[:], in_=w_bf[:].rearrange("p t m j -> p (t m j)"))

        neg_gain = held.tile([P, PACK], F32, name="neg_gain")
        nc.scalar.activation(neg_gain[:], gain[:], ACT.Copy, scale=-1.0)
        raw_factors = [held.tile([P, 2, 2], F32, name=f"raw_factors{i}") for i in range(2)]
        for i in range(2):
            nc.scalar.activation(raw_factors[i][:, :, 0], gain[:, 2 * i : 2 * i + 2], ACT.Copy)

        picked = held.tile([P, S], U32, name="x_picked", align_bytes=64)
        for lo in range(0, S, QUARTER):
            nc.vector.tensor_copy(picked[:, lo : lo + QUARTER], x_table[:].indirect(offsets[:, lo // 16 : (lo + QUARTER) // 16]))

        banks = {}
        sums = {}

        def open_bank(b, name):
            banks[b] = psum.tile([P, BANK], F32, name=name, tag=f"bank{b}")

        def multiply(t, q, b, side, n=QUARTER):
            lo = QUARTER * q
            for k in range(n // QUARTER):
                sums[t, q + k] = banks[b][:, QUARTER * (side + k) : QUARTER * (side + k + 1)]
            nc.tensor.matmul_mx(
                out=banks[b][:, QUARTER * side : QUARTER * side + n],
                lhsT=w_codes[:, P * t : P * (t + 1)].bitcast(FP8X4),
                lhsT_scale=w_plane[:, P * t : P * (t + 1)],
                rhs=picked[:, lo : lo + n].bitcast(FP8X4),
                rhs_scale=x_plane[:, lo : lo + n],
                start=True,
                stop=True,
            )

        def multiply_fresh(t, q, b, n=QUARTER):
            open_bank(b, f"h{t}{q}")
            multiply(t, q, b, 0, n)

        affine = {t: held.tile([P, 2], F32, name=f"affine{t}") for t in (0, 2, 3)}
        rstd = [held.tile([P, 1], F32, name=f"rstd{t}")[:] for t in range(2)]
        last_roots = held.tile([P, 2], F32, name="last_roots")
        rstd.extend(last_roots[:, i : i + 1] for i in range(2))
        moments = [held.tile([P, 2], F32, name=f"moments{t}")[:] for t in range(2)]
        last_moments = held.tile([P, 2, 2], F32, name="last_moments")
        moments.extend(last_moments[:, i] for i in range(2))
        z_first = held.tile([P, 2, PACK, QUARTER], BF16, name="z_first", align_bytes=64)
        z_rows = [z_first[:, q] for q in range(2)]
        wide_gain = held.tile([P, PACK], F32, name="wide_gain")
        nc.scalar.activation(wide_gain[:], gain[:], ACT.Copy, scale=float(QUARTER))
        gained = {t: held.tile([P, QUARTER], F32, name=f"gained{t}", align_bytes=64) for t in (1, 2, 3)}
        gained_half = held.tile([P, 2, QUARTER], F32, name="gained_half", align_bytes=64)
        kept_half = held.tile([P, 2, QUARTER], F32, name="kept_half", align_bytes=64)
        kept = {(0, q): kept_half[:, q] for q in range(2)}
        for t, q in KEPT:
            if t > 0:
                kept[t, q] = held.tile([P, QUARTER], F32, name=f"kept{t}{q}", align_bytes=64)[:]
        after_stats3 = 128
        squares = [
            held.tile([P, QUARTER], BF16, name="squares0", align_bytes=64),
            late.tile([P, QUARTER], BF16, name="squares1", offset=after_stats3, align_bytes=64),
        ]

        def keep(t, q):
            at = slot[t, q]
            nc.scalar.activation(kept[t, q], sums[t, q], ACT.Copy, scale=1.0 / QUARTER, accum_out=stats[t][:, at + 1 : at + 2])

        def spread(t, q):
            at = slot[t, q]
            nc.scalar.activation(
                squares[KEPT.index((t, q)) % 2][:],
                kept[t, q],
                ACT.Square,
                scale=-float(QUARTER),
                bias=stats[t][:, at + 1 : at + 2],
                accum_out=stats[t][:, at + 2 : at + 3],
            )

        def tally(t, q, src):
            nc.vector.bn_stats(stats[t][:, slot[t, q] : slot[t, q] + 6], src)

        def aggregate(t):
            nc.vector.bn_aggr(moments[t], stats[t])

        def root(dst, variance):
            nc.scalar.activation(dst, variance, ACT.Abs_reciprocal_sqrt, bias=EPS)

        def shifted(t):
            return raw_factors[t // 2][:, t % 2, 1:2]

        def shift(t, engine):
            if engine is nc.scalar:
                nc.scalar.activation(shifted(t), moments[t][:, 0:1], ACT.Copy, scale=neg_gain[:, t : t + 1])
            else:
                engine.tensor_scalar(shifted(t), moments[t][:, 0:1], neg_gain[:, t : t + 1], 0.0, ALU.mult, ALU.add)

        def finish(t):
            nc.scalar.activation(affine[t][:], raw_factors[t // 2][:, t % 2], ACT.Copy, scale=rstd[t])

        def amplify(t, dst, src):
            nc.gpsimd.tensor_scalar(dst, src, wide_gain[:, t : t + 1], 0.0, ALU.mult, ALU.add)

        def centre(t, dst, src, engine):
            engine.tensor_scalar(dst, src, shifted(t), rstd[t], ALU.add, ALU.mult)

        def normalise(t, dst, src, engine):
            scale, bias = affine[t][:, 0:1], affine[t][:, 1:2]
            if engine is nc.scalar:
                nc.scalar.activation(dst, src, ACT.Identity, scale=scale, bias=bias)
            else:
                engine.tensor_scalar(dst, src, scale, bias, ALU.mult, ALU.add)

        def normalise_unit(t, q, engine):
            normalise(t, z_rows[q][:, t], sums[t, q], engine)

        open_bank(0, "h00")
        for lo in range(0, WARM_PASSES * WARM_ROWS, WARM_ROWS):
            nc.tensor.matmul_mx(
                out=banks[0][:WARM_ROWS],
                lhsT=w_codes[:, lo : lo + WARM_ROWS].bitcast(FP8X4),
                lhsT_scale=w_plane[:, lo : lo + WARM_ROWS],
                rhs=w_codes[:].bitcast(FP8X4),
                rhs_scale=w_plane[:],
                start=True,
                stop=True,
            )

        multiply(0, 0, 0, 0)
        multiply_fresh(1, 0, 1)
        multiply_fresh(1, 1, 2)
        multiply_fresh(0, 1, 3)
        multiply_fresh(2, 1, 4)
        multiply(3, 1, 4, 1)
        keep(0, 0)
        keep(1, 0)
        spread(0, 0)
        keep(0, 1)
        spread(1, 0)
        spread(0, 1)
        for t in range(1, PACK):
            tally(t, 1, sums[t, 1])
        multiply_fresh(0, 2, 5)
        multiply_fresh(2, 0, 6)
        multiply_fresh(0, 3, 7)
        multiply_fresh(1, 2, 0)
        multiply(3, 0, 2, 1)
        multiply_fresh(1, 3, 1)
        amplify(1, gained[1][:], kept[1, 0])
        amplify(0, gained_half[:], kept_half[:])
        keep(2, 0)
        multiply(3, 3, 6, 1)
        multiply_fresh(2, 2, 3, BANK)
        keep(3, 0)
        spread(2, 0)
        amplify(2, gained[2][:], kept[2, 0])
        tally(0, 2, sums[0, 2])
        tally(0, 3, sums[0, 3])
        multiply(3, 2, 5, 1)
        keep(3, 3)
        tally(1, 2, sums[1, 2])
        aggregate(0)
        shift(0, nc.gpsimd)
        amplify(3, gained[3][:], kept[3, 0])
        tally(1, 3, sums[1, 3])
        tally(2, 2, banks[3][:])
        aggregate(1)
        tally(3, 2, sums[3, 2])
        root(rstd[0], moments[0][:, 1:2])
        spread(3, 0)
        spread(3, 3)

        finish(0)
        root(rstd[1], moments[1][:, 1:2])
        shift(1, nc.scalar)
        z_second = late.tile([P, 2, PACK, QUARTER], BF16, name="z_second", offset=after_stats3, align_bytes=64)
        z_rows.extend(z_second[:, q] for q in range(2))
        normalise_unit(0, 2, nc.scalar)
        centre(0, z_first[:, :, 0], gained_half[:], nc.gpsimd)
        aggregate(2)
        aggregate(3)
        affine[1] = late.tile([P, 2], F32, name="affine1", offset=0)
        normalise_unit(0, 3, nc.vector)
        shift(3, nc.vector)
        centre(1, z_rows[0][:, 1], gained[1][:], nc.vector)
        root(last_roots[:], last_moments[:, :, 1])
        shift(2, nc.scalar)
        centre(2, z_rows[0][:, 2], gained[2][:], nc.vector)
        for lo in (0, P):
            centre(3, z_rows[0][:, 3, lo : lo + P], gained[3][:, lo : lo + P], nc.vector)
        finish(1)
        finish(2)
        normalise_unit(1, 1, nc.scalar)
        finish(3)

        woven, codes, planes = {}, {}, {}
        res = [held.tile([P, 2, QUARTER], F32, name=f"res{q}", align_bytes=64) for q in range(S // QUARTER)]

        def weave(c):
            woven[c] = held.tile([P, P, PACK], BF16, name=f"woven{c}", align_bytes=64)
            q, lo = divmod(P * c, QUARTER)
            nc.vector.tensor_copy(
                woven[c][:].rearrange("p (g i) t -> p g t i", i=4),
                z_rows[q][:, :, lo : lo + P].rearrange("p t (g i) -> p g t i", i=4),
            )

        def quantise(c):
            codes[c] = held.tile([P, P], U32, name=f"z_codes{c}", align_bytes=64)
            planes[c] = held.tile([P, P], U8, name=f"z_plane{c}", align_bytes=64)
            nc.vector.quantize_mx(out=codes[c][:].bitcast(FP8X4), scales=planes[c][:], in_=woven[c][:].rearrange("p n t -> p (n t)"))

        def project(chunks, us, engine, b):
            first, n = P * chunks[0], P * len(chunks)
            acc = psum.tile([P, len(us), n], F32, name=f"acc{chunks[0]}{us[0]}", tag=f"bank{b}")
            for c in chunks:
                for i, u in enumerate(us):
                    nc.tensor.matmul_mx(
                        out=acc[:, i, P * c - first : P * (c + 1) - first],
                        lhsT=w2_codes[:, 2 * P * u : 2 * P * (u + 1)].bitcast(FP4X4),
                        lhsT_scale=w2_plane[:, P * u : P * (u + 1)],
                        rhs=codes[c][:].bitcast(FP8X4),
                        rhs_scale=planes[c][:],
                        start=True,
                        stop=True,
                    )
            dst = res[first // QUARTER][:, us[0] : us[-1] + 1, first % QUARTER : first % QUARTER + n]
            if engine is nc.vector:
                nc.vector.tensor_copy(dst, acc[:])
            else:
                nc.scalar.copy(dst, acc[:])

        out_rows = out.rearrange("(u p) s -> p u s", p=P)

        def store(lo, n, us):
            rows = slice(us[0], us[-1] + 1)
            nc.sync.dma_start(out_rows[:, rows, lo : lo + n], res[lo // QUARTER][:, rows, lo % QUARTER : lo % QUARTER + n])

        free = ((7, 5), (2, 4), (0, 3))
        for t in (2, 3):
            normalise_unit(t, 1, nc.scalar)
        for t in (1, 3):
            normalise_unit(t, 2, nc.scalar)
        normalise(2, z_second[:, :, 2], banks[3][:].rearrange("p (q n) -> p q n", q=2), nc.scalar)
        weave(0)
        for q in range(3):
            weave(2 * q + 1)
            quantise(2 * q)
            if q < 2:
                weave(2 * q + 2)
            quantise(2 * q + 1)
            for i in range(2):
                if q == 0:
                    project((i,), (0, 1), nc.scalar, free[q][i])
                    store(P * i, P, (0, 1))
                    normalise_unit(1 + 2 * i, 3, nc.scalar)
                else:
                    project((2 * q, 2 * q + 1), (i,), nc.scalar, free[q][i])
                    store(QUARTER * q, QUARTER, (i,))
        weave(6)
        weave(7)
        quantise(6)
        quantise(7)
        for c in (6, 7):
            for u, engine in enumerate((nc.scalar, nc.vector)):
                project((c,), (u,), engine, free[c - 6][u])
            store(P * c, P, (0, 1))
